import numpy as np, ml_dtypes
CORES = [3,7,11,15,131,135,139,143]
N = 8
BF = ml_dtypes.bfloat16
def gentries(a):
    return np.ascontiguousarray(a.reshape(8, 16, -1).transpose(0, 2, 1)).reshape(8, -1)
def gtable(e):
    e = np.asarray(e); return np.ascontiguousarray(e.reshape(8, -1, 16).transpose(0, 2, 1)).reshape(128, -1).astype(np.int32)
def f(rng, *shape):
    return (rng.standard_normal(shape, dtype=np.float32) * np.exp2(rng.integers(-2, 3, shape[:-1] + (1,)))).astype(BF)
def wide(rng, *shape):
    v = f(rng, *shape).astype(np.float32); k = shape[:-2] + (1, shape[-1])
    return (v * np.exp2(rng.integers(-6, 7, k)) * (rng.random(k) > 0.0625)).astype(BF)
W, C, LOOK, RO = 4096, 512, 4, 3
def cuts(rng, least=3):
    room = W - least * C - W // 16
    e = np.sort(rng.integers(0, room + 1, C - 1))
    return least + np.diff(np.concatenate([np.array([0]), e, np.array([room])])).astype(np.int64)
def laid(rng, le, first):
    o = rng.permutation(C); o = np.concatenate([np.array([first]), o[o != first]])
    st = np.zeros(C, np.int64); st[o] = np.add.accumulate(le[o]) - le[o]
    return st
def walk(le):
    cyc = np.repeat(np.arange(C), le)
    return cyc, np.arange(cyc.size) - np.repeat(np.add.accumulate(le) - le, le)
def rings(s, order, st, le):
    cyc, off = walk(le); a, n = st[cyc], le[cyc]
    s[order[a + off]] = order[a + (off + 1) % n] + order[a + (off + n - 1) % n]
    return s, order[st], np.concatenate([order[st + 1], order[st + le - 1]])
def hang(rng, order, st, le, near, mix):
    kid = np.full(W, -1, np.int64)
    a, b = rng.permutation(np.arange(0, C, 2)), rng.permutation(np.arange(1, C, 2))
    m = np.array(a[:mix]); a[:mix] = b[:mix]; b[:mix] = m
    for par, kids in ((0, b), (1, a)):
        i = np.arange(par, C, 2); w = st[i] + 1
        if not near: w = np.concatenate([w, st[i] + 2, (st[i] + 3)[le[i] > 3]])
        kid[order[rng.permutation(w)[:C // 2]]] = kids
    return kid
def skeleton(rng, near, far=()):
    out = []
    for g in range(N * 8):
        order = rng.permutation(W); le = cuts(rng, 5 if g in far else 3); st = laid(rng, le, int(rng.integers(0, C)))
        s, r, e = rings(rng.integers(1, 2 * W - 2, W), order, st, le); tight = near and g % 2 == 1 and g not in far
        out.append((s, r, e, hang(rng, order, st, le, tight, 0 if tight else C // 8)))
    return out
def items(rng):
    a = np.exp2(rng.integers(-2, 3, (N, 128, 1))).astype(np.float32)
    x = rng.standard_normal((N, 128, W), dtype=np.float32) * a
    h = np.repeat(rng.choice(np.array([-0.7, -0.4, -0.1, 0.2], np.float32), (N, 8, RO * C)), 16, axis=1)
    return x, (np.float32(0.7) * rng.standard_normal((N, 128, RO * C), dtype=np.float32) + h) * a
def pat(rng, u):
    m = rng.choice(np.array([1, 3, 5, 7]), u.shape); sh = rng.integers(0, 16, u.shape)
    return ((np.arange(16)[:, None] * m + sh) & 15) < u
def pack(x, q, out):
    s, r, e, k = [np.stack(a) for a in zip(*out)]
    return {"x": np.ascontiguousarray(x.reshape(N, 128, W)).astype(BF), "nsum": s.reshape(N, 8, W).astype(np.int32), "rho": np.stack([gtable(a) for a in r.reshape(N, 8, C)]),
            "nei": np.stack([gtable(a) for a in e.reshape(N, 8, 2 * C)]), "kid": k.reshape(N, 8, W).astype(np.int32), "dem": np.ascontiguousarray(q.reshape(N, 128, RO * C)).astype(BF)}
def setup_inputs(rng):
    x, q = items(rng)
    return pack(x, q, skeleton(rng, False))
def setup_inputs_corners(rng):
    out = []; fit = np.zeros((N * 8, W), bool)
    for g in range(N * 8):
        if g % 8 == 0: modes = rng.permutation(8)
        mode = int(modes[g % 8]); order = rng.permutation(W)
        le = rng.choice(np.array([3, 4, LOOK + 1, LOOK + 2, 2 * LOOK, 2 * LOOK + 1, 2 * LOOK + 2]), C).astype(np.int64)
        le = np.where(np.add.accumulate(le - 3) > W - 3 * C, 3, le)
        if g % 2 == 1: le[rng.integers(0, C)] += W - np.sum(le)
        st = laid(rng, le, int(rng.integers(0, C))); s, r, e = rings(rng.integers(1, 2 * W - 2, W), order, st, le)
        cyc, p = walk(le); k = rng.choice(np.array([0, 0, 1, 2, 3, 4, 5, 5, 6, 6]), C)[cyc]; n = le[cyc]; back = n - p
        fit[g] = rng.random(W) < 0.5
        fit[g, order[st[cyc] + p]] = (p == 0) | ((k == 0) & ((p == LOOK) | (back == LOOK))) | ((k == 1) & ((p == LOOK + 1) | (back == 1))) | ((k == 2) & (p == n // 2)) | (k == 4) | ((k == 5) & ((p == 1) | (back == 1))) | ((k == 6) & (rng.random(p.size) < 0.5))
        kid = np.full(W, -1, np.int64)
        if mode == 0: kid[order[st + 1]] = (np.arange(C) + 1) % C
        elif mode == 2: kid[order[st]] = rng.permutation(C)
        elif mode == 3: kid[order[st + 1]] = np.arange(C)
        elif mode >= 4: kid = hang(rng, order, st, le, mode < 6, 0 if mode < 6 else C // 8)
        out.append((s, r, e, kid))
    fit = fit.reshape(N, 8, 1, W)
    u = np.where(fit, rng.choice(np.array([9, 16]), fit.shape), rng.choice(np.array([0, 8]), fit.shape))
    x = np.where(pat(rng, u), np.float32(1), np.float32(-1)) * (2 + rng.random((N, 8, 16, W), dtype=np.float32))
    q = 2 * rng.random((N, 8, 16, RO * C), dtype=np.float32) - 1
    return pack(x, q + rng.choice(np.array([0, 8, -8], np.float32), (N, 8, 1, RO * C), p=[0.8, 0.1, 0.1]), out)
def setup_inputs_crowd(rng):
    x, q = items(rng); q = q.reshape(N, 8, 16, RO, C); xv = x.reshape(N * 8, 16, W)
    h = int(rng.integers(0, 8)); k = (h + 1) % 8; deep = []
    for r in range(N):
        for t in range(RO):
            o = rng.permutation(8); i = rng.choice(np.array([0, C - 1, C // 2, C // 2 + 1]), 2)
            if t == 0:
                o = o[(o != h) & (o != k)]
                if r == 0:
                    j = int(np.argmax(o % 2)); o[[1, j]] = o[[j, 1]]
                o = np.concatenate([np.array([h]), o]); deep.append(r * 8 + int(o[4])); q[r, o[4], :, 0] = -72
            q[r, o[0], :, t] = 128; q[r, o[1], :, t] = 128; q[r, o[1], :, t, i[0]] = -128
            q[r, o[2], :, t] = -128; q[r, o[3], :, t] = -128; q[r, o[3], :, t, i[1]] = 128
    q[:, k, :, 0, C - 1] = 128; q[:, k, :, 1, C - 1] = -72
    out = skeleton(rng, True, set(deep) | set(r * 8 + k for r in range(N)))
    for r in range(N):
        for g, e in ((deep[r], np.arange(2 * C)), (r * 8 + k, np.array([C - 1, 2 * C - 1]))):
            a = out[g][2][e]; b = out[g][0][a] - out[g][1][e % C]
            xv[g][:, a] -= 96; xv[g][:, b] -= 48
    return pack(x, q, out)
def setup_inputs_ends(rng):
    zig = np.zeros(W, np.int64); zig[0::2] = np.arange(W // 2); zig[1::2] = W - 1 - np.arange(W // 2)
    out = []
    for g in range(N * 8):
        order = zig if g % 2 == 0 else W - 1 - zig; first = C - 1 if (g // 2) % 2 == 1 else 0
        le = cuts(rng); le[first] = max(int(le[first]), 5); st = laid(rng, le, first)
        s, r, e = rings(rng.choice(np.array([1, 2 * W - 3]), W), order, st, le)
        out.append((s, r, e, hang(rng, order, st, le, False, C // 8)))
    u = rng.choice(np.array([0, 8, 9, 16]), (N, 8, 1, W), p=[0.15, 0.25, 0.35, 0.25])
    u[:, 0::2, 0, 0] = 8; u[:, 0::2, 0, W - 1] = 9; u[:, 1::2, 0, 0] = 9; u[:, 1::2, 0, W - 1] = 8
    m = rng.choice(np.array([0, 8, 16]), (N, 8, 1, RO * C), p=[0.15, 0.25, 0.6])
    for g in range(N * 8):
        if (g // 2) % 2 == 0:
            s, r, e, kd = out[g]; a = int(e[0]); b = int(s[a] - r[0]); c = int(s[b] - a)
            u[g // 8, g % 8, 0, a] = 8; u[g // 8, g % 8, 0, b] = 8; u[g // 8, g % 8, 0, c] = 9; u[g // 8, g % 8, 0, int(e[C])] = 9
            kd[r[0]] = kd[a]; kd[a] = -1
            m[g // 8, g % 8, 0, 0] = 0; m[g // 8, g % 8, 0, C] = 16
    return pack(np.where(pat(rng, u), np.float32(1024), np.float32(-1024)), np.where(pat(rng, m), np.float32(1024), np.float32(-1024)), out)
def setup_inputs_spread(rng):
    return pack(wide(rng, N, 128, W), wide(rng, N, 128, RO * C), skeleton(rng, False))
def setup_inputs_ties(rng):
    a = np.exp2(rng.integers(-2, 3, (1, 1, 16, 1))).astype(np.float32)
    m = rng.integers(0, 4, (N, 8, 16, W)); k = rng.integers(0, 4, (N, 8, 16, RO * C)) + rng.choice(np.array([0, 0, 1]), (N, 8, 1, RO * C))
    return pack(a * (1 + m * np.float32(0.0078125)), a * (1 + k * np.float32(0.0078125)), skeleton(rng, False))
def check_inputs(d):
    bad = []
    for k, lo, hi in (("nsum", 1, 2 * W - 3), ("rho", 0, W - 1), ("nei", 0, W - 1), ("kid", -1, C - 1)):
        if np.min(d[k]) < lo or np.max(d[k]) > hi: bad.append("range of " + k)
    for k in ("x", "dem"):
        a = np.abs(d[k].astype(np.float32))
        if not np.all(np.isfinite(a)): bad.append("numbers of " + k + " finite")
        if np.any((a > 0) & (a < 2.0 ** -126)): bad.append("no subnormal number in " + k)
    kd = np.sort(d["kid"].reshape(N * 8, W), axis=1)
    if np.any((kd[:, 1:] == kd[:, :-1]) & (kd[:, 1:] >= 0)): bad.append("no lane twice in a row of kid")
    if bad: return bad
    s = d["nsum"].astype(np.int64).reshape(-1)
    ro = np.stack([gentries(a) for a in d["rho"]]).astype(np.int64).reshape(-1)
    ne = np.stack([gentries(a) for a in d["nei"]]).astype(np.int64).reshape(N * 8, 2, C)
    cur, last = ne[:, 0].reshape(-1), ne[:, 1].reshape(-1); base = np.repeat(np.arange(N * 8) * W, C); prev = ro
    seen = np.zeros(N * 8 * W, np.int64); np.add.at(seen, base + ro, 1)
    good = bool(np.max(seen) == 1 and np.all(s[base + ro] == cur + last) and np.all(cur != last))
    while good and cur.size:
        at = base + cur; np.add.at(seen, at, 1); nx = s[at] - prev; home = nx == ro
        good = not (np.any(seen[at] > 1) or np.any(nx < 0) or np.any(nx >= W) or np.any(home & (cur != last)))
        go = ~home; prev, cur, ro, last, base = cur[go], nx[go], ro[go], last[go], base[go]
    if not good: bad.append("cycles whole and apart")
    return bad
def reach(a, b):
    return np.sum((a >= b).astype(np.int64), axis=-2) >= 9
def reference(x, nsum, rho, nei, kid, dem):
    xs = x.astype(np.float32).reshape(N * 8, 16, W); s = nsum.astype(np.int64).reshape(N * 8, W); kd = kid.astype(np.int64).reshape(N * 8, W)
    ro = np.stack([gentries(a) for a in rho]).astype(np.int64).reshape(N * 8, C)
    ne = np.stack([gentries(a) for a in nei]).astype(np.int64).reshape(N * 8, 2, C)
    q = dem.astype(np.float32).reshape(N * 8, 16, RO, C); lane = np.arange(C)
    live = np.ones((N * 8, C), bool); z = q[:, :, 0]
    for t in range(RO):
        w, pv, emb = [], [], live
        for side in range(2):
            prev, cur = ro, ne[:, side] + 0; stop = ~live; hit = np.zeros((N * 8, C), bool)
            for k in range(LOOK):
                home = cur == ro; fit = reach(np.take_along_axis(xs, cur[:, None, :], 2), z) & ~home
                hit = hit | (fit & ~stop); go = ~(stop | fit | home); stop = ~go
                nxt = np.take_along_axis(s, cur, 1) - prev
                prev, cur = np.where(go, cur, prev), np.where(go, nxt, cur)
            w.append(cur); pv.append(prev); emb = emb & hit
        emb = emb & (w[0] != w[1])
        g, i = np.nonzero(emb)
        for side in range(2):
            s[g, w[side][g, i]] += ro[g, i] - pv[side][g, i]
            ne[g, side, i] = w[side][g, i]
        s[g, ro[g, i]] = w[0][g, i] + w[1][g, i]
        j = np.take_along_axis(kd, w[0], 1); jj = np.maximum(j, 0)
        g, i = np.nonzero(emb & (lane % 2 == t % 2) & (j >= 0) & (jj % 2 != lane % 2) & np.take_along_axis(emb, jj, 1))
        h = jj[g, i]; v = w[0][g, i]; b = s[g, v] - ro[g, i]
        c, d = ne[g, 0, h], ne[g, 1, h]
        keep = np.sum((xs[g, :, c] >= xs[g, :, d]).astype(np.int64), axis=1) >= 9
        c, d = np.where(keep, c, d), np.where(keep, d, c)
        s[g, v] += c - b
        s[g, c] += v - ro[g, h]
        s[g, d] += b - ro[g, h]
        s[g, b] += d - v
        live = live & True; live[g, h] = False
        if t < RO - 1:
            fl = np.roll((~emb).reshape(N, 8, C), 1, axis=0); zc = np.roll(z.reshape(N, 8, 16, C), 1, axis=0)
            fl = np.where(lane % 2 == 1, np.roll(fl, 1, axis=1), fl); zc = np.where(lane % 2 == 1, np.roll(zc, 1, axis=1), zc)
            z = np.where(fl[:, :, None, :], zc, q[:, :, t + 1].reshape(N, 8, 16, C)).reshape(N * 8, 16, C)
    return {"ys": s.reshape(N, 8, W).astype(np.float32), "yn": ne.reshape(N, 8, 2 * C).astype(np.float32), "yl": live.reshape(N, 8, C).astype(np.float32)}

@@ -1,0 +1,715 @@
+import numpy as np
+from concourse.mybir import AluOpType as OP, ActivationFunctionType as AF
+
+NLF, NLB, NLU, NLI = 20480, 30720, 4096, 1024
+SCRATCH = {
+    "XW": ("sbuf", [128, 4096], "bfloat16"),
+    "ST": ("sbuf", [128, 5120], "float32"),
+    "IDT": ("sbuf", [128, 8192], "float32"),
+    "LF": ("sbuf", [128, NLF], "float32"),
+    "LB": ("sbuf", [128, NLB], "bfloat16"),
+    "LU": ("sbuf", [128, NLU], "uint16"),
+    "LI": ("sbuf", [128, NLI], "int32"),
+}
+for _b in range(8):
+    SCRATCH["PS%d" % _b] = ("psum", [128, 512], "float32")
+NDMA = 40
+SEMAPHORES = ["sV", "sS", "sP", "sG", "sent"] + ["d%d" % i for i in range(NDMA)] + ["r%d" % i for i in range(8)]
+
+CFG = {
+    "pre": [[0, 0, 0, 0, 0, 0, 0, 0], [0, 0, 0, 0, 0, 0, 0, 0], [0, 0, 0, 0, 0, 0, 0, 0]],
+    "nb": [2, 2],
+    "idv": 2,
+    "lD": 0, "lP": 0, "ld": 0, "lS": 0, "lo": 0, "lv": 0, "E": 0, "st": 0, "c3": [1, 0],
+    "silu": [[1, 0, 1], [1, 0, 1], [1, 0, 0], [1, 1]],
+    "early": 1, "llv": 0, "cpv": 4,
+    "split": [0, 1],
+    "g": 1.62, "s": 3.95, "c": 1.04, "pe": 0.52, "lat": 80.0, "iters": 500,
+}
+INFO = {}
+
+
+def arrange(ops, lat, iters):
+    N = len(ops)
+    pred = [sorted(o["deps"]) for o in ops]
+    succ = [[] for _ in range(N)]
+    for i in range(N):
+        for j in pred[i]:
+            succ[j].append(i)
+    cost, tail, eng = [o["cost"] for o in ops], [o["lat"] + lat for o in ops], [o["eng"] for o in ops]
+
+    def place(key, back):
+        before, after = (succ, pred) if back else (pred, succ)
+        left = [len(b) for b in before]
+        ready = [(key[i], i) for i in range(N) if left[i] == 0]
+        busy = {e: [] for e in "VSPGYN"}
+        t0 = [0.0] * N
+        while ready:
+            m = min(ready)
+            ready.remove(m)
+            i = m[1]
+            t = tail[i] if back else 0.0
+            for j in before[i]:
+                x = t0[j] + cost[j] + (tail[i] if back else tail[j])
+                if x > t:
+                    t = x
+            b, c = busy[eng[i]], cost[i]
+            k = len(b)
+            while k > 0 and b[k - 1][1] > t:
+                k -= 1
+            while k < len(b) and b[k][0] < t + c:
+                t = max(t, b[k][1])
+                k += 1
+            b.insert(k, (t, t + c))
+            t0[i] = t
+            for j in after[i]:
+                left[j] -= 1
+                if left[j] == 0:
+                    ready.append((key[j], j))
+        return t0, max(t0[i] + cost[i] + (0.0 if back else tail[i]) for i in range(N))
+
+    pr = [0.0] * N
+    for i in range(N - 1, -1, -1):
+        pr[i] = cost[i] + tail[i] + max([pr[j] for j in succ[i]] + [0.0])
+    early = [1e6 * o.get("early", 0) for o in ops]
+    for i in range(N - 1, -1, -1):
+        for j in pred[i]:
+            early[j] = max(early[j], early[i])
+    best = place([-pr[i] - early[i] for i in range(N)], False)
+    cur = best
+    rng = np.random.default_rng(1)
+    for it in range(iters):
+        amp = 0.0 if it < 4 else (200.0, 600.0, 1500.0, 4000.0)[it % 4]
+        nz = rng.random(N) * amp
+        tb, _ = place([-(cur[0][i] + cost[i]) + nz[i] for i in range(N)], True)
+        new = place([-(tb[i] + cost[i]) - early[i] for i in range(N)], False)
+        if new[1] <= cur[1] * (1.0 + 0.006 * (1.0 - it / iters)):
+            cur = new
+        if new[1] < best[1]:
+            best = new
+    return best
+
+
+def rank_program(g, core, T, topo):
+    rank = T.rank_of(core)
+    if rank is None:
+        return
+    n = len(T.cores)
+    nxt, prv = T.cores[(rank + 1) % n], T.cores[(rank - 1) % n]
+    rid, pid = topo.addr(nxt, core)
+    mask_out = topo.mask(core, nxt)
+    n_out, n_in = len(topo.engines(core, nxt)), len(topo.engines(prv, core))
+    C = CFG
+    ops, acc, top = [], {}, {"LF": 0, "LB": 0, "LU": 0, "LI": 0}
+    nsem, used = {"d": 0, "r": 0}, []
+
+    def al(buf, k):
+        a = top[buf]
+        top[buf] = a + (k + 15) // 16 * 16
+        assert top[buf] <= T[buf].shape[1], buf
+        return (buf, a)
+
+    def A(b, lo, hi, step=1, p=None):
+        buf, a = b
+        ps = p if p is not None else slice(0, 128)
+        ap = T[buf][ps, a + lo:a + hi] if step == 1 else T[buf][ps, a + lo:a + hi:step]
+        return {"ap": ap, "rg": [(buf, a + lo, a + hi)], "n": len(range(lo, hi, step)), "buf": buf, "ind": False}
+
+    def IND(win, off):
+        return {"ap": win["ap"].indirect(off["ap"]), "rg": win["rg"], "off": off["rg"], "n": 16 * off["n"], "buf": win["buf"], "ind": True}
+
+    def add(eng, fn, ins, outs, cost, kind="c", lat=0.0, extra=()):
+        rd, wr = [], []
+        for a in ins:
+            if isinstance(a, dict):
+                rd += a["rg"] + a.get("off", [])
+        for a in outs:
+            wr += a["rg"]
+            rd += a.get("off", [])
+        me = len(ops)
+        deps = set(extra)
+        for lst, w in ((rd, False), (wr, True)):
+            for buf, lo, hi in lst:
+                psum = buf.startswith("PS")
+                for (l2, h2, o2, w2) in acc.get(buf, []):
+                    e2 = ops[o2]["eng"]
+                    if psum and (e2 != eng or eng == "P"):
+                        deps.add(o2)
+                    elif (w or w2) and l2 < hi and lo < h2:
+                        deps.add(o2)
+        for lst, w in ((rd, False), (wr, True)):
+            for buf, lo, hi in lst:
+                acc.setdefault(buf, []).append((lo, hi, me, w))
+        o = {"eng": eng, "fn": fn, "deps": deps, "cost": cost, "kind": kind, "lat": lat}
+        if kind in ("d", "r"):
+            o["sem"] = "%s%d" % (kind, nsem[kind])
+            nsem[kind] += 1
+        ops.append(o)
+        return me
+
+    def vcost(out, ins, two):
+        for a in ins:
+            if isinstance(a, dict) and a["ind"]:
+                return 60 + C["g"] * a["n"]
+        if out["ind"]:
+            return 60 + C["s"] * out["n"]
+        full = [a for a in ins if isinstance(a, dict)]
+        f = 1.0
+        if two:
+            f = 1.0 if any(a["buf"].startswith("PS") for a in full) else 2.0
+        elif all(a["buf"] in ("LB", "LU", "XW") for a in full[:1] + [out]):
+            f = 0.5
+        return 20 + C["c"] * max(64, f * out["n"])
+
+    def sc(x):
+        return x["ap"] if isinstance(x, dict) else x
+
+    def tt(out, a, b, op):
+        return add("V", lambda: [g.vector.tensor_tensor(out["ap"], a["ap"], b["ap"], op)], [a, b], [out], vcost(out, [a, b], True))
+
+    def ts(out, a, s1, op0, s2=None, op1=None):
+        if op1 is None:
+            fn = lambda: [g.vector.tensor_scalar(out["ap"], a["ap"], sc(s1), None, op0)]
+        else:
+            fn = lambda: [g.vector.tensor_scalar(out["ap"], a["ap"], sc(s1), sc(s2), op0, op1)]
+        return add("V", fn, [a, s1, s2], [out], vcost(out, [a], False))
+
+    def cp(out, a):
+        return add("V", lambda: [g.vector.tensor_copy(out["ap"], a["ap"])], [a], [out], vcost(out, [a], False))
+
+    def ms(out, v):
+        return add("V", lambda: [g.vector.memset(out["ap"], v)], [], [out], vcost(out, [], False))
+
+    def act(out, a, bias=None, scale=None):
+        cost = 80 + (C["g"] if a["ind"] else C["c"]) * a["n"]
+        if scale is not None:
+            return add("S", lambda: [g.scalar.activation(out["ap"], a["ap"], AF.Identity, scale=sc(scale))], [a, scale], [out], cost)
+        if bias is None:
+            fn = lambda: [g.scalar.activation(out["ap"], a["ap"], AF.Copy)]
+        else:
+            fn = lambda: [g.scalar.activation(out["ap"], a["ap"], AF.Identity, bias=bias["ap"])]
+        return add("S", fn, [a, bias], [out], cost)
+
+    def put(on_s, off, val):
+        out = IND(STS, off)
+        if not on_s:
+            return cp(out, val)
+        used.append(1)
+        return add("S", lambda: [g.scalar.activation(out["ap"], val["ap"], AF.Silu)], [val], [out],
+                   80 + (1600 if len(used) == 1 else 0) + C["s"] * out["n"])
+
+    def mm(lst):
+        def fn():
+            r = []
+            for i, (o, l, x, st, sp) in enumerate(lst):
+                ins = g.tensor.matmul(o["ap"], l["ap"], x["ap"], st, sp)
+                if sp or i == len(lst) - 1:
+                    r.append(ins)
+            return r
+        k = sum(1 for i, m in enumerate(lst) if m[4] or i == len(lst) - 1)
+        me = add("P", fn, [m[1] for m in lst] + [m[2] for m in lst], [m[0] for m in lst],
+                 40 + sum(C["pe"] * max(64, m[2]["n"]) * (4 if m[2]["buf"] == "LF" else 1) for m in lst), lat=60.0)
+        ops[me]["k"] = k
+        return me
+
+    def dma(q, out, in_, nbytes, ins=(), outs=()):
+        e = g.sync if q == "Y" else g.scalar
+        return add(q, lambda: [e.dma_start(out, in_)], list(ins), list(outs), 60, "d", 1900 + nbytes / 250.0)
+
+    def iota(out, pat, base, cm):
+        if out["buf"] == "LI":
+            fn = lambda: [g.iota(out["ap"], pat, base, cm)]
+        else:
+            fn = lambda: [g.iota(out["ap"], pat, base, cm, allow_small_or_imprecise_dtypes=True)]
+        return add("G", fn, [], [out], 160 + 2 * C["c"] * out["n"])
+
+    def send(src, land, nbytes):
+        sem = "r%d" % nsem["r"]
+        s = add("G", lambda: [g.remote_dma(land["ap"], src["ap"], T.sem[sem], T.sem.sent, pid, rid, mask_out)], [src], [], 200, "x")
+        return add("N", None, [], [land], 0, "r", 2500 + nbytes / 60.0, extra=[s])
+
+    F = lambda k: al("LF", k)
+    B = lambda k: al("LB", k)
+    U = lambda k: al("LU", k)
+    PS = [("PS%d" % i, 0) for i in range(8)]
+    PATH, CNT, ZB, MA, MB = PS[0:2], PS[2:4], PS[4:6], PS[6], PS[7]
+    XW, STW, STS, IDW = A(("XW", 0), 0, 4096), A(("ST", 0), 0, 4096), A(("ST", 0), 0, 5120), A(("IDT", 0), 0, 8192)
+    ST, IDT = ("ST", 0), ("IDT", 0)
+    lo64, hi64 = slice(0, 64), slice(64, 128)
+
+    ns, kd, ro, ne = al("LI", 512), al("LI", 256), al("LI", 32), al("LI", 64)
+    dma("Y", A(ns, 0, 512, p=lo64)["ap"], T.nsum[:], 131072, outs=[A(ns, 0, 256)])
+    dma("S", A(ns, 0, 512, p=hi64)["ap"], T.nsum[:], 131072, outs=[A(ns, 256, 512)])
+    dma("S", XW["ap"], T.x[:], 1 << 20, outs=[XW])
+    d0 = B(512)
+    dma("Y", A(d0, 0, 512)["ap"], T.dem[:, 0:512], 400000, outs=[A(d0, 0, 512)])
+    for par in range(2):
+        for s in range(2):
+            o = A(ne, 32 * par + 16 * s, 32 * par + 16 * s + 16)
+            dma("Y", o["ap"], T.nei[par::2, 32 * s:32 * s + 32], 8192, outs=[o])
+        o = A(ro, 16 * par, 16 * par + 16)
+        dma("Y", o["ap"], T.rho[par::2, :], 8192, outs=[o])
+    dma("Y", A(kd, 0, 256)["ap"], T.kid[:], 900000, outs=[A(kd, 0, 256)])
+    DW = [None, B(1024), B(1024)]
+    for t in (1, 2):
+        o = A(DW[t], 256, 768)
+        dma("Y", o["ap"], T.dem[:, 512 * t:512 * t + 512], 900000, outs=[o])
+
+    Z, ones = B(1024), B(128)
+    ms(A(Z, 0, 1024), 0.0)
+    ms(A(ones, 0, 64), 1.0)
+    ms(A(ones, 64, 128), -1.0)
+    for half, fs in ((lo64, (0, 1)), (hi64, (1, 2))):
+        for f in fs:
+            o, i_ = A(Z, f, 1024, 16, p=half), A(ones, 64 * (f // 2), 64 * (f // 2) + 64, p=half)
+            me = add("G", lambda o=o, i_=i_: [g.affine_select(o["ap"], i_["ap"], [[-1, 8], [-8, 8]], OP.is_equal, 0.0, 0, 1)], [i_], [o], 350)
+            ops[me]["early"] = 1.5 * C["early"]
+    pi, J, cols = al("LI", 48), F(144), F(16)
+    ops[iota(A(pi, 0, 1), [[0, 1]], 0, 1)]["early"] = 2 * C["early"]
+    ops[iota(A(J, 0, 144), [[1, 144]], -15, -1)]["early"] = 2 * C["early"]
+    ts(A(pi, 16, 17), A(pi, 0, 1), 15, OP.bitwise_and)
+    ts(A(pi, 32, 33), A(pi, 0, 1), 1, OP.bitwise_and)
+    col = lambda i: A(cols, i, i + 1)
+    q, h, qz, qy, dl0, dl1, wlo, whi, c255, c1k, m1k = [col(i) for i in range(11)]
+    lift = 1024.0 if any(sum(C["silu"], [])) else 0.0
+    if not lift:
+        c1k = m1k = None
+    cp(q, A(pi, 16, 17))
+    cp(h, A(pi, 32, 33))
+    ts(qz, h, 255.0, OP.mult, q, OP.add)
+    ts(qy, h, 767.0, OP.mult, q, OP.add)
+    ts(dl0, h, -255.0, OP.mult, -256.0, OP.add)
+    ts(dl1, h, -255.0, OP.mult, 511.0, OP.add)
+    i16, oh, mk = F(16), F(16), F(8)
+    ts(A(i16, 0, 1), A(J, 15, 16), q, OP.add)
+    ts(A(oh, 0, 16), A(J, 15, 31), A(i16, 0, 1), OP.is_equal)
+    ts(wlo, A(oh, 1, 2), A(oh, 2, 3), OP.subtract, A(oh, 6, 7), OP.subtract)
+    ts(whi, A(oh, 0, 1), A(oh, 1, 2), OP.add, A(oh, 4, 5), OP.add)
+    tt(A(mk, 0, 2), A(oh, 0, 8, 4), A(oh, 2, 8, 4), OP.subtract)
+    tt(A(mk, 4, 6), A(oh, 0, 8, 4), A(oh, 2, 8, 4), OP.add)
+    tt(A(mk, 2, 3), A(oh, 3, 4), A(oh, 5, 6), OP.add)
+    tt(A(mk, 3, 4), A(mk, 4, 5), A(mk, 2, 3), OP.add)
+    ts(A(mk, 6, 7), A(mk, 4, 5), A(mk, 5, 6), OP.add, 256.0, OP.mult)
+    ts(c255, A(oh, 5, 6), 255.0, OP.mult, A(mk, 6, 7), OP.add)
+    if lift:
+        ts(c1k, A(oh, 1, 2), lift, OP.mult)
+        ms(m1k, -lift)
+        tt(c255, c255, c1k, OP.add)
+    Bc, Id = B(144), B(144)
+    Bm = [B(144) for _ in range(3)]
+    ts(A(Bc, 0, 144), A(J, 0, 144), q, OP.add, 0.0, OP.is_equal)
+    for u in range(3):
+        act(A(Bm[u], 0, 144), A(Bc, 0, 144), scale=A(mk, u, u + 1))
+    ts(A(Id, 0, 144), A(J, 0, 144), 0.0, OP.is_equal)
+    I32, I256, I512, Sh, Sh2, Ip, In = B(128), B(128), B(128), F(128), F(128), F(128), F(128)
+    act(A(Ip, 0, 128), A(Id, 15, 143))
+    if any(C[k] for k in ("ld", "lS", "lo", "E", "st")):
+        act(A(In, 0, 128), A(Id, 15, 143), scale=-1.0)
+
+    def lin(terms, start=True):
+        return [(m[0], A(Ip if m[1] > 0 else In, 0, 128), m[2], start and i == 0, i == len(terms) - 1) for i, m in enumerate(terms) if m]
+
+    def comb(pe, bank, lo, k, whole, parts=()):
+        if pe:
+            o = lambda a, b: A(bank, lo + a, lo + b)
+            if whole:
+                mm(lin([(o(0, k), s_, x) for s_, x in whole] + [(o(a, b), s_, x) for a, b, tm in parts for s_, x in tm]))
+            else:
+                mm([m for a, b, tm in parts for m in lin([(o(a, b), s_, x) for s_, x in tm])])
+            return (bank[0], lo)
+        r = F(k)
+        for a, b, tm in list(parts) + [(0, k, ([(1, A(r, 0, k))] if parts else []) + list(whole))]:
+            for i in range(1, len(tm)):
+                tt(A(r, a, b), tm[0][1] if i == 1 else A(r, a, b), tm[i][1], OP.add if tm[i][0] > 0 else OP.subtract)
+        return r
+
+    for b_, v in ((I32, -32.0), (I256, -256.0), (I512, -512.0)):
+        act(A(b_, 0, 128), A(Id, 15, 143), scale=v)
+    ts(A(Sh, 0, 128), A(J, 15, 143), 16.0, OP.is_equal)
+    ts(A(Sh2, 0, 128), A(J, 15, 143), -112.0, OP.is_equal)
+    L = lambda b_, k: A(b_, 15 - k, 143 - k)
+    full = lambda b_: A(b_, 0, 128)
+    c16, dump, dumpl, base, zo, yi, yo = F(64), F(64), F(16), F(32), U(32), F(96), U(96)
+    iota(A(c16, 0, 64), [[16, 64]], 0, 0)
+    ts(A(dump, 0, 64), A(c16, 0, 64), q, OP.add, 4096.0, OP.add)
+    ts(A(dumpl, 0, 16), A(c16, 0, 16), q, OP.add, 512.0, OP.add)
+    ts(A(base, 0, 16), A(c16, 0, 16), qz, OP.add, 256.0, OP.add)
+    ts(A(base, 16, 32), A(c16, 0, 16), qz, OP.add, 1.0, OP.add)
+    ts(A(zo, 0, 16), A(base, 0, 16), -256.0, OP.add)
+    cp(A(zo, 16, 32), A(base, 16, 32))
+    iota(A(yi, 0, 96), [[256, 3], [1, 2], [16, 16]], 0, 0)
+    ts(A(yo, 0, 96), A(yi, 0, 96), qy, OP.add)
+    LW = [B(768) for _ in range(3)]
+    for t in range(3):
+        iota(A(LW[t], 0, 512), [[0, 512]], 0, 0)
+
+    nb_, nt = B(512), al("LI", 0)
+    nsr = [A(ns, 0, 512)]
+    for c0 in (0, 256):
+        o = A(nb_, c0, c0 + 256)
+        i_ = A(ns, c0, c0 + 256)
+        add("V", lambda o=o, i_=i_: [g.vector.tensor_copy(o["ap"], i_["ap"])], nsr, [o], 20 + C["c"] * 256)
+        o = A(nb_, c0, c0 + 256, p=hi64)
+        i_ = A(ns, c0, c0 + 256, p=hi64)
+        add("V", lambda o=o, i_=i_: [g.vector.tensor_tensor(o["ap"], i_["ap"], o["ap"], OP.subtract)], nsr + [o], [o], 20 + C["c"] * 512)
+    for c0 in (0, 256):
+        for k in range(8):
+            mm([(A(PS[k], c0, c0 + 256), A(Z, 128 * k, 128 * k + 128), A(nb_, c0, c0 + 256), True, True)])
+    for k in range(8):
+        o = A(ST, 512 * k, 512 * k + 512)
+        if not (k % 2 and k < 2 * C["cpv"]):
+            act(o, A(PS[k], 0, 512), c1k)
+        elif lift:
+            ts(o, A(PS[k], 0, 512), c1k, OP.add)
+        else:
+            cp(o, A(PS[k], 0, 512))
+        ops[-1]["early"] = 3 * C["early"]
+
+    j128, bi, kf = F(128), F(64), F(256)
+    ts(A(j128, 0, 1), A(J, 15, 16), wlo, OP.mult, -1.0, OP.mult)
+    tt(c255, c255, A(j128, 0, 1), OP.add)
+    ts(A(IDT, 0, 128), A(J, 15, 143), wlo, OP.mult, c255, OP.add)
+    ts(A(bi, 0, 32), A(c16, 0, 32), whi, OP.mult, 8.0, OP.mult)
+    for w in (128, 256):
+        ops[act(A(IDT, w, 2 * w), A(IDT, 0, w), A(bi, w // 128, w // 128 + 1))]["early"] = C["early"]
+    for k in range(1, 8):
+        o, bb = A(IDT, 512 * k, 512 * k + 512), A(bi, 4 * k, 4 * k + 1)
+        if k <= C["idv"]:
+            ts(o, A(IDT, 0, 512), bb, OP.add)
+        else:
+            act(o, A(IDT, 0, 512), bb)
+    hc, lc, q256 = F(256), F(256), F(1)
+    for k in range(4):
+        iota(A(IDT, 4096 + 1024 * k, 5120 + 1024 * k), [[1, 1024]], 4096 + 1024 * k + int(lift), 0)
+    iota(A(hc, 0, 256), [[128, 2], [0, 128]], 4096 + 256, 0)
+    iota(A(lc, 0, 256), [[0, 2], [-1, 128]], 256, 0)
+    ts(A(q256, 0, 1), q, 256.0, OP.mult)
+    act(A(hc, 0, 256), A(hc, 0, 256), A(q256, 0, 1))
+    dma("Y", T.IDT[0:128:16, 4096:8192], A(hc, 0, 256)["ap"], 131072, ins=[A(hc, 0, 256), A(IDT, 4096, 8192)], outs=[A(IDT, 4096, 4100)])
+    dma("Y", T.IDT[2:128:16, 4096:8192], A(lc, 0, 256)["ap"], 131072, ins=[A(lc, 0, 256), A(IDT, 4100, 8192)], outs=[A(IDT, 4100, 4104)])
+    ts(A(kf, 0, 256), A(kd, 0, 256), -255.0, OP.add)
+    dma("Y", T.IDT[3:128:16, 0:4096], A(kf, 0, 256)["ap"], 131072, ins=[A(kf, 0, 256)], outs=[A(IDT, 0, 4096)])
+
+    R, ru = [F(32), F(32)], U(32)
+    for par in range(2):
+        for s in range(2):
+            cp(A(R[par], 16 * s, 16 * s + 16), A(ro, 16 * par, 16 * par + 16))
+    cp(A(ru, 0, 32), A(ro, 0, 32))
+    V = [[F(160), F(160)] for _ in range(4)]
+    O = [[U(128), U(128)] for _ in range(4)]
+    for par in range(2):
+        cp(A(O[0][par], 0, 32), A(ne, 32 * par, 32 * par + 32))
+        cp(A(V[0][par], 0, 32), A(ne, 32 * par, 32 * par + 32))
+    dead, DD = [None, None], [None, None]
+    z = [[B(256), B(256)] for _ in range(3)]
+    sg = [[B(512), B(512)], [B(512), B(512)]]
+    xg = [[B(512), B(512)], [B(512), B(512)]]
+    cm = [B(2048), B(2048)]
+    zoff = [None, [U(16), U(16)], [U(16), U(16)]]
+    lod = [None, B(256), B(256)]
+    YW, YO = F(1536), F(1536)
+
+    def w2l(out, lo, wide, a, k, lhs, start=True, stop=True, more=()):
+        o = A(out, lo, lo + k // 16)
+        lst = [(o, L(lhs, i), A(wide, a + i, a + k, 16), start and i == 0, stop and i == 15) for i in range(16)]
+        return lst[:1] + list(more) + lst[1:]
+
+    def step(t, par, k):
+        w = 32
+        v, o, s = V[t][par], O[t][par], sg[par][k % 2]
+        act(A(s, 0, 16 * w), IND(STW, A(o, 32 * k - 32, 32 * k - 32 + w)))
+        prev = A(R[par], 0, 32) if k == 1 else A(v, 32 * k - 64, 32 * k - 64 + w)
+        if C["st"] and k < 4:
+            mm(w2l(PATH[par], 0, s, 0, 16 * w, Bm[0], more=[(A(PATH[par], 0, w), full(In), prev, False, False)]))
+            ts(A(o, 32 * k, 32 * k + 32), A(PATH[par], 0, w), 4095.0, OP.min)
+            act(A(v, 32 * k, 32 * k + w), A(PATH[par], 0, w))
+            return
+        mm(w2l(PATH[par], 0, s, 0, 16 * w, Bm[0]))
+        tt(A(v, 32 * k, 32 * k + w), A(PATH[par], 0, w), prev, OP.subtract)
+        if k < 4:
+            ts(A(o, 32 * k, 32 * k + 32), A(v, 32 * k, 32 * k + 32), 4095.0, OP.min)
+
+    def demand(t, par):
+        zz = A(z[t][par], 0, 256)
+        if t == 0:
+            act(zz, IND(A(d0, 0, 512), A(zo, 16 * par, 16 * par + 16)))
+        else:
+            act(zz, IND(A(DW[t], 256 * par, 256 * par + 768), A(zoff[t][par], 0, 16)))
+        if t < 2:
+            if par == 0:
+                send(zz, A(DW[t + 1], 0, 256), 65536)
+            else:
+                lo_ = lod[t + 1]
+                send(zz, A(lo_, 0, 256), 65536)
+                for a, b_ in ((slice(16, 128), slice(0, 112)), (slice(0, 16), slice(112, 128))):
+                    dma("Y", A(DW[t + 1], 768, 1024, p=a)["ap"], A(lo_, 0, 256, p=b_)["ap"], 60000,
+                        ins=[A(lo_, 0, 256)], outs=[A(DW[t + 1], 768 + (a.start > 0) * 128, 896 + (a.start > 0) * 128)])
+        role = 0 if par == t % 2 else 1
+        if any(C["pre"][t][4 * role:4 * role + 4]):
+            mm([(A(ZB[par], 256 * s, 256 * s + 256), A(Id, 15, 143), zz, True, True) for s in range(2)])
+
+    def look(t, par, k):
+        role = 0 if par == t % 2 else 1
+        o = O[t][par]
+        if C["pre"][t][4 * role + k]:
+            xx = A(xg[par][k % 2], 0, 512)
+            act(xx, IND(XW, A(o, 32 * k, 32 * k + 32)))
+            tt(A(cm[par], 512 * k, 512 * k + 512), xx, A(ZB[par], 0, 512), OP.is_ge)
+        else:
+            for s in range(2):
+                tt(A(cm[par], 512 * k + 256 * s, 512 * k + 256 * s + 256), IND(XW, A(o, 32 * k + 16 * s, 32 * k + 16 * s + 16)),
+                   A(z[t][par], 0, 256), OP.is_ge)
+
+    def decide(t, par):
+        isp = par == t % 2
+        v, cn = V[t][par], CNT[par]
+        fl, NG, E, PR, D, Wl, hit, emb, Bl = B(48), B(96), F(128), F(192), F(64), F(32), F(32), F(32), F(64)
+        for k in range(4):
+            look(t, par, k)
+        tt(A(fl, 0, 16), A(v, 32, 48), A(v, 16, 32), OP.is_equal)
+        tt(A(fl, 16, 32), A(v, 64, 80), A(v, 16, 32), OP.is_equal)
+        more = [(A(cn, 64, 80), full(I32), A(fl, 0, 16), False, False)]
+        if C["c3"][0 if isp else 1]:
+            mm(w2l(cn, 0, cm[par], 0, 1536, Bc, more=more))
+        else:
+            mm(w2l(cn, 0, cm[par], 0, 1024, Bc))
+            mm(w2l(cn, 64, cm[par], 1024, 512, Bc, more=more))
+        ts(A(NG, 0, 96), A(cn, 0, 96), 8.5, OP.is_lt)
+        tt(A(NG, 32, 64), A(NG, 32, 64), A(NG, 0, 32), OP.mult)
+        tt(A(NG, 64, 96), A(NG, 64, 96), A(NG, 32, 64), OP.mult)
+        more = [(A(cn, 96, 112), full(I32), A(fl, 16 * i, 16 * i + 16), False, False) for i in range(2)]
+        if dead[par] is not None:
+            more.append((A(cn, 96, 112), full(I512), A(dead[par], 0, 16), False, False))
+        mm(w2l(cn, 96, cm[par], 1536, 512, Bc, stop=False, more=more))
+        if C["E"]:
+            E = (MA[0], 128)
+            mm(lin([(A(E, 0, 128), 1, A(v, 32, 160)), (A(E, 0, 128), -1, A(v, 0, 128))]))
+        elif C["split"][0 if isp else 1]:
+            tt(A(E, 0, 96), A(v, 32, 128), A(v, 0, 96), OP.subtract)
+            tt(A(E, 96, 128), A(v, 128, 160), A(v, 96, 128), OP.subtract)
+        else:
+            tt(A(E, 0, 128), A(v, 32, 160), A(v, 0, 128), OP.subtract)
+        Dv = []
+        for i in range(2):
+            tt(A(PR, 96 * i, 96 * i + 96), A(E, 32 * i, 32 * i + 96), A(NG, 0, 96), OP.mult)
+            Dv.append(A(comb(C["lD"], PATH[par], 64 + 32 * i, 32, [(1, A(PR, 96 * i + 32 * k, 96 * i + 32 * k + 32)) for k in range(3)]), 0, 32))
+        tt(A(Wl, 0, 32), Dv[0], A(v, 0, 32), OP.add)
+        tt(A(fl, 32, 48), A(Wl, 0, 16), A(Wl, 16, 32), OP.is_equal)
+        mm([(A(cn, 96, 112), full(I512), A(fl, 32, 48), False, False), (A(cn, 96, 128), full(I256), A(NG, 64, 96), False, True)])
+        ts(A(hit, 0, 32), A(cn, 96, 128), -247.5, OP.is_gt)
+        for s in range(2):
+            tt(A(emb, 16 * s, 16 * s + 16), A(hit, 0, 16), A(hit, 16, 32), OP.mult)
+        for i in range(2):
+            tt(A(Bl, 32 * i, 32 * i + 32), Dv[i], A(emb, 0, 32), OP.mult)
+        nv, no = V[t + 1][par], O[t + 1][par]
+        tt(A(nv, 0, 64), A(Bl, 0, 64), A(v, 0, 64), OP.add)
+        if isp or t < 2:
+            ts(A(no, 0, 64), A(nv, 0, 64), 4095.0, OP.min)
+        return {"W": Wl, "emb": emb, "nv": nv, "no": no}
+
+    def flags(t, par, emb):
+        tf, uo = F(16), U(16)
+        ts(A(tf, 0, 16), A(emb, 0, 16), 0.5, OP.is_lt, dl1 if par else dl0, OP.mult)
+        o = A(CNT[par], 128, 144)
+        mv = [(o, full(m_), A(tf, 0, 16), False, False) for m_ in ((Sh, Sh2) if par else (Ip,))]
+        mm([(o, full(Ip), A(base, 16 * par, 16 * par + 16), True, False)] + mv[:-1] + [mv[-1][:4] + (True,)])
+        cp(A(uo, 0, 16), o)
+        send(A(uo, 0, 16), A(zoff[t + 1][par], 0, 16), 4096)
+
+    def targets(par, nv, no, out):
+        if DD[par] is None:
+            return A(no, 0, 32)
+        tmp = F(32)
+        tt(A(tmp, 0, 32), A(nv, 0, 32), A(DD[par], 0, 32), OP.max)
+        cp(out, A(tmp, 0, 32))
+        return out
+
+    def results(par, nv, deadnow):
+        yu = U(48)
+        cp(A(yu, 0, 32), A(nv, 0, 32))
+        ts(A(yu, 32, 48), A(deadnow, 0, 16), 0.5, OP.is_lt)
+        act(A(YW, 768 * par, 768 * par + 768), IND(IDW, A(yu, 0, 48)))
+
+    for par in range(2):
+        demand(0, par)
+    for k in range(1, 5):
+        step(0, 0, k)
+        step(0, 1, k)
+
+    for t in range(3):
+        P, K = t % 2, 1 - t % 2
+        last = t == 2
+        d = decide(t, P)
+        nv, no, emb = d["nv"], d["no"], d["emb"]
+        if not last:
+            flags(t, P, emb)
+        vu, cn = U(64), CNT[P]
+        nval = 48 if last else 32
+        pts = [(0, 32, [(1, A(nv, 32, 64)), (1, A(R[P], 0, 32))]), (32, 48, [(1, A(nv, 0, 16)), (1, A(nv, 16, 32))])]
+        ts(A(vu, 0, nval), A(comb(C["lP"], cn, 160, nval, [], pts[:1 + last]), 0, nval), 8191.0, OP.min)
+        gw = B(512)
+        act(A(gw, 0, 256), IND(A(IDT, 0, 4096), A(no, 0, 16)), scale=A(mk, 3, 4))
+        act(A(gw, 256, 512), IND(A(IDT, 0, 4096), A(no, 32, 48)), scale=A(mk, 5, 6))
+        mm(w2l(MB, 64, gw, 0, 256, Bm[2]))
+        k1, k2, ku = F(16), F(16), U(16)
+        ts(A(k1, 0, 16), A(emb, 0, 16), -512.0, OP.mult, 512.0, OP.add)
+        tt(A(k2, 0, 16), A(MB, 64, 80), A(k1, 0, 16), OP.is_lt)
+        tt(A(k2, 0, 16), A(k2, 0, 16), A(dumpl, 0, 16), OP.mult)
+        tt(A(k1, 0, 16), A(MB, 64, 80), A(k2, 0, 16), OP.max)
+        cp(A(ku, 0, 16), A(k1, 0, 16))
+        tt(IND(A(LW[t], 0, 768), A(ku, 0, 16)), A(gw, 0, 256), A(gw, 256, 512), OP.add)
+        lst = []
+        for u in range(2):
+            for i in range(16):
+                a = 256 * (i % 2) + (i - i % 2) + K
+                lst.append((A(MB, 16 * u, 16 * u + 16), L(Bm[u], i), A(LW[t], a, a + 241, 16), i == 0, i == 15))
+        mm(lst)
+        LL, lu, sv = F(32), U(32), B(512)
+        cp(A(lu, 0, 32), A(MB, 0, 32))
+        (cp if C["llv"] else act)(A(LL, 0, 32), A(MB, 0, 32))
+        pw, pu = F(768), U(32)
+        act(A(pw, 0, 16 * nval), IND(IDW, A(vu, 0, nval)))
+        put(C["silu"][t][0], targets(P, nv, no, A(pu, 0, 32)), A(pw, 0, 512))
+        act(A(sv, 0, 512), IND(STW, A(lu, 0, 32)))
+        svm = w2l(MA, 0, sv, 0, 512, Bm[0], stop=not C["lS"])
+        if last:
+            put(C["silu"][3][0], A(ru, 16 * P, 16 * P + 16), A(pw, 512, 768))
+            results(P, nv, dead[P])
+        d = decide(t, K)
+        nv, no, emb, Wl = d["nv"], d["no"], d["emb"], d["W"]
+        if not last:
+            flags(t, K, emb)
+        wu, x1, kc = U(32), B(256), B(256)
+        ts(A(wu, 0, 32), A(Wl, 0, 32), 4095.0, OP.min)
+        act(A(x1, 0, 256), IND(XW, A(wu, 16, 32)))
+        tt(A(kc, 0, 256), IND(XW, A(wu, 0, 16)), A(x1, 0, 256), OP.is_ge)
+        kp, tk, ot, fg, sp, vu, of, ou = F(16), F(32), F(32), F(16), B(32), U(80), F(32), U(64)
+        w0, w1, pv, pb = A(Wl, 0, 16), A(Wl, 16, 32), A(LL, 0, 16), A(LL, 16, 32)
+        tw, tv, cn = A(tk, 0, 16), A(tk, 16, 32), CNT[K]
+        dd = comb(C["ld"], MB, 160, 32, [], [(0, 16, [(1, w0), (-1, w1)]), (16, 32, [(1, pv), (-1, pb)])])
+        ts(A(fg, 0, 16), A(dd, 16, 32), 0.0, OP.not_equal)
+        mm(svm)
+        if C["lS"]:
+            mm(lin([(A(MA, 0, 16), 1, w1), (A(MA, 0, 16), -1, pb), (A(MA, 16, 32), 1, w0), (A(MA, 16, 32), -1, pv), None], False))
+        else:
+            cd = comb(0, None, 0, 32, [(1, A(MA, 0, 32))], [(0, 16, [(1, w1), (-1, pb)]), (16, 32, [(1, w0), (-1, pv)])])
+        mm(w2l(MB, 128, kc, 0, 256, Bc))
+        ts(A(kp, 0, 16), A(MB, 128, 144), 8.5, OP.is_gt)
+        for s in range(2):
+            tt(A(tk, 16 * s, 16 * s + 16), A(dd, 16 * s, 16 * s + 16), A(kp, 0, 16), OP.mult)
+        if C["lS"]:
+            mm(lin([(A(MA, 0, 16), 1, tw), (A(MA, 16, 32), -1, tw)], False))
+            cd = MA
+        else:
+            cd = comb(0, None, 0, 32, [], [(0, 16, [(1, A(cd, 0, 16)), (1, tw)]), (16, 32, [(1, A(cd, 16, 32)), (-1, tw)])])
+        ts(A(vu, 32, 64), A(cd, 0, 32), 8191.0, OP.min)
+        o0 = comb(C["lo"], MB, 192, 32, [(-1, A(R[K], 0, 32))], [(0, 16, [(1, pb), (1, tv)]), (16, 32, [(1, pv), (-1, tv)])])
+        for s in range(2):
+            tt(A(sp, 16 * s, 16 * s + 16), A(fg, 0, 16), A(emb, 0, 16), OP.mult)
+        tt(A(ot, 0, 32), A(o0, 0, 32), A(sp, 0, 32), OP.mult)
+        if last:
+            cp(A(vu, 64, 80), A(comb(C["lv"], cn, 192, 16, [(1, A(nv, 0, 16)), (1, A(nv, 16, 32))]), 0, 16))
+        vl = comb(C["lv"], cn, 160, 32, [(1, A(nv, 32, 64)), (1, A(R[K], 0, 32)), (1, A(ot, 0, 32))])
+        ts(A(vu, 0, 32), A(vl, 0, 32), 8191.0, OP.min)
+        o2, sd = F(32), F(32)
+        tt(A(sd, 0, 32), A(sp, 0, 32), A(dump, 0, 32), OP.mult)
+        tt(A(o2, 0, 32), A(dump, 0, 32), A(sd, 0, 32), OP.subtract)
+        tt(A(of, 0, 32), A(o2, 0, 32), A(LL, 0, 32), OP.max)
+        cp(A(ou, 32, 64), A(of, 0, 32))
+        tg = targets(K, nv, no, A(ou, 0, 32))
+        kw = F(1280)
+        act(A(kw, 512, 1024), IND(IDW, A(vu, 32, 64)))
+        act(A(kw, 0, 512), IND(IDW, A(vu, 0, 32)))
+        nd = sp
+        if dead[K] is not None:
+            nd = B(16)
+            tt(A(nd, 0, 16), A(dead[K], 0, 16), A(sp, 0, 16), OP.max)
+        if not last:
+            DD[K] = sd
+            for k in range(2, 2 + C["nb"][t]):
+                step(t + 1, K, k)
+        else:
+            act(A(kw, 1024, 1280), IND(IDW, A(vu, 64, 80)))
+            put(C["silu"][3][1], A(ru, 16 * K, 16 * K + 16), A(kw, 1024, 1280))
+        dead[K] = nd
+        put(C["silu"][t][1], A(ou, 32, 64), A(kw, 512, 1024))
+        put(C["silu"][t][2], tg, A(kw, 0, 512))
+        if not last:
+            demand(t + 1, P)
+            demand(t + 1, K)
+            for k in range(1, 5):
+                step(t + 1, P, k)
+            for k in range(2 + C["nb"][t], 5):
+                step(t + 1, K, k)
+        else:
+            results(K, nv, nd)
+            act(A(YO, 0, 1024), IND(A(YW, 0, 1536), A(yo, 0, 64)), m1k)
+            act(A(YO, 1024, 1536), IND(A(YW, 0, 1536), A(yo, 64, 96)), m1k)
+            rows = slice(1, 128, 16)
+            dma("Y", T.yn[:], A(YO, 0, 1024, p=rows)["ap"], 32768, ins=[A(YO, 0, 1024)])
+            dma("Y", T.yl[:], A(YO, 1024, 1536, p=rows)["ap"], 16384, ins=[A(YO, 1024, 1536)])
+            if lift:
+                yc = A(F(256), 0, 256)
+                dma("Y", yc["ap"], A(ST, 0, 4096, p=rows)["ap"], 131072, ins=[STW], outs=[yc])
+                ts(yc, yc, 12582912.0 - lift, OP.add, 12582912.0, OP.subtract)
+                dma("Y", T.ys[:], yc["ap"], 131072, ins=[yc])
+            else:
+                dma("Y", T.ys[:], A(ST, 0, 4096, p=rows)["ap"], 131072, ins=[STW])
+
+    if "t0" not in INFO:
+        INFO["t0"], INFO["end"] = arrange(ops, C["lat"], C["iters"])
+    order = {e: [] for e in "VSPGYN"}
+    for i in sorted(range(len(ops)), key=lambda j: (INFO["t0"][j], j)):
+        ops[i]["t0"] = INFO["t0"][i]
+        order[ops[i]["eng"]].append(i)
+    prev = None
+    for i in order["G"]:
+        if ops[i]["kind"] == "c":
+            if prev is not None:
+                ops[i]["deps"].add(prev)
+            prev = i
+    INFO["busy"] = {e: sum(ops[i]["cost"] for i in order[e]) for e in order}
+    INFO["ops"] = ops
+    INFO["order"] = order
+    INFO["top"] = dict(top)
+
+    tot = {}
+    for e in "VSPG":
+        c = 0
+        for i in order[e]:
+            if ops[i]["kind"] == "c":
+                c += ops[i].get("k", 1)
+                ops[i]["done"] = ("s" + e, c)
+        tot["s" + e] = c
+    for o in ops:
+        if o["kind"] == "d":
+            o["done"] = (o["sem"], 16)
+            tot[o["sem"]] = 16
+        elif o["kind"] == "r":
+            o["done"] = (o["sem"], n_in)
+            tot[o["sem"]] = n_in
+    tot["sent"] = n_out * nsem["r"]
+    queue = {"V": g.vector, "S": g.scalar, "P": g.tensor, "G": g, "Y": g.sync}
+    for e in "YSVPG":
+        seen = {}
+        for i in order[e]:
+            o = ops[i]
+            need = {}
+            for j in o["deps"]:
+                if e == "P" and ops[j]["eng"] == "P":
+                    continue
+                s, c = ops[j]["done"]
+                need[s] = max(need.get(s, 0), c)
+            for s in sorted(need):
+                if need[s] > seen.get(s, 0):
+                    queue[e].wait_ge(T.sem[s], need[s])
+                    seen[s] = need[s]
+            for ins in o["fn"]():
+                if o["kind"] == "c":
+                    ins.then_inc(T.sem["s" + e], 1)
+                elif o["kind"] == "d":
+                    ins.then_inc(T.sem[o["sem"]], 16)
+        if e == "G":
+            for s in sorted(tot):
+                if tot[s] > seen.get(s, 0):
+                    g.wait_ge(T.sem[s], tot[s])

@@ -22,9 +22,9 @@ CFG = {
     "idv": 2,
     "lD": 0, "lP": 0, "ld": 0, "lS": 0, "lo": 0, "lv": 0, "E": 0, "st": 0, "c3": [1, 0],
     "silu": [[1, 0, 1], [1, 0, 1], [1, 0, 0], [1, 1]],
-    "early": 1, "llv": 0, "cpv": 4,
-    "split": [0, 1],
-    "g": 1.62, "s": 3.95, "c": 1.04, "pe": 0.52, "lat": 80.0, "iters": 500,
+    "early": 1, "llv": 1, "cpv": 4,
+    "split": [1, 1],
+    "g": 0.83 * 1.3 * 1.7, "s": 0.83 * 1.3 * 4.4, "c": 0.83 * 1.3, "pe": 0.417 * 1.3, "lat": 150.0, "iters": 800,
 }
 INFO = {}
 

@@ -17,14 +17,16 @@ NDMA = 40
 SEMAPHORES = ["sV", "sS", "sP", "sG", "sent"] + ["d%d" % i for i in range(NDMA)] + ["r%d" % i for i in range(8)]
 
 CFG = {
-    "pre": [[0, 0, 0, 0, 0, 0, 0, 0], [0, 0, 0, 0, 0, 0, 0, 0], [0, 0, 0, 0, 0, 0, 0, 0]],
+    "pre": [[0, 0, 0, 0, 0, 0, 0, 0], [0, 0, 1, 0, 0, 0, 0, 0], [0, 0, 0, 0, 0, 0, 1, 1]],
     "nb": [2, 2],
     "idv": 2,
-    "lD": 0, "lP": 0, "ld": 0, "lS": 0, "lo": 0, "lv": 0, "E": 0, "st": 0, "c3": [1, 0],
+    "lD": 0, "lP": 0, "ld": 0, "lS": 0, "lo": 0, "lv": 0, "E": 0, "st": 2, "c3": [1, 0],
     "silu": [[1, 0, 1], [1, 0, 1], [1, 0, 0], [1, 1]],
+    "nf": [0, 0, 0], "cx": [1, 1, 1], "ide": 0,
+    "ps": [0, 0, 0], "win": 10000.0, "tol": 0.003,
     "early": 1, "llv": 1, "cpv": 4,
     "split": [1, 1],
-    "g": 0.83 * 1.3 * 1.7, "s": 0.83 * 1.3 * 4.4, "c": 0.83 * 1.3, "pe": 0.417 * 1.3, "lat": 150.0, "iters": 800,
+    "g": 0.83 * 1.3 * 1.6, "s": 0.83 * 1.3 * 3.8, "c": 0.83 * 1.3, "pe": 0.417 * 1.3, "lat": 200.0, "iters": 700,
 }
 INFO = {}
 
@@ -50,7 +52,7 @@ def arrange(ops, lat, iters):
             i = m[1]
             t = tail[i] if back else 0.0
             for j in before[i]:
-                x = t0[j] + cost[j] + (tail[i] if back else tail[j])
+                x = t0[j] + cost[j] + (0.0 if eng[i] == eng[j] == "P" else tail[i] if back else tail[j])
                 if x > t:
                     t = x
             b, c = busy[eng[i]], cost[i]
@@ -81,9 +83,12 @@ def arrange(ops, lat, iters):
     for it in range(iters):
         amp = 0.0 if it < 4 else (200.0, 600.0, 1500.0, 4000.0)[it % 4]
         nz = rng.random(N) * amp
+        if it >= iters // 4:
+            a = rng.random() * cur[1]
+            nz = nz * (np.abs(np.array(cur[0]) - a) < CFG["win"])
         tb, _ = place([-(cur[0][i] + cost[i]) + nz[i] for i in range(N)], True)
         new = place([-(tb[i] + cost[i]) - early[i] for i in range(N)], False)
-        if new[1] <= cur[1] * (1.0 + 0.006 * (1.0 - it / iters)):
+        if new[1] <= cur[1] * (1.0 + CFG["tol"] * (1.0 - it / iters)):
             cur = new
         if new[1] < best[1]:
             best = new
@@ -263,7 +268,7 @@ def rank_program(g, core, T, topo):
         for f in fs:
             o, i_ = A(Z, f, 1024, 16, p=half), A(ones, 64 * (f // 2), 64 * (f // 2) + 64, p=half)
             me = add("G", lambda o=o, i_=i_: [g.affine_select(o["ap"], i_["ap"], [[-1, 8], [-8, 8]], OP.is_equal, 0.0, 0, 1)], [i_], [o], 350)
-            ops[me]["early"] = 1.5 * C["early"]
+            ops[me]["early"] = 6 * C["early"]
     pi, J, cols = al("LI", 48), F(144), F(16)
     ops[iota(A(pi, 0, 1), [[0, 1]], 0, 1)]["early"] = 2 * C["early"]
     ops[iota(A(J, 0, 144), [[1, 144]], -15, -1)]["early"] = 2 * C["early"]
@@ -329,10 +334,11 @@ def rank_program(g, core, T, topo):
     ts(A(Sh2, 0, 128), A(J, 15, 143), -112.0, OP.is_equal)
     L = lambda b_, k: A(b_, 15 - k, 143 - k)
     full = lambda b_: A(b_, 0, 128)
-    c16, dump, dumpl, base, zo, yi, yo = F(64), F(64), F(16), F(32), U(32), F(96), U(96)
+    c16, dump, dumpl, base, zo, yi, yo = F(64), F(64), F(48), F(32), U(32), F(96), U(96)
     iota(A(c16, 0, 64), [[16, 64]], 0, 0)
     ts(A(dump, 0, 64), A(c16, 0, 64), q, OP.add, 4096.0, OP.add)
-    ts(A(dumpl, 0, 16), A(c16, 0, 16), q, OP.add, 512.0, OP.add)
+    act(A(dumpl, 0, 32), A(dump, 0, 32))
+    ts(A(dumpl, 32, 48), A(c16, 0, 16), q, OP.add, 512.0, OP.add)
     ts(A(base, 0, 16), A(c16, 0, 16), qz, OP.add, 256.0, OP.add)
     ts(A(base, 16, 32), A(c16, 0, 16), qz, OP.add, 1.0, OP.add)
     ts(A(zo, 0, 16), A(base, 0, 16), -256.0, OP.add)
@@ -355,6 +361,7 @@ def rank_program(g, core, T, topo):
     for c0 in (0, 256):
         for k in range(8):
             mm([(A(PS[k], c0, c0 + 256), A(Z, 128 * k, 128 * k + 128), A(nb_, c0, c0 + 256), True, True)])
+            ops[-1]["early"] = 4 * C["early"] * (c0 == 0)
     for k in range(8):
         o = A(ST, 512 * k, 512 * k + 512)
         if not (k % 2 and k < 2 * C["cpv"]):
@@ -369,22 +376,29 @@ def rank_program(g, core, T, topo):
     ts(A(j128, 0, 1), A(J, 15, 16), wlo, OP.mult, -1.0, OP.mult)
     tt(c255, c255, A(j128, 0, 1), OP.add)
     ts(A(IDT, 0, 128), A(J, 15, 143), wlo, OP.mult, c255, OP.add)
-    ts(A(bi, 0, 32), A(c16, 0, 32), whi, OP.mult, 8.0, OP.mult)
+    ts(whi, whi, 128.0, OP.mult)
+    ts(A(bi, 0, 32), A(J, 15, 47), A(J, 15, 16), OP.subtract, whi, OP.mult)
     for w in (128, 256):
-        ops[act(A(IDT, w, 2 * w), A(IDT, 0, w), A(bi, w // 128, w // 128 + 1))]["early"] = C["early"]
+        ops[act(A(IDT, w, 2 * w), A(IDT, 0, w), A(bi, w // 128, w // 128 + 1))]["early"] = 5 * C["early"]
     for k in range(1, 8):
         o, bb = A(IDT, 512 * k, 512 * k + 512), A(bi, 4 * k, 4 * k + 1)
         if k <= C["idv"]:
             ts(o, A(IDT, 0, 512), bb, OP.add)
         else:
             act(o, A(IDT, 0, 512), bb)
+        ops[-1]["early"] = C["early"] * (k <= C["ide"])
     hc, lc, q256 = F(256), F(256), F(1)
     for k in range(4):
         iota(A(IDT, 4096 + 1024 * k, 5120 + 1024 * k), [[1, 1024]], 4096 + 1024 * k + int(lift), 0)
     iota(A(hc, 0, 256), [[128, 2], [0, 128]], 4096 + 256, 0)
     iota(A(lc, 0, 256), [[0, 2], [-1, 128]], 256, 0)
     ts(A(q256, 0, 1), q, 256.0, OP.mult)
-    act(A(hc, 0, 256), A(hc, 0, 256), A(q256, 0, 1))
+    if lift:
+        used.append(1)
+        add("S", lambda: [g.scalar.activation(A(hc, 0, 256)["ap"], A(hc, 0, 256)["ap"], AF.Silu, bias=A(q256, 0, 1)["ap"])],
+            [A(hc, 0, 256), A(q256, 0, 1)], [A(hc, 0, 256)], 1900)
+    else:
+        act(A(hc, 0, 256), A(hc, 0, 256), A(q256, 0, 1))
     dma("Y", T.IDT[0:128:16, 4096:8192], A(hc, 0, 256)["ap"], 131072, ins=[A(hc, 0, 256), A(IDT, 4096, 8192)], outs=[A(IDT, 4096, 4100)])
     dma("Y", T.IDT[2:128:16, 4096:8192], A(lc, 0, 256)["ap"], 131072, ins=[A(lc, 0, 256), A(IDT, 4100, 8192)], outs=[A(IDT, 4100, 4104)])
     ts(A(kf, 0, 256), A(kd, 0, 256), -255.0, OP.add)
@@ -422,7 +436,7 @@ def rank_program(g, core, T, topo):
         if C["st"] and k < 4:
             mm(w2l(PATH[par], 0, s, 0, 16 * w, Bm[0], more=[(A(PATH[par], 0, w), full(In), prev, False, False)]))
             ts(A(o, 32 * k, 32 * k + 32), A(PATH[par], 0, w), 4095.0, OP.min)
-            act(A(v, 32 * k, 32 * k + w), A(PATH[par], 0, w))
+            (act if C["st"] == 1 else cp)(A(v, 32 * k, 32 * k + w), A(PATH[par], 0, w))
             return
         mm(w2l(PATH[par], 0, s, 0, 16 * w, Bm[0]))
         tt(A(v, 32 * k, 32 * k + w), A(PATH[par], 0, w), prev, OP.subtract)
@@ -495,6 +509,9 @@ def rank_program(g, core, T, topo):
             Dv.append(A(comb(C["lD"], PATH[par], 64 + 32 * i, 32, [(1, A(PR, 96 * i + 32 * k, 96 * i + 32 * k + 32)) for k in range(3)]), 0, 32))
         tt(A(Wl, 0, 32), Dv[0], A(v, 0, 32), OP.add)
         tt(A(fl, 32, 48), A(Wl, 0, 16), A(Wl, 16, 32), OP.is_equal)
+        Xl, ed = F(32), F(64)
+        tt(A(Xl, 0, 32), Dv[1], A(v, 32, 64), OP.add)
+        tt(A(ed, 0, 32), A(Wl, 0, 32), A(dump, 0, 32), OP.subtract)
         mm([(A(cn, 96, 112), full(I512), A(fl, 32, 48), False, False), (A(cn, 96, 128), full(I256), A(NG, 64, 96), False, True)])
         ts(A(hit, 0, 32), A(cn, 96, 128), -247.5, OP.is_gt)
         for s in range(2):
@@ -503,9 +520,9 @@ def rank_program(g, core, T, topo):
             tt(A(Bl, 32 * i, 32 * i + 32), Dv[i], A(emb, 0, 32), OP.mult)
         nv, no = V[t + 1][par], O[t + 1][par]
         tt(A(nv, 0, 64), A(Bl, 0, 64), A(v, 0, 64), OP.add)
-        if isp or t < 2:
+        if t < 2:
             ts(A(no, 0, 64), A(nv, 0, 64), 4095.0, OP.min)
-        return {"W": Wl, "emb": emb, "nv": nv, "no": no}
+        return {"W": Wl, "X": Xl, "emb": emb, "nv": nv, "e": ed}
 
     def flags(t, par, emb):
         tf, uo = F(16), U(16)
@@ -540,24 +557,29 @@ def rank_program(g, core, T, topo):
         P, K = t % 2, 1 - t % 2
         last = t == 2
         d = decide(t, P)
-        nv, no, emb = d["nv"], d["no"], d["emb"]
+        nv, emb, ed = d["nv"], d["emb"], d["e"]
         if not last:
             flags(t, P, emb)
-        vu, cn = U(64), CNT[P]
-        nval = 48 if last else 32
-        pts = [(0, 32, [(1, A(nv, 32, 64)), (1, A(R[P], 0, 32))]), (32, 48, [(1, A(nv, 0, 16)), (1, A(nv, 16, 32))])]
-        ts(A(vu, 0, nval), A(comb(C["lP"], cn, 160, nval, [], pts[:1 + last]), 0, nval), 8191.0, OP.min)
+        vu, cn, wu = U(64), CNT[P], U(32)
+        ts(A(vu, 0, 32), A(comb(C["lP"], cn, 160, 32, [(1, A(d["X"], 0, 32)), (1, A(R[P], 0, 32))]), 0, 32), 8191.0, OP.min)
+        if last:
+            cp(A(vu, 32, 48), A(comb(C["lP"], cn, 192, 16, [(1, A(nv, 0, 16)), (1, A(nv, 16, 32))]), 0, 16))
+        ts(A(wu, 0, 16), A(d["W"], 0, 16), 4095.0, OP.min)
+        ts(A(wu, 16, 32), A(d["X"], 0, 16), 4095.0, OP.min)
         gw = B(512)
-        act(A(gw, 0, 256), IND(A(IDT, 0, 4096), A(no, 0, 16)), scale=A(mk, 3, 4))
-        act(A(gw, 256, 512), IND(A(IDT, 0, 4096), A(no, 32, 48)), scale=A(mk, 5, 6))
+        act(A(gw, 0, 256), IND(A(IDT, 0, 4096), A(wu, 0, 16)), scale=A(mk, 3, 4))
+        act(A(gw, 256, 512), IND(A(IDT, 0, 4096), A(wu, 16, 32)), scale=A(mk, 5, 6))
         mm(w2l(MB, 64, gw, 0, 256, Bm[2]))
-        k1, k2, ku = F(16), F(16), U(16)
-        ts(A(k1, 0, 16), A(emb, 0, 16), -512.0, OP.mult, 512.0, OP.add)
-        tt(A(k2, 0, 16), A(MB, 64, 80), A(k1, 0, 16), OP.is_lt)
-        tt(A(k2, 0, 16), A(k2, 0, 16), A(dumpl, 0, 16), OP.mult)
-        tt(A(k1, 0, 16), A(MB, 64, 80), A(k2, 0, 16), OP.max)
-        cp(A(ku, 0, 16), A(k1, 0, 16))
-        tt(IND(A(LW[t], 0, 768), A(ku, 0, 16)), A(gw, 0, 256), A(gw, 256, 512), OP.add)
+        k1, k2, of, pu = F(16), F(16), F(48), U(48)
+        ts(A(k1, 0, 16), A(MB, 64, 80), -0.5, OP.is_gt)
+        tt(A(k2, 0, 16), A(MB, 64, 80), A(dumpl, 32, 48), OP.subtract)
+        tt(A(ed, 32, 48), A(k1, 0, 16), A(k2, 0, 16), OP.mult)
+        tt(A(of, 0, 32), A(ed, 0, 32), A(emb, 0, 32), OP.mult)
+        tt(A(of, 32, 48), A(ed, 32, 48), A(emb, 0, 16), OP.mult)
+        for a, b_ in ((0, 32), (32, 48)) if C["ps"][t] else ((0, 48),):
+            tt(A(of, a, b_), A(of, a, b_), A(dumpl, a, b_), OP.add)
+            cp(A(pu, a, b_), A(of, a, b_))
+        tt(IND(A(LW[t], 0, 768), A(pu, 32, 48)), A(gw, 0, 256), A(gw, 256, 512), OP.add)
         lst = []
         for u in range(2):
             for i in range(16):
@@ -567,32 +589,34 @@ def rank_program(g, core, T, topo):
         LL, lu, sv = F(32), U(32), B(512)
         cp(A(lu, 0, 32), A(MB, 0, 32))
         (cp if C["llv"] else act)(A(LL, 0, 32), A(MB, 0, 32))
-        pw, pu = F(768), U(32)
-        act(A(pw, 0, 16 * nval), IND(IDW, A(vu, 0, nval)))
-        put(C["silu"][t][0], targets(P, nv, no, A(pu, 0, 32)), A(pw, 0, 512))
+        pw = F(768)
+        act(A(pw, 0, 512), IND(IDW, A(vu, 0, 32)))
+        put(C["silu"][t][0], A(pu, 0, 32), A(pw, 0, 512))
         act(A(sv, 0, 512), IND(STW, A(lu, 0, 32)))
         svm = w2l(MA, 0, sv, 0, 512, Bm[0], stop=not C["lS"])
         if last:
+            act(A(pw, 512, 768), IND(IDW, A(vu, 32, 48)))
             put(C["silu"][3][0], A(ru, 16 * P, 16 * P + 16), A(pw, 512, 768))
             results(P, nv, dead[P])
         d = decide(t, K)
-        nv, no, emb, Wl = d["nv"], d["no"], d["emb"], d["W"]
+        nv, emb, Wl, ed = d["nv"], d["emb"], d["W"], d["e"]
         if not last:
             flags(t, K, emb)
         wu, x1, kc = U(32), B(256), B(256)
         ts(A(wu, 0, 32), A(Wl, 0, 32), 4095.0, OP.min)
         act(A(x1, 0, 256), IND(XW, A(wu, 16, 32)))
         tt(A(kc, 0, 256), IND(XW, A(wu, 0, 16)), A(x1, 0, 256), OP.is_ge)
-        kp, tk, ot, fg, sp, vu, of, ou = F(16), F(32), F(32), F(16), B(32), U(80), F(32), U(64)
+        kp, tk, ot, fg, sp, vu, of, ou = F(16), F(32), F(32), F(32), B(32), U(80), F(32), U(64)
         w0, w1, pv, pb = A(Wl, 0, 16), A(Wl, 16, 32), A(LL, 0, 16), A(LL, 16, 32)
         tw, tv, cn = A(tk, 0, 16), A(tk, 16, 32), CNT[K]
         dd = comb(C["ld"], MB, 160, 32, [], [(0, 16, [(1, w0), (-1, w1)]), (16, 32, [(1, pv), (-1, pb)])])
-        ts(A(fg, 0, 16), A(dd, 16, 32), 0.0, OP.not_equal)
+        for s in range(2):
+            ts(A(fg, 16 * s, 16 * s + 16), A(dd, 16, 32), 0.0, OP.not_equal)
         mm(svm)
         if C["lS"]:
             mm(lin([(A(MA, 0, 16), 1, w1), (A(MA, 0, 16), -1, pb), (A(MA, 16, 32), 1, w0), (A(MA, 16, 32), -1, pv), None], False))
         else:
-            cd = comb(0, None, 0, 32, [(1, A(MA, 0, 32))], [(0, 16, [(1, w1), (-1, pb)]), (16, 32, [(1, w0), (-1, pv)])])
+            cd = comb(0, None, 0, 32, [(1, A(MA, 0, 32))][C["cx"][t]:], [(0, 16, [(1, w1), (-1, pb)]), (16, 32, [(1, w0), (-1, pv)])])
         mm(w2l(MB, 128, kc, 0, 256, Bc))
         ts(A(kp, 0, 16), A(MB, 128, 144), 8.5, OP.is_gt)
         for s in range(2):
@@ -601,22 +625,23 @@ def rank_program(g, core, T, topo):
             mm(lin([(A(MA, 0, 16), 1, tw), (A(MA, 16, 32), -1, tw)], False))
             cd = MA
         else:
-            cd = comb(0, None, 0, 32, [], [(0, 16, [(1, A(cd, 0, 16)), (1, tw)]), (16, 32, [(1, A(cd, 16, 32)), (-1, tw)])])
+            cd = comb(0, None, 0, 32, [(1, A(MA, 0, 32))][:C["cx"][t]], [(0, 16, [(1, A(cd, 0, 16)), (1, tw)]), (16, 32, [(1, A(cd, 16, 32)), (-1, tw)])])
         ts(A(vu, 32, 64), A(cd, 0, 32), 8191.0, OP.min)
         o0 = comb(C["lo"], MB, 192, 32, [(-1, A(R[K], 0, 32))], [(0, 16, [(1, pb), (1, tv)]), (16, 32, [(1, pv), (-1, tv)])])
-        for s in range(2):
-            tt(A(sp, 16 * s, 16 * s + 16), A(fg, 0, 16), A(emb, 0, 16), OP.mult)
-        tt(A(ot, 0, 32), A(o0, 0, 32), A(sp, 0, 32), OP.mult)
+        tt(A(sp, 0, 16), A(fg, 0, 16), A(emb, 0, 16), OP.mult)
+        tt(A(ot, 0, 32), A(o0, 0, 32), A(fg, 0, 32), OP.mult)
         if last:
             cp(A(vu, 64, 80), A(comb(C["lv"], cn, 192, 16, [(1, A(nv, 0, 16)), (1, A(nv, 16, 32))]), 0, 16))
-        vl = comb(C["lv"], cn, 160, 32, [(1, A(nv, 32, 64)), (1, A(R[K], 0, 32)), (1, A(ot, 0, 32))])
+        vl = comb(C["lv"], cn, 160, 32, [(1, A(d["X"], 0, 32)), (1, A(R[K], 0, 32)), (1, A(ot, 0, 32))])
         ts(A(vu, 0, 32), A(vl, 0, 32), 8191.0, OP.min)
-        o2, sd = F(32), F(32)
-        tt(A(sd, 0, 32), A(sp, 0, 32), A(dump, 0, 32), OP.mult)
-        tt(A(o2, 0, 32), A(dump, 0, 32), A(sd, 0, 32), OP.subtract)
-        tt(A(of, 0, 32), A(o2, 0, 32), A(LL, 0, 32), OP.max)
-        cp(A(ou, 32, 64), A(of, 0, 32))
-        tg = targets(K, nv, no, A(ou, 0, 32))
+        o2, of = F(32), F(64)
+        tt(A(o2, 0, 32), A(LL, 0, 32), A(dump, 32, 64), OP.subtract)
+        tt(A(ed, 32, 64), A(o2, 0, 32), A(fg, 0, 32), OP.mult)
+        for i in range(2):
+            tt(A(of, 32 * i, 32 * i + 32), A(ed, 32 * i, 32 * i + 32), A(emb, 0, 32), OP.mult)
+        tt(A(of, 0, 64), A(of, 0, 64), A(dump, 0, 64), OP.add)
+        cp(A(ou, 0, 64), A(of, 0, 64))
+        tg = A(ou, 0, 32)
         kw = F(1280)
         act(A(kw, 512, 1024), IND(IDW, A(vu, 32, 64)))
         act(A(kw, 0, 512), IND(IDW, A(vu, 0, 32)))
@@ -625,15 +650,15 @@ def rank_program(g, core, T, topo):
             nd = B(16)
             tt(A(nd, 0, 16), A(dead[K], 0, 16), A(sp, 0, 16), OP.max)
         if not last:
-            DD[K] = sd
             for k in range(2, 2 + C["nb"][t]):
                 step(t + 1, K, k)
         else:
             act(A(kw, 1024, 1280), IND(IDW, A(vu, 64, 80)))
             put(C["silu"][3][1], A(ru, 16 * K, 16 * K + 16), A(kw, 1024, 1280))
         dead[K] = nd
-        put(C["silu"][t][1], A(ou, 32, 64), A(kw, 512, 1024))
-        put(C["silu"][t][2], tg, A(kw, 0, 512))
+        both = [(A(ou, 32, 64), A(kw, 512, 1024)), (tg, A(kw, 0, 512))]
+        for i in range(2):
+            put(C["silu"][t][1 + i], *both[i ^ C["nf"][t]])
         if not last:
             demand(t + 1, P)
             demand(t + 1, K)

@@ -17,23 +17,33 @@ NDMA = 40
 SEMAPHORES = ["sV", "sS", "sP", "sG", "sent"] + ["d%d" % i for i in range(NDMA)] + ["r%d" % i for i in range(8)]
 
 CFG = {
-    "pre": [[0, 0, 0, 0, 0, 0, 0, 0], [0, 0, 1, 0, 0, 0, 0, 0], [0, 0, 0, 0, 0, 0, 1, 1]],
-    "nb": [2, 2],
-    "idv": 2,
-    "lD": 0, "lP": 0, "ld": 0, "lS": 0, "lo": 0, "lv": 0, "E": 0, "st": 2, "c3": [1, 0],
+    "pre": [[0, 0, 0, 0, 0, 0, 0, 0], [0, 0, 0, 0, 0, 0, 0, 0], [0, 0, 0, 0, 0, 0, 1, 1]],
+    "nb": [[1, 1], [1, 1], [0, 1]], "pp": [[4, 4], [4, 4], [4, 4]],
+    "idv": 0, "ide": 2,
+    "lP": 0, "ld": 0, "lS": 0, "lv": 0, "c3": [1, 0],
     "silu": [[1, 0, 1], [1, 0, 1], [1, 0, 0], [1, 1]],
-    "nf": [0, 0, 0], "cx": [1, 1, 1], "ide": 0,
-    "ps": [0, 0, 0], "win": 10000.0, "tol": 0.003,
-    "early": 1, "llv": 1, "cpv": 4,
-    "split": [1, 1],
-    "g": 0.83 * 1.3 * 1.6, "s": 0.83 * 1.3 * 3.8, "c": 0.83 * 1.3, "pe": 0.417 * 1.3, "lat": 200.0, "iters": 700,
+    "nf": [1, 1, 1], "xl": [1, 1, 1], "ws": [1, 1, 1],
+    "zd": [[1, 1], [0, 1], [0, 1]],
+    "late4": [1, 1],
+    "fill": [1536, 1024], "vS": [0, 0], "d0S": 0, "llv": 1,
+    "win": 3000.0, "tol": 0.006, "seed": 1, "amp": (500.0, 1000.0, 2000.0, 4000.0),
+    "g": 0.83 * 1.35, "s": 0.83 * 2.8, "c": 0.83 * 1.15, "pe": 0.417 * 1.15, "lat": 200.0, "iters": 2500,
 }
 INFO = {}
+LIFT = 1024.0
 
 
 def arrange(ops, lat, iters):
     N = len(ops)
-    pred = [sorted(o["deps"]) for o in ops]
+    pred, anc = [], []
+    for o in ops:
+        keep, seen = [], 0
+        for j in sorted(o["deps"], reverse=True):
+            if not seen >> j & 1:
+                keep.append(j)
+                seen |= anc[j] | 1 << j
+        pred.append(keep)
+        anc.append(seen)
     succ = [[] for _ in range(N)]
     for i in range(N):
         for j in pred[i]:
@@ -79,9 +89,9 @@ def arrange(ops, lat, iters):
             early[j] = max(early[j], early[i])
     best = place([-pr[i] - early[i] for i in range(N)], False)
     cur = best
-    rng = np.random.default_rng(1)
+    rng = np.random.default_rng(CFG["seed"])
     for it in range(iters):
-        amp = 0.0 if it < 4 else (200.0, 600.0, 1500.0, 4000.0)[it % 4]
+        amp = 0.0 if it < 4 else CFG["amp"][it % 4]
         nz = rng.random(N) * amp
         if it >= iters // 4:
             a = rng.random() * cur[1]
@@ -106,7 +116,7 @@ def rank_program(g, core, T, topo):
     n_out, n_in = len(topo.engines(core, nxt)), len(topo.engines(prv, core))
     C = CFG
     ops, acc, top = [], {}, {"LF": 0, "LB": 0, "LU": 0, "LI": 0}
-    nsem, used = {"d": 0, "r": 0}, []
+    nsem = {"d": 0, "r": 0}
 
     def al(buf, k):
         a = top[buf]
@@ -118,7 +128,13 @@ def rank_program(g, core, T, topo):
         buf, a = b
         ps = p if p is not None else slice(0, 128)
         ap = T[buf][ps, a + lo:a + hi] if step == 1 else T[buf][ps, a + lo:a + hi:step]
-        return {"ap": ap, "rg": [(buf, a + lo, a + hi)], "n": len(range(lo, hi, step)), "buf": buf, "ind": False}
+        return {"ap": ap, "rg": [(buf, ((1 << (hi - lo + step - 1) // step * step) - 1) // ((1 << step) - 1) << a + lo)], "n": len(range(lo, hi, step)), "buf": buf, "ind": False}
+
+    def five(b, i0, i1, pos=4):
+        return A(b, 5 * i0 + pos, 5 * (i1 - 1) + pos + 1, 5)
+
+    def two(b, i0, i1, pos):
+        return A(b, 2 * i0 + pos, 2 * (i1 - 1) + pos + 1, 2)
 
     def IND(win, off):
         return {"ap": win["ap"].indirect(off["ap"]), "rg": win["rg"], "off": off["rg"], "n": 16 * off["n"], "buf": win["buf"], "ind": True}
@@ -134,17 +150,17 @@ def rank_program(g, core, T, topo):
         me = len(ops)
         deps = set(extra)
         for lst, w in ((rd, False), (wr, True)):
-            for buf, lo, hi in lst:
+            for buf, bits in lst:
                 psum = buf.startswith("PS")
-                for (l2, h2, o2, w2) in acc.get(buf, []):
+                for (b2, o2, w2) in acc.get(buf, []):
                     e2 = ops[o2]["eng"]
                     if psum and (e2 != eng or eng == "P"):
                         deps.add(o2)
-                    elif (w or w2) and l2 < hi and lo < h2:
+                    elif (w or w2) and bits & b2:
                         deps.add(o2)
         for lst, w in ((rd, False), (wr, True)):
-            for buf, lo, hi in lst:
-                acc.setdefault(buf, []).append((lo, hi, me, w))
+            for buf, bits in lst:
+                acc.setdefault(buf, []).append((bits, me, w))
         o = {"eng": eng, "fn": fn, "deps": deps, "cost": cost, "kind": kind, "lat": lat}
         if kind in ("d", "r"):
             o["sem"] = "%s%d" % (kind, nsem[kind])
@@ -152,19 +168,22 @@ def rank_program(g, core, T, topo):
         ops.append(o)
         return me
 
-    def vcost(out, ins, two):
+    def soon(k, i=-1):
+        ops[i]["early"] = k
+
+    def vcost(out, ins, two_):
         for a in ins:
             if isinstance(a, dict) and a["ind"]:
-                return 60 + C["g"] * a["n"]
+                return 55 + C["g"] * a["n"]
         if out["ind"]:
-            return 60 + C["s"] * out["n"]
-        full = [a for a in ins if isinstance(a, dict)]
+            return 55 + C["s"] * out["n"]
+        full_ = [a for a in ins if isinstance(a, dict)]
         f = 1.0
-        if two:
-            f = 1.0 if any(a["buf"].startswith("PS") for a in full) else 2.0
-        elif all(a["buf"] in ("LB", "LU", "XW") for a in full[:1] + [out]):
+        if two_:
+            f = 1.0 if any(a["buf"].startswith("PS") for a in full_) else 2.0
+        elif all(a["buf"] in ("LB", "LU", "XW") for a in full_ + [out]):
             f = 0.5
-        return 20 + C["c"] * max(64, f * out["n"])
+        return 5 + C["c"] * max(64, f * out["n"])
 
     def sc(x):
         return x["ap"] if isinstance(x, dict) else x
@@ -179,6 +198,9 @@ def rank_program(g, core, T, topo):
             fn = lambda: [g.vector.tensor_scalar(out["ap"], a["ap"], sc(s1), sc(s2), op0, op1)]
         return add("V", fn, [a, s1, s2], [out], vcost(out, [a], False))
 
+    def scan(out, a, b):
+        return add("V", lambda: [g.vector.tensor_tensor_scan(out["ap"], a["ap"], b["ap"], 0.0, OP.mult, OP.add)], [a, b], [out], vcost(out, [a, b], False))
+
     def cp(out, a):
         return add("V", lambda: [g.vector.tensor_copy(out["ap"], a["ap"])], [a], [out], vcost(out, [a], False))
 
@@ -186,7 +208,7 @@ def rank_program(g, core, T, topo):
         return add("V", lambda: [g.vector.memset(out["ap"], v)], [], [out], vcost(out, [], False))
 
     def act(out, a, bias=None, scale=None):
-        cost = 80 + (C["g"] if a["ind"] else C["c"]) * a["n"]
+        cost = 70 + C["g"] * a["n"] if a["ind"] else 40 + C["c"] * max(64, a["n"])
         if scale is not None:
             return add("S", lambda: [g.scalar.activation(out["ap"], a["ap"], AF.Identity, scale=sc(scale))], [a, scale], [out], cost)
         if bias is None:
@@ -199,9 +221,7 @@ def rank_program(g, core, T, topo):
         out = IND(STS, off)
         if not on_s:
             return cp(out, val)
-        used.append(1)
-        return add("S", lambda: [g.scalar.activation(out["ap"], val["ap"], AF.Silu)], [val], [out],
-                   80 + (1600 if len(used) == 1 else 0) + C["s"] * out["n"])
+        return add("S", lambda: [g.scalar.activation(out["ap"], val["ap"], AF.Silu)], [val], [out], 70 + C["s"] * out["n"])
 
     def mm(lst):
         def fn():
@@ -213,7 +233,7 @@ def rank_program(g, core, T, topo):
             return r
         k = sum(1 for i, m in enumerate(lst) if m[4] or i == len(lst) - 1)
         me = add("P", fn, [m[1] for m in lst] + [m[2] for m in lst], [m[0] for m in lst],
-                 40 + sum(C["pe"] * max(64, m[2]["n"]) * (4 if m[2]["buf"] == "LF" else 1) for m in lst), lat=60.0)
+                 10 + sum(C["pe"] * max(min(64, m[1]["n"]), m[2]["n"]) * (4 if m[2]["buf"] == "LF" else 1) for m in lst), lat=30.0)
         ops[me]["k"] = k
         return me
 
@@ -226,11 +246,14 @@ def rank_program(g, core, T, topo):
             fn = lambda: [g.iota(out["ap"], pat, base, cm)]
         else:
             fn = lambda: [g.iota(out["ap"], pat, base, cm, allow_small_or_imprecise_dtypes=True)]
-        return add("G", fn, [], [out], 160 + 2 * C["c"] * out["n"])
+        return add("G", fn, [], [out], 260 + 2 * C["c"] * out["n"])
+
+    def pick(out, a, pat, op, base):
+        return add("G", lambda: [g.affine_select(out["ap"], a["ap"], pat, op, 0.0, base, 1)], [a], [out], 300 + 2 * C["c"] * out["n"])
 
     def send(src, land, nbytes):
         sem = "r%d" % nsem["r"]
-        s = add("G", lambda: [g.remote_dma(land["ap"], src["ap"], T.sem[sem], T.sem.sent, pid, rid, mask_out)], [src], [], 200, "x")
+        s = add("G", lambda: [g.remote_dma(land["ap"], src["ap"], T.sem[sem], T.sem.sent, pid, rid, mask_out)], [src], [], 400, "x")
         return add("N", None, [], [land], 0, "r", 2500 + nbytes / 60.0, extra=[s])
 
     F = lambda k: al("LF", k)
@@ -240,76 +263,55 @@ def rank_program(g, core, T, topo):
     PATH, CNT, ZB, MA, MB = PS[0:2], PS[2:4], PS[4:6], PS[6], PS[7]
     XW, STW, STS, IDW = A(("XW", 0), 0, 4096), A(("ST", 0), 0, 4096), A(("ST", 0), 0, 5120), A(("IDT", 0), 0, 8192)
     ST, IDT = ("ST", 0), ("IDT", 0)
-    lo64, hi64 = slice(0, 64), slice(64, 128)
 
-    ns, kd, ro, ne = al("LI", 512), al("LI", 256), al("LI", 32), al("LI", 64)
-    dma("Y", A(ns, 0, 512, p=lo64)["ap"], T.nsum[:], 131072, outs=[A(ns, 0, 256)])
-    dma("S", A(ns, 0, 512, p=hi64)["ap"], T.nsum[:], 131072, outs=[A(ns, 256, 512)])
-    dma("S", XW["ap"], T.x[:], 1 << 20, outs=[XW])
-    d0 = B(512)
-    dma("Y", A(d0, 0, 512)["ap"], T.dem[:, 0:512], 400000, outs=[A(d0, 0, 512)])
+    ns, kd, ro, ne = al("LI", 256), al("LI", 256), al("LI", 32), al("LI", 64)
+    soon(30, dma("Y", A(ns, 0, 256)["ap"], T.nsum[:], 131072, outs=[A(ns, 0, 256)]))
     for par in range(2):
         for s in range(2):
             o = A(ne, 32 * par + 16 * s, 32 * par + 16 * s + 16)
-            dma("Y", o["ap"], T.nei[par::2, 32 * s:32 * s + 32], 8192, outs=[o])
+            soon(29, dma("YS"[par], o["ap"], T.nei[par::2, 32 * s:32 * s + 32], 8192, outs=[o]))
         o = A(ro, 16 * par, 16 * par + 16)
-        dma("Y", o["ap"], T.rho[par::2, :], 8192, outs=[o])
-    dma("Y", A(kd, 0, 256)["ap"], T.kid[:], 900000, outs=[A(kd, 0, 256)])
-    DW = [None, B(1024), B(1024)]
-    for t in (1, 2):
-        o = A(DW[t], 256, 768)
-        dma("Y", o["ap"], T.dem[:, 512 * t:512 * t + 512], 900000, outs=[o])
+        soon(28, dma("YS"[par], o["ap"], T.rho[par::2, :], 8192, outs=[o]))
+    d0 = B(512)
+    soon(27.5, dma("S", A(d0, 0, 512)["ap"], T.dem[:, 0:512], 131072, outs=[A(d0, 0, 512)]))
+    soon(27, dma("S", XW["ap"], T.x[:], 1 << 20, outs=[XW]))
+    DW = [None, [B(768), B(768)], [B(768), B(768)]]
 
-    Z, ones = B(1024), B(128)
-    ms(A(Z, 0, 1024), 0.0)
-    ms(A(ones, 0, 64), 1.0)
-    ms(A(ones, 64, 128), -1.0)
-    for half, fs in ((lo64, (0, 1)), (hi64, (1, 2))):
-        for f in fs:
-            o, i_ = A(Z, f, 1024, 16, p=half), A(ones, 64 * (f // 2), 64 * (f // 2) + 64, p=half)
-            me = add("G", lambda o=o, i_=i_: [g.affine_select(o["ap"], i_["ap"], [[-1, 8], [-8, 8]], OP.is_equal, 0.0, 0, 1)], [i_], [o], 350)
-            ops[me]["early"] = 6 * C["early"]
-    pi, J, cols = al("LI", 48), F(144), F(16)
-    ops[iota(A(pi, 0, 1), [[0, 1]], 0, 1)]["early"] = 2 * C["early"]
-    ops[iota(A(J, 0, 144), [[1, 144]], -15, -1)]["early"] = 2 * C["early"]
+    pi, J, Jc, cols = al("LI", 48), F(144), F(128), F(16)
+    soon(22, iota(A(pi, 0, 1), [[0, 1]], 0, 1))
+    soon(21, iota(A(Jc, 0, 128), [[1, 128]], 0, 0))
+    soon(20, iota(A(J, 0, 144), [[1, 144]], -15, -1))
     ts(A(pi, 16, 17), A(pi, 0, 1), 15, OP.bitwise_and)
-    ts(A(pi, 32, 33), A(pi, 0, 1), 1, OP.bitwise_and)
     col = lambda i: A(cols, i, i + 1)
-    q, h, qz, qy, dl0, dl1, wlo, whi, c255, c1k, m1k = [col(i) for i in range(11)]
-    lift = 1024.0 if any(sum(C["silu"], [])) else 0.0
-    if not lift:
-        c1k = m1k = None
+    q, wlo, whi, ca, cb, c1k = [col(i) for i in range(6)]
     cp(q, A(pi, 16, 17))
-    cp(h, A(pi, 32, 33))
-    ts(qz, h, 255.0, OP.mult, q, OP.add)
-    ts(qy, h, 767.0, OP.mult, q, OP.add)
-    ts(dl0, h, -255.0, OP.mult, -256.0, OP.add)
-    ts(dl1, h, -255.0, OP.mult, 511.0, OP.add)
-    i16, oh, mk = F(16), F(16), F(8)
-    ts(A(i16, 0, 1), A(J, 15, 16), q, OP.add)
-    ts(A(oh, 0, 16), A(J, 15, 31), A(i16, 0, 1), OP.is_equal)
+    oh, mk = F(16), F(8)
+    ts(A(oh, 0, 16), A(Jc, 0, 16), q, OP.is_equal)
     ts(wlo, A(oh, 1, 2), A(oh, 2, 3), OP.subtract, A(oh, 6, 7), OP.subtract)
     ts(whi, A(oh, 0, 1), A(oh, 1, 2), OP.add, A(oh, 4, 5), OP.add)
+    ts(ca, A(oh, 0, 1), A(oh, 2, 3), OP.add, A(oh, 4, 5), OP.add)
+    ts(cb, A(oh, 1, 2), LIFT / 256.0, OP.mult, A(oh, 6, 7), OP.add)
+    ts(ca, ca, cb, OP.add, 256.0, OP.mult)
+    ts(c1k, A(oh, 5, 6), 255.0, OP.mult, ca, OP.add)
     tt(A(mk, 0, 2), A(oh, 0, 8, 4), A(oh, 2, 8, 4), OP.subtract)
     tt(A(mk, 4, 6), A(oh, 0, 8, 4), A(oh, 2, 8, 4), OP.add)
     tt(A(mk, 2, 3), A(oh, 3, 4), A(oh, 5, 6), OP.add)
     tt(A(mk, 3, 4), A(mk, 4, 5), A(mk, 2, 3), OP.add)
-    ts(A(mk, 6, 7), A(mk, 4, 5), A(mk, 5, 6), OP.add, 256.0, OP.mult)
-    ts(c255, A(oh, 5, 6), 255.0, OP.mult, A(mk, 6, 7), OP.add)
-    if lift:
-        ts(c1k, A(oh, 1, 2), lift, OP.mult)
-        ms(m1k, -lift)
-        tt(c255, c255, c1k, OP.add)
     Bc, Id = B(144), B(144)
     Bm = [B(144) for _ in range(3)]
     ts(A(Bc, 0, 144), A(J, 0, 144), q, OP.add, 0.0, OP.is_equal)
     for u in range(3):
         act(A(Bm[u], 0, 144), A(Bc, 0, 144), scale=A(mk, u, u + 1))
     ts(A(Id, 0, 144), A(J, 0, 144), 0.0, OP.is_equal)
-    I32, I256, I512, Sh, Sh2, Ip, In = B(128), B(128), B(128), F(128), F(128), F(128), F(128)
-    act(A(Ip, 0, 128), A(Id, 15, 143))
-    if any(C[k] for k in ("ld", "lS", "lo", "E", "st")):
-        act(A(In, 0, 128), A(Id, 15, 143), scale=-1.0)
+    I32, I64, I256, I512, Sh, Sh2, Ip, In, In2 = B(128), B(128), B(128), B(128), B(128), B(128), F(128), F(128), F(128)
+    if any(C[k] for k in ("lP", "ld", "lS", "lv")):
+        act(A(Ip, 0, 128), A(Id, 15, 143))
+    for b_, v in ((In, -1.0), (In2, -2.0), (I32, -32.0), (I64, -64.0), (I256, -256.0), (I512, -512.0)):
+        act(A(b_, 0, 128), A(Id, 15, 143), scale=v)
+    ts(A(Sh, 0, 128), A(J, 15, 143), 16.0, OP.is_equal, -256.0, OP.mult)
+    ts(A(Sh2, 0, 128), A(J, 15, 143), -112.0, OP.is_equal, -256.0, OP.mult)
+    L = lambda b_, k: A(b_, 15 - k, 143 - k)
+    full = lambda b_: A(b_, 0, 128)
 
     def lin(terms, start=True):
         return [(m[0], A(Ip if m[1] > 0 else In, 0, 128), m[2], start and i == 0, i == len(terms) - 1) for i, m in enumerate(terms) if m]
@@ -328,80 +330,81 @@ def rank_program(g, core, T, topo):
                 tt(A(r, a, b), tm[0][1] if i == 1 else A(r, a, b), tm[i][1], OP.add if tm[i][0] > 0 else OP.subtract)
         return r
 
-    for b_, v in ((I32, -32.0), (I256, -256.0), (I512, -512.0)):
-        act(A(b_, 0, 128), A(Id, 15, 143), scale=v)
-    ts(A(Sh, 0, 128), A(J, 15, 143), 16.0, OP.is_equal)
-    ts(A(Sh2, 0, 128), A(J, 15, 143), -112.0, OP.is_equal)
-    L = lambda b_, k: A(b_, 15 - k, 143 - k)
-    full = lambda b_: A(b_, 0, 128)
-    c16, dump, dumpl, base, zo, yi, yo = F(64), F(64), F(48), F(32), U(32), F(96), U(96)
-    iota(A(c16, 0, 64), [[16, 64]], 0, 0)
-    ts(A(dump, 0, 64), A(c16, 0, 64), q, OP.add, 4096.0, OP.add)
-    act(A(dumpl, 0, 32), A(dump, 0, 32))
-    ts(A(dumpl, 32, 48), A(c16, 0, 16), q, OP.add, 512.0, OP.add)
-    ts(A(base, 0, 16), A(c16, 0, 16), qz, OP.add, 256.0, OP.add)
-    ts(A(base, 16, 32), A(c16, 0, 16), qz, OP.add, 1.0, OP.add)
-    ts(A(zo, 0, 16), A(base, 0, 16), -256.0, OP.add)
-    cp(A(zo, 16, 32), A(base, 16, 32))
-    iota(A(yi, 0, 96), [[256, 3], [1, 2], [16, 16]], 0, 0)
-    ts(A(yo, 0, 96), A(yi, 0, 96), qy, OP.add)
-    LW = [B(768) for _ in range(3)]
-    for t in range(3):
-        iota(A(LW[t], 0, 512), [[0, 512]], 0, 0)
+    c2, dump, dumk, base, FD = F(128), F(64), F(16), B(16), F(224)
+    iota(A(c2, 0, 128), [[16, 64], [0, 2]], 0, 0)
+    ts(A(dump, 0, 64), two(c2, 0, 64, 0), q, OP.add, 4096.0, OP.add)
+    ts(A(dumk, 0, 16), two(c2, 0, 16, 0), q, OP.add, 512.0, OP.add)
+    ts(A(FD, 0, 128), A(c2, 0, 128), q, OP.add, 4096.0, OP.add)
+    act(A(FD, 128, 192), A(FD, 0, 64))
+    ts(A(FD, 192, 224), A(c2, 0, 32), q, OP.add, 512.0, OP.add)
+    FDK, FD2, FDP, FDL = [(FD[0], FD[1] + a) for a in (0, 64, 128, 192)]
+    act(A(base, 0, 16), two(c2, 0, 16, 0))
+    LW, Z0 = [B(768) for _ in range(3)], B(128)
+    if C["lS"]:
+        ms(A(Z0, 0, 128), 0.0)
+    NN, EZ, EB = B(352), B(320), [F(320), F(320)]
+    ms(A(NN, 0, 352), 1.0)
+    N = [(NN[0], NN[1] + 176 * par) for par in range(2)]
+    for par in range(2):
+        ms(five(N[par], 0, 32, 1), 0.0)
+        ms(five(EB[par], 0, 32, 0), 0.0)
+    ms(A(EZ, 0, 320), 0.0)
+    EM, SP = [(EZ[0], EZ[1] + 64 * i) for i in range(2)], [(EZ[0], EZ[1] + 64 * i) for i in range(2, 5)]
+    Sel = F(128)
+    ms(A(Sel, 0, 128), 1.0)
+    pick(A(Sel, 0, 128), A(Sel, 0, 128), [[-2, 8], [-16, 8], [-1, 2]], OP.is_equal, 0)
 
-    nb_, nt = B(512), al("LI", 0)
-    nsr = [A(ns, 0, 512)]
-    for c0 in (0, 256):
-        o = A(nb_, c0, c0 + 256)
-        i_ = A(ns, c0, c0 + 256)
-        add("V", lambda o=o, i_=i_: [g.vector.tensor_copy(o["ap"], i_["ap"])], nsr, [o], 20 + C["c"] * 256)
-        o = A(nb_, c0, c0 + 256, p=hi64)
-        i_ = A(ns, c0, c0 + 256, p=hi64)
-        add("V", lambda o=o, i_=i_: [g.vector.tensor_tensor(o["ap"], i_["ap"], o["ap"], OP.subtract)], nsr + [o], [o], 20 + C["c"] * 512)
-    for c0 in (0, 256):
-        for k in range(8):
-            mm([(A(PS[k], c0, c0 + 256), A(Z, 128 * k, 128 * k + 128), A(nb_, c0, c0 + 256), True, True)])
-            ops[-1]["early"] = 4 * C["early"] * (c0 == 0)
-    for k in range(8):
-        o = A(ST, 512 * k, 512 * k + 512)
-        if not (k % 2 and k < 2 * C["cpv"]):
-            act(o, A(PS[k], 0, 512), c1k)
-        elif lift:
-            ts(o, A(PS[k], 0, 512), c1k, OP.add)
-        else:
-            cp(o, A(PS[k], 0, 512))
-        ops[-1]["early"] = 3 * C["early"]
+    fa, fb = C["fill"]
+    for a in range(0, fa, 512):
+        soon(15, ms(A(ST, a, a + 512), 0.0))
+    if fb:
+        soon(15, iota(A(ST, fa, fa + fb), [[0, fb]], 0, 0))
+    for a in range(fa + fb, 4096, 512):
+        soon(15, act(A(ST, a, a + 512), A(ST, 0, 512)))
+    hi_, lo_, wh_ = A(F(256), 0, 256), A(F(256), 0, 256), A(F(256), 0, 256)
+    ts(hi_, A(ns, 0, 256), 1610612736.0, OP.add, 1610612736.0, OP.subtract)
+    tt(lo_, hi_, A(ns, 0, 256), OP.subtract)
+    ts(wh_, A(ns, 0, 256), LIFT, OP.add)
+    for r_, src in ((0, hi_), (2, lo_), (1, wh_)):
+        soon(14, dma("Y", T.ST[r_:128:16, 0:4096], src["ap"], 131072, ins=[src, A(ST, 16, 4096)], outs=[A(ST, 4 * r_, 4 * r_ + 4)]))
+    soon(13, dma("Y", A(kd, 0, 256)["ap"], T.kid[:], 131072, ins=[wh_], outs=[A(kd, 0, 256)]))
+    for t in (1, 2):
+        dr = B(512)
+        dma("Y", A(dr, 0, 512)["ap"], T.dem[:, 512 * t:512 * t + 512], 131072, ins=[A(kd, 0, 256)], outs=[A(dr, 0, 512)])
+        for par in range(2):
+            for hh in range(2):
+                pick(two(DW[t][par], 0, 128, hh), two(dr, 128 * hh, 128 * hh + 128, par), [[0, 128]], OP.is_ge, 0)
 
-    j128, bi, kf = F(128), F(64), F(256)
-    ts(A(j128, 0, 1), A(J, 15, 16), wlo, OP.mult, -1.0, OP.mult)
-    tt(c255, c255, A(j128, 0, 1), OP.add)
-    ts(A(IDT, 0, 128), A(J, 15, 143), wlo, OP.mult, c255, OP.add)
-    ts(whi, whi, 128.0, OP.mult)
-    ts(A(bi, 0, 32), A(J, 15, 47), A(J, 15, 16), OP.subtract, whi, OP.mult)
+    bi, kf = F(64), F(256)
+    ts(A(IDT, 0, 128), A(Jc, 0, 128), wlo, OP.mult, c1k, OP.add)
+    ts(A(bi, 0, 32), A(Jc, 0, 32), 128.0, OP.mult, whi, OP.mult)
     for w in (128, 256):
-        ops[act(A(IDT, w, 2 * w), A(IDT, 0, w), A(bi, w // 128, w // 128 + 1))]["early"] = 5 * C["early"]
+        soon(18, act(A(IDT, w, 2 * w), A(IDT, 0, w), A(bi, w // 128, w // 128 + 1)))
     for k in range(1, 8):
         o, bb = A(IDT, 512 * k, 512 * k + 512), A(bi, 4 * k, 4 * k + 1)
         if k <= C["idv"]:
             ts(o, A(IDT, 0, 512), bb, OP.add)
         else:
             act(o, A(IDT, 0, 512), bb)
-        ops[-1]["early"] = C["early"] * (k <= C["ide"])
+        soon(4 * (k <= C["ide"]))
     hc, lc, q256 = F(256), F(256), F(1)
     for k in range(4):
-        iota(A(IDT, 4096 + 1024 * k, 5120 + 1024 * k), [[1, 1024]], 4096 + 1024 * k + int(lift), 0)
+        iota(A(IDT, 4096 + 1024 * k, 5120 + 1024 * k), [[1, 1024]], 4096 + 1024 * k + int(LIFT), 0)
     iota(A(hc, 0, 256), [[128, 2], [0, 128]], 4096 + 256, 0)
     iota(A(lc, 0, 256), [[0, 2], [-1, 128]], 256, 0)
     ts(A(q256, 0, 1), q, 256.0, OP.mult)
-    if lift:
-        used.append(1)
-        add("S", lambda: [g.scalar.activation(A(hc, 0, 256)["ap"], A(hc, 0, 256)["ap"], AF.Silu, bias=A(q256, 0, 1)["ap"])],
-            [A(hc, 0, 256), A(q256, 0, 1)], [A(hc, 0, 256)], 1900)
-    else:
-        act(A(hc, 0, 256), A(hc, 0, 256), A(q256, 0, 1))
-    dma("Y", T.IDT[0:128:16, 4096:8192], A(hc, 0, 256)["ap"], 131072, ins=[A(hc, 0, 256), A(IDT, 4096, 8192)], outs=[A(IDT, 4096, 4100)])
-    dma("Y", T.IDT[2:128:16, 4096:8192], A(lc, 0, 256)["ap"], 131072, ins=[A(lc, 0, 256), A(IDT, 4100, 8192)], outs=[A(IDT, 4100, 4104)])
-    ts(A(kf, 0, 256), A(kd, 0, 256), -255.0, OP.add)
+    add("S", lambda: [g.scalar.activation(A(hc, 0, 256)["ap"], A(hc, 0, 256)["ap"], AF.Silu, bias=A(q256, 0, 1)["ap"])],
+        [A(hc, 0, 256), A(q256, 0, 1)], [A(hc, 0, 256)], 1700)
+    dma("Y", T.IDT[0:128:16, 4096:8192], A(hc, 0, 256)["ap"], 131072, ins=[A(hc, 0, 256), A(IDT, 4104, 8192)], outs=[A(IDT, 4096, 4100)])
+    dma("Y", T.IDT[2:128:16, 4096:8192], A(lc, 0, 256)["ap"], 131072, ins=[A(lc, 0, 256), A(IDT, 4104, 8192)], outs=[A(IDT, 4100, 4104)])
+    rn, rnu, k2 = al("LI", 32), U(32), A(al("LI", 256), 0, 256)
+    dma("Y", A(rn, 0, 32)["ap"], T.rho[:], 16384, ins=[wh_], outs=[A(rn, 0, 32)])
+    cp(A(rnu, 0, 32), A(rn, 0, 32))
+    act(A(LW[0], 0, 512), IND(A(IDT, 0, 4096), A(rnu, 0, 32)))
+    for t in (1, 2):
+        dma("Y", A(LW[t], 0, 512)["ap"], A(LW[0], 0, 512)["ap"], 131072, ins=[A(LW[0], 0, 512)], outs=[A(LW[t], 0, 512)])
+    ts(k2, A(kd, 0, 256), 1023, OP.bitwise_and)
+    ts(A(kf, 0, 256), k2, -255.0, OP.add)
     dma("Y", T.IDT[3:128:16, 0:4096], A(kf, 0, 256)["ap"], 131072, ins=[A(kf, 0, 256)], outs=[A(IDT, 0, 4096)])
 
     R, ru = [F(32), F(32)], U(32)
@@ -409,19 +412,19 @@ def rank_program(g, core, T, topo):
         for s in range(2):
             cp(A(R[par], 16 * s, 16 * s + 16), A(ro, 16 * par, 16 * par + 16))
     cp(A(ru, 0, 32), A(ro, 0, 32))
-    V = [[F(160), F(160)] for _ in range(4)]
-    O = [[U(128), U(128)] for _ in range(4)]
+    V3 = [F(32), F(32)]
+    O = [[U(128), U(128)] for _ in range(3)]
     for par in range(2):
         cp(A(O[0][par], 0, 32), A(ne, 32 * par, 32 * par + 32))
-        cp(A(V[0][par], 0, 32), A(ne, 32 * par, 32 * par + 32))
-    dead, DD = [None, None], [None, None]
-    z = [[B(256), B(256)] for _ in range(3)]
+        cp(five(EB[par], 0, 32), A(ne, 32 * par, 32 * par + 32))
+    dead = [None, None]
+    z = [[B(512), B(512)] for _ in range(3)]
     sg = [[B(512), B(512)], [B(512), B(512)]]
     xg = [[B(512), B(512)], [B(512), B(512)]]
     cm = [B(2048), B(2048)]
     zoff = [None, [U(16), U(16)], [U(16), U(16)]]
     lod = [None, B(256), B(256)]
-    YW, YO = F(1536), F(1536)
+    YO = F(768)
 
     def w2l(out, lo, wide, a, k, lhs, start=True, stop=True, more=()):
         o = A(out, lo, lo + k // 16)
@@ -429,36 +432,42 @@ def rank_program(g, core, T, topo):
         return lst[:1] + list(more) + lst[1:]
 
     def step(t, par, k):
-        w = 32
-        v, o, s = V[t][par], O[t][par], sg[par][k % 2]
-        act(A(s, 0, 16 * w), IND(STW, A(o, 32 * k - 32, 32 * k - 32 + w)))
-        prev = A(R[par], 0, 32) if k == 1 else A(v, 32 * k - 64, 32 * k - 64 + w)
-        if C["st"] and k < 4:
-            mm(w2l(PATH[par], 0, s, 0, 16 * w, Bm[0], more=[(A(PATH[par], 0, w), full(In), prev, False, False)]))
-            ts(A(o, 32 * k, 32 * k + 32), A(PATH[par], 0, w), 4095.0, OP.min)
-            (act if C["st"] == 1 else cp)(A(v, 32 * k, 32 * k + w), A(PATH[par], 0, w))
-            return
-        mm(w2l(PATH[par], 0, s, 0, 16 * w, Bm[0]))
-        tt(A(v, 32 * k, 32 * k + w), A(PATH[par], 0, w), prev, OP.subtract)
+        e, o, s, ps = EB[par], O[t][par], sg[par][k % 2], A(PATH[par], 0, 32)
+        v = [A(R[par], 0, 32), five(e, 0, 32), five(e, 32, 64), A(V3[par], 0, 32)]
+        act(A(s, 0, 512), IND(STW, A(o, 32 * k - 32, 32 * k)))
+        less = [(In, v[k - 1])] if k < 4 else [(In2, v[3]), (In, five(e, 0, 32, 1))]
+        mm([(ps, full(m_), x, i == 0, False) for i, (m_, x) in enumerate(less)])
+        mm(w2l(PATH[par], 0, s, 0, 512, Bm[0], start=False))
         if k < 4:
-            ts(A(o, 32 * k, 32 * k + 32), A(v, 32 * k, 32 * k + 32), 4095.0, OP.min)
+            ts(A(o, 32 * k, 32 * k + 32), ps, 4095.0, OP.min)
+            if k < 3:
+                (act if C["vS"][k - 1] else cp)(v[k + 1], ps)
+            tt(five(e, 0, 32, 4 - k), ps, v[k], OP.subtract)
+        elif not C["late4"][par != t % 2]:
+            cp(five(e, 0, 32, 0), ps)
 
     def demand(t, par):
         zz = A(z[t][par], 0, 256)
+        role = 0 if par == t % 2 else 1
         if t == 0:
-            act(zz, IND(A(d0, 0, 512), A(zo, 16 * par, 16 * par + 16)))
+            for hh in range(2):
+                (act if C["d0S"] else cp)(two(z[t][par], 0, 128, hh), two(d0, 128 * hh, 128 * hh + 128, par))
         else:
-            act(zz, IND(A(DW[t], 256 * par, 256 * par + 768), A(zoff[t][par], 0, 16)))
+            act(zz, IND(A(DW[t][par], 0, 768), A(zoff[t][par], 0, 16)))
+        if C["zd"][t][role]:
+            pick(A(z[t][par], 256, 512), zz, [[0, 256]], OP.is_ge, 0)
         if t < 2:
             if par == 0:
-                send(zz, A(DW[t + 1], 0, 256), 65536)
+                ld = A(DW[t + 1][0], 256, 512)
+                send(zz, ld, 65536)
+                dma("Y", A(DW[t + 1][0], 512, 768)["ap"], ld["ap"], 65536, ins=[ld], outs=[A(DW[t + 1][0], 512, 768)])
             else:
-                lo_ = lod[t + 1]
-                send(zz, A(lo_, 0, 256), 65536)
-                for a, b_ in ((slice(16, 128), slice(0, 112)), (slice(0, 16), slice(112, 128))):
-                    dma("Y", A(DW[t + 1], 768, 1024, p=a)["ap"], A(lo_, 0, 256, p=b_)["ap"], 60000,
-                        ins=[A(lo_, 0, 256)], outs=[A(DW[t + 1], 768 + (a.start > 0) * 128, 896 + (a.start > 0) * 128)])
-        role = 0 if par == t % 2 else 1
+                ld = lod[t + 1]
+                send(zz, A(ld, 0, 256), 65536)
+                for c0 in (256, 512):
+                    for a, b_ in ((slice(16, 128), slice(0, 112)), (slice(0, 16), slice(112, 128))):
+                        dma("Y", A(DW[t + 1][1], c0, c0 + 256, p=a)["ap"], A(ld, 0, 256, p=b_)["ap"], 60000,
+                            ins=[A(ld, 0, 256)], outs=[A(DW[t + 1][1], c0 + (a.start > 0) * 128, c0 + 128 + (a.start > 0) * 128)])
         if any(C["pre"][t][4 * role:4 * role + 4]):
             mm([(A(ZB[par], 256 * s, 256 * s + 256), A(Id, 15, 143), zz, True, True) for s in range(2)])
 
@@ -469,6 +478,8 @@ def rank_program(g, core, T, topo):
             xx = A(xg[par][k % 2], 0, 512)
             act(xx, IND(XW, A(o, 32 * k, 32 * k + 32)))
             tt(A(cm[par], 512 * k, 512 * k + 512), xx, A(ZB[par], 0, 512), OP.is_ge)
+        elif C["zd"][t][role]:
+            tt(A(cm[par], 512 * k, 512 * k + 512), IND(XW, A(o, 32 * k, 32 * k + 32)), A(z[t][par], 0, 512), OP.is_ge)
         else:
             for s in range(2):
                 tt(A(cm[par], 512 * k + 256 * s, 512 * k + 256 * s + 256), IND(XW, A(o, 32 * k + 16 * s, 32 * k + 16 * s + 16)),
@@ -476,110 +487,99 @@ def rank_program(g, core, T, topo):
 
     def decide(t, par):
         isp = par == t % 2
-        v, cn = V[t][par], CNT[par]
-        fl, NG, E, PR, D, Wl, hit, emb, Bl = B(48), B(96), F(128), F(192), F(64), F(32), F(32), F(32), F(64)
+        e, cn, nn, em = EB[par], CNT[par], N[par], EM[par]
+        fl, OS, hit, ed = B(48), F(320), B(32), FDP if isp else FDK
         for k in range(4):
             look(t, par, k)
-        tt(A(fl, 0, 16), A(v, 32, 48), A(v, 16, 32), OP.is_equal)
-        tt(A(fl, 16, 32), A(v, 64, 80), A(v, 16, 32), OP.is_equal)
+        tt(A(fl, 0, 32), five(e, 16, 48), five(e, 32, 64), OP.is_equal)
         more = [(A(cn, 64, 80), full(I32), A(fl, 0, 16), False, False)]
         if C["c3"][0 if isp else 1]:
             mm(w2l(cn, 0, cm[par], 0, 1536, Bc, more=more))
         else:
             mm(w2l(cn, 0, cm[par], 0, 1024, Bc))
+            for k in range(2):
+                ts(five(nn, 0, 32, 4 - k), A(cn, 32 * k, 32 * k + 32), 8.5, OP.is_lt)
             mm(w2l(cn, 64, cm[par], 1024, 512, Bc, more=more))
-        ts(A(NG, 0, 96), A(cn, 0, 96), 8.5, OP.is_lt)
-        tt(A(NG, 32, 64), A(NG, 32, 64), A(NG, 0, 32), OP.mult)
-        tt(A(NG, 64, 96), A(NG, 64, 96), A(NG, 32, 64), OP.mult)
+        for k in range(0 if C["c3"][0 if isp else 1] else 2, 3):
+            ts(five(nn, 0, 32, 4 - k), A(cn, 32 * k, 32 * k + 32), 8.5, OP.is_lt)
         more = [(A(cn, 96, 112), full(I32), A(fl, 16 * i, 16 * i + 16), False, False) for i in range(2)]
         if dead[par] is not None:
-            more.append((A(cn, 96, 112), full(I512), A(dead[par], 0, 16), False, False))
+            more.append((A(cn, 96, 112), full(I512), dead[par], False, False))
         mm(w2l(cn, 96, cm[par], 1536, 512, Bc, stop=False, more=more))
-        if C["E"]:
-            E = (MA[0], 128)
-            mm(lin([(A(E, 0, 128), 1, A(v, 32, 160)), (A(E, 0, 128), -1, A(v, 0, 128))]))
-        elif C["split"][0 if isp else 1]:
-            tt(A(E, 0, 96), A(v, 32, 128), A(v, 0, 96), OP.subtract)
-            tt(A(E, 96, 128), A(v, 128, 160), A(v, 96, 128), OP.subtract)
-        else:
-            tt(A(E, 0, 128), A(v, 32, 160), A(v, 0, 128), OP.subtract)
-        Dv = []
-        for i in range(2):
-            tt(A(PR, 96 * i, 96 * i + 96), A(E, 32 * i, 32 * i + 96), A(NG, 0, 96), OP.mult)
-            Dv.append(A(comb(C["lD"], PATH[par], 64 + 32 * i, 32, [(1, A(PR, 96 * i + 32 * k, 96 * i + 32 * k + 32)) for k in range(3)]), 0, 32))
-        tt(A(Wl, 0, 32), Dv[0], A(v, 0, 32), OP.add)
-        tt(A(fl, 32, 48), A(Wl, 0, 16), A(Wl, 16, 32), OP.is_equal)
-        Xl, ed = F(32), F(64)
-        tt(A(Xl, 0, 32), Dv[1], A(v, 32, 64), OP.add)
-        tt(A(ed, 0, 32), A(Wl, 0, 32), A(dump, 0, 32), OP.subtract)
-        mm([(A(cn, 96, 112), full(I512), A(fl, 32, 48), False, False), (A(cn, 96, 128), full(I256), A(NG, 64, 96), False, True)])
-        ts(A(hit, 0, 32), A(cn, 96, 128), -247.5, OP.is_gt)
-        for s in range(2):
-            tt(A(emb, 16 * s, 16 * s + 16), A(hit, 0, 16), A(hit, 16, 32), OP.mult)
-        for i in range(2):
-            tt(A(Bl, 32 * i, 32 * i + 32), Dv[i], A(emb, 0, 32), OP.mult)
-        nv, no = V[t + 1][par], O[t + 1][par]
-        tt(A(nv, 0, 64), A(Bl, 0, 64), A(v, 0, 64), OP.add)
+        scan(A(OS, 0, 160), A(nn, 0, 160), A(e, 0, 160))
+        tt(A(fl, 32, 48), five(OS, 0, 16), five(OS, 16, 32), OP.is_equal)
+        tt(two(ed, 0, 32, 0), five(OS, 0, 32), A(dump, 0, 32), OP.subtract)
+        if C["late4"][0 if isp else 1]:
+            cp(five(e, 0, 32, 0), A(PATH[par], 0, 32))
+        scan(A(OS, 160, 320), A(nn, 1, 161), A(e, 0, 160))
+        mm([(A(cn, 96, 128), full(I64), five(nn, 0, 32, 2 + i), False, False) for i in range(3)]
+           + [(A(cn, 96, 112), full(I512), A(fl, 32, 48), False, True)])
+        ts(A(hit, 0, 32), A(cn, 96, 128), -183.5, OP.is_gt)
         if t < 2:
-            ts(A(no, 0, 64), A(nv, 0, 64), 4095.0, OP.min)
-        return {"W": Wl, "X": Xl, "emb": emb, "nv": nv, "e": ed}
+            flags(t, par, hit)
+        for s in range(2):
+            tt(two(em, 16 * s, 16 * s + 16, 1), A(hit, 0, 16), A(hit, 16, 32), OP.mult)
+        return OS
 
-    def flags(t, par, emb):
-        tf, uo = F(16), U(16)
-        ts(A(tf, 0, 16), A(emb, 0, 16), 0.5, OP.is_lt, dl1 if par else dl0, OP.mult)
+    def move(t, par, OS):
+        k = 64 if t < 2 and par != t % 2 else 32
+        e, D = EB[par], F(64)
+        tt(A(D, 0, k), five(OS, 0, k), five(e, 0, k), OP.subtract)
+        for a in range(0, k, 32):
+            tt(A(D, a, a + 32), A(D, a, a + 32), two(EM[par], 0, 32, 1), OP.mult)
+        tt(five(e, 0, k), five(e, 0, k), A(D, 0, k), OP.add)
+        if t < 2:
+            ts(A(O[t + 1][par], 0, k), five(e, 0, k), 4095.0, OP.min)
+        if k == 64:
+            tt(five(e, 0, 32, 3), five(e, 32, 64), five(e, 0, 32), OP.subtract)
+
+    def flags(t, par, hit):
+        uo = U(16)
         o = A(CNT[par], 128, 144)
-        mv = [(o, full(m_), A(tf, 0, 16), False, False) for m_ in ((Sh, Sh2) if par else (Ip,))]
-        mm([(o, full(Ip), A(base, 16 * par, 16 * par + 16), True, False)] + mv[:-1] + [mv[-1][:4] + (True,)])
-        cp(A(uo, 0, 16), o)
+        mv = [(o, full(m_), A(hit, 16 * s, 16 * s + 16), False, False) for s in range(2) for m_ in ((Sh, Sh2) if par else (I256,))]
+        mm([(o, A(Id, 15, 143), A(base, 0, 16), True, False)] + mv[:-1] + [mv[-1][:4] + (True,)])
+        ts(A(uo, 0, 16), o, q, OP.add, 512.0, OP.add)
         send(A(uo, 0, 16), A(zoff[t + 1][par], 0, 16), 4096)
 
-    def targets(par, nv, no, out):
-        if DD[par] is None:
-            return A(no, 0, 32)
-        tmp = F(32)
-        tt(A(tmp, 0, 32), A(nv, 0, 32), A(DD[par], 0, 32), OP.max)
-        cp(out, A(tmp, 0, 32))
-        return out
+    def roots(par, on_s):
+        vu, w = U(16), F(256)
+        cp(A(vu, 0, 16), A(comb(C["lP"], CNT[par], 192, 16, [(1, five(EB[par], 0, 16)), (1, five(EB[par], 16, 32))]), 0, 16))
+        act(A(w, 0, 256), IND(IDW, A(vu, 0, 16)))
+        put(on_s, A(ru, 16 * par, 16 * par + 16), A(w, 0, 256))
 
-    def results(par, nv, deadnow):
-        yu = U(48)
-        cp(A(yu, 0, 32), A(nv, 0, 32))
-        ts(A(yu, 32, 48), A(deadnow, 0, 16), 0.5, OP.is_lt)
-        act(A(YW, 768 * par, 768 * par + 768), IND(IDW, A(yu, 0, 48)))
+    top16 = slice(0, 16)
+
+    def results(par):
+        lv = F(16)
+        ts(A(lv, 0, 16), dead[par], 0.5, OP.is_lt)
+        mm([(A(PATH[0], 2 * a + par, 512, 16, p=top16), A(Sel, 16 * a, 16 * a + 16), five(EB[par], 0, 32), True, True) for a in range(8)])
+        mm([(A(CNT[0], 256 + 2 * a + par, 512, 16, p=top16), A(Sel, 16 * a, 16 * a + 16), A(lv, 0, 16), True, True) for a in range(8)])
 
     for par in range(2):
         demand(0, par)
     for k in range(1, 5):
         step(0, 0, k)
-        step(0, 1, k)
 
     for t in range(3):
         P, K = t % 2, 1 - t % 2
         last = t == 2
-        d = decide(t, P)
-        nv, emb, ed = d["nv"], d["emb"], d["e"]
-        if not last:
-            flags(t, P, emb)
-        vu, cn, wu = U(64), CNT[P], U(32)
-        ts(A(vu, 0, 32), A(comb(C["lP"], cn, 160, 32, [(1, A(d["X"], 0, 32)), (1, A(R[P], 0, 32))]), 0, 32), 8191.0, OP.min)
-        if last:
-            cp(A(vu, 32, 48), A(comb(C["lP"], cn, 192, 16, [(1, A(nv, 0, 16)), (1, A(nv, 16, 32))]), 0, 16))
-        ts(A(wu, 0, 16), A(d["W"], 0, 16), 4095.0, OP.min)
-        ts(A(wu, 16, 32), A(d["X"], 0, 16), 4095.0, OP.min)
+        OS = decide(t, P)
+        pp, ps = C["pp"][t]
+        vu, cn, wu = U(32), CNT[P], U(48)
+        ts(A(vu, 0, 32), A(comb(C["lP"], cn, 160, 32, [(1, five(OS, 32, 64)), (1, A(R[P], 0, 32))]), 0, 32), 8191.0, OP.min)
+        for a, b_ in ((0, 16), (32, 48)) if C["ws"][t] else ((0, 48),):
+            ts(A(wu, a, b_), five(OS, a, b_), 4095.0, OP.min)
         gw = B(512)
         act(A(gw, 0, 256), IND(A(IDT, 0, 4096), A(wu, 0, 16)), scale=A(mk, 3, 4))
-        act(A(gw, 256, 512), IND(A(IDT, 0, 4096), A(wu, 16, 32)), scale=A(mk, 5, 6))
-        mm(w2l(MB, 64, gw, 0, 256, Bm[2]))
-        k1, k2, of, pu = F(16), F(16), F(48), U(48)
-        ts(A(k1, 0, 16), A(MB, 64, 80), -0.5, OP.is_gt)
-        tt(A(k2, 0, 16), A(MB, 64, 80), A(dumpl, 32, 48), OP.subtract)
-        tt(A(ed, 32, 48), A(k1, 0, 16), A(k2, 0, 16), OP.mult)
-        tt(A(of, 0, 32), A(ed, 0, 32), A(emb, 0, 32), OP.mult)
-        tt(A(of, 32, 48), A(ed, 32, 48), A(emb, 0, 16), OP.mult)
-        for a, b_ in ((0, 32), (32, 48)) if C["ps"][t] else ((0, 48),):
-            tt(A(of, a, b_), A(of, a, b_), A(dumpl, a, b_), OP.add)
-            cp(A(pu, a, b_), A(of, a, b_))
+        act(A(gw, 256, 512), IND(A(IDT, 0, 4096), A(wu, 32, 48)), scale=A(mk, 5, 6))
+        mm(w2l(MB, 64, gw, 0, 256, Bm[2], more=[(A(MB, 64, 80), full(In), A(dumk, 0, 16), False, False)]))
+        ts(two(FDL, 0, 16, 0), A(MB, 64, 80), 0.0, OP.min)
+        of, pu = F(96), U(48)
+        scan(A(of, 0, 64), A(EM[P], 0, 64), A(FDP, 0, 64))
+        scan(A(of, 64, 96), A(EM[P], 0, 32), A(FDL, 0, 32))
+        cp(A(pu, 0, 48), two(of, 0, 48, 1))
         tt(IND(A(LW[t], 0, 768), A(pu, 32, 48)), A(gw, 0, 256), A(gw, 256, 512), OP.add)
+        move(t, P, OS)
         lst = []
         for u in range(2):
             for i in range(16):
@@ -589,97 +589,94 @@ def rank_program(g, core, T, topo):
         LL, lu, sv = F(32), U(32), B(512)
         cp(A(lu, 0, 32), A(MB, 0, 32))
         (cp if C["llv"] else act)(A(LL, 0, 32), A(MB, 0, 32))
-        pw = F(768)
+        pw = F(512)
         act(A(pw, 0, 512), IND(IDW, A(vu, 0, 32)))
+        for k in range(1, pp + 1):
+            step(t, K, k)
         put(C["silu"][t][0], A(pu, 0, 32), A(pw, 0, 512))
+        for k in range(pp + 1, ps + 1):
+            step(t, K, k)
         act(A(sv, 0, 512), IND(STW, A(lu, 0, 32)))
-        svm = w2l(MA, 0, sv, 0, 512, Bm[0], stop=not C["lS"])
+        for k in range(ps + 1, 5):
+            step(t, K, k)
+        svm = w2l(MA, 0, sv, 0, 512, Bm[0], start=not C["lS"])
         if last:
-            act(A(pw, 512, 768), IND(IDW, A(vu, 32, 48)))
-            put(C["silu"][3][0], A(ru, 16 * P, 16 * P + 16), A(pw, 512, 768))
-            results(P, nv, dead[P])
-        d = decide(t, K)
-        nv, emb, Wl, ed = d["nv"], d["emb"], d["W"], d["e"]
-        if not last:
-            flags(t, K, emb)
+            roots(P, C["silu"][3][0])
+            results(P)
+        OS = decide(t, K)
         wu, x1, kc = U(32), B(256), B(256)
-        ts(A(wu, 0, 32), A(Wl, 0, 32), 4095.0, OP.min)
+        ts(A(wu, 0, 32), five(OS, 0, 32), 4095.0, OP.min)
         act(A(x1, 0, 256), IND(XW, A(wu, 16, 32)))
         tt(A(kc, 0, 256), IND(XW, A(wu, 0, 16)), A(x1, 0, 256), OP.is_ge)
-        kp, tk, ot, fg, sp, vu, of, ou = F(16), F(32), F(32), F(32), B(32), U(80), F(32), U(64)
-        w0, w1, pv, pb = A(Wl, 0, 16), A(Wl, 16, 32), A(LL, 0, 16), A(LL, 16, 32)
+        kp, tk, nf, vu, of, ou = F(16), F(32), F(16), U(64), F(128), U(64)
+        w0, w1, pv, pb, X = five(OS, 0, 16), five(OS, 16, 32), A(LL, 0, 16), A(LL, 16, 32), five(OS, 32, 64)
         tw, tv, cn = A(tk, 0, 16), A(tk, 16, 32), CNT[K]
-        dd = comb(C["ld"], MB, 160, 32, [], [(0, 16, [(1, w0), (-1, w1)]), (16, 32, [(1, pv), (-1, pb)])])
-        for s in range(2):
-            ts(A(fg, 16 * s, 16 * s + 16), A(dd, 16, 32), 0.0, OP.not_equal)
-        mm(svm)
+        dd = comb(C["ld"], ZB[P], 160, 32, [], [(0, 16, [(1, w0), (-1, w1)]), (16, 32, [(1, pv), (-1, pb)])])
+        tt(A(nf, 0, 16), pv, pb, OP.is_equal)
         if C["lS"]:
-            mm(lin([(A(MA, 0, 16), 1, w1), (A(MA, 0, 16), -1, pb), (A(MA, 16, 32), 1, w0), (A(MA, 16, 32), -1, pv), None], False))
+            mm([(A(MA, 0, 32), full(Z0), A(Z0, 0, 32), True, False)]
+               + lin([(A(MA, 0, 16), 1, w1), (A(MA, 0, 16), -1, pb), (A(MA, 16, 32), 1, w0), (A(MA, 16, 32), -1, pv), None], False))
         else:
-            cd = comb(0, None, 0, 32, [(1, A(MA, 0, 32))][C["cx"][t]:], [(0, 16, [(1, w1), (-1, pb)]), (16, 32, [(1, w0), (-1, pv)])])
-        mm(w2l(MB, 128, kc, 0, 256, Bc))
-        ts(A(kp, 0, 16), A(MB, 128, 144), 8.5, OP.is_gt)
+            mm(svm)
+            cd = comb(0, None, 0, 32, [], [(0, 16, [(1, w1), (-1, pb)]), (16, 32, [(1, w0), (-1, pv)])])
+        mm(w2l(ZB[P], 128, kc, 0, 256, Bc))
+        ts(A(kp, 0, 16), A(ZB[P], 128, 144), 8.5, OP.is_gt)
         for s in range(2):
             tt(A(tk, 16 * s, 16 * s + 16), A(dd, 16 * s, 16 * s + 16), A(kp, 0, 16), OP.mult)
         if C["lS"]:
-            mm(lin([(A(MA, 0, 16), 1, tw), (A(MA, 16, 32), -1, tw)], False))
+            mm(lin([(A(MA, 0, 16), 1, tw), (A(MA, 16, 32), -1, tw), None], False))
+            mm(svm)
             cd = MA
         else:
-            cd = comb(0, None, 0, 32, [(1, A(MA, 0, 32))][:C["cx"][t]], [(0, 16, [(1, A(cd, 0, 16)), (1, tw)]), (16, 32, [(1, A(cd, 16, 32)), (-1, tw)])])
+            cd = comb(0, None, 0, 32, [(1, A(MA, 0, 32))], [(0, 16, [(1, A(cd, 0, 16)), (1, tw)]), (16, 32, [(1, A(cd, 16, 32)), (-1, tw)])])
         ts(A(vu, 32, 64), A(cd, 0, 32), 8191.0, OP.min)
-        o0 = comb(C["lo"], MB, 192, 32, [(-1, A(R[K], 0, 32))], [(0, 16, [(1, pb), (1, tv)]), (16, 32, [(1, pv), (-1, tv)])])
-        tt(A(sp, 0, 16), A(fg, 0, 16), A(emb, 0, 16), OP.mult)
-        tt(A(ot, 0, 32), A(o0, 0, 32), A(fg, 0, 32), OP.mult)
-        if last:
-            cp(A(vu, 64, 80), A(comb(C["lv"], cn, 192, 16, [(1, A(nv, 0, 16)), (1, A(nv, 16, 32))]), 0, 16))
-        vl = comb(C["lv"], cn, 160, 32, [(1, A(d["X"], 0, 32)), (1, A(R[K], 0, 32)), (1, A(ot, 0, 32))])
+        if C["lv"]:
+            vl = comb(1, cn, 160, 32, [(1, X)], [(0, 16, [(1, pb), (1, tv)]), (16, 32, [(1, pv), (-1, tv)])])
+        elif C["xl"][t]:
+            vl = comb(0, None, 0, 32, [(1, X)], [(0, 16, [(1, pb), (1, tv)]), (16, 32, [(1, pv), (-1, tv)])])
+        else:
+            vl = comb(0, None, 0, 32, [], [(0, 16, [(1, pb), (1, five(OS, 32, 48)), (1, tv)]), (16, 32, [(1, pv), (1, five(OS, 48, 64)), (-1, tv)])])
         ts(A(vu, 0, 32), A(vl, 0, 32), 8191.0, OP.min)
-        o2, of = F(32), F(64)
-        tt(A(o2, 0, 32), A(LL, 0, 32), A(dump, 32, 64), OP.subtract)
-        tt(A(ed, 32, 64), A(o2, 0, 32), A(fg, 0, 32), OP.mult)
+        tt(two(FD2, 0, 32, 0), A(LL, 0, 32), A(dump, 32, 64), OP.subtract)
+        for s in range(2):
+            tt(two(SP[t], 16 * s, 16 * s + 16, 1), two(EM[K], 0, 16, 1), A(nf, 0, 16), OP.is_gt)
+        scan(A(of, 0, 64), A(EM[K], 0, 64), A(FDK, 0, 64))
+        scan(A(of, 64, 128), A(SP[t], 0, 64), A(FD2, 0, 64))
         for i in range(2):
-            tt(A(of, 32 * i, 32 * i + 32), A(ed, 32 * i, 32 * i + 32), A(emb, 0, 32), OP.mult)
-        tt(A(of, 0, 64), A(of, 0, 64), A(dump, 0, 64), OP.add)
-        cp(A(ou, 0, 64), A(of, 0, 64))
-        tg = A(ou, 0, 32)
-        kw = F(1280)
+            cp(A(ou, 32 * i, 32 * i + 32), two(of, 32 * i, 32 * i + 32, 1))
+        move(t, K, OS)
+        kw = F(1024)
         act(A(kw, 512, 1024), IND(IDW, A(vu, 32, 64)))
         act(A(kw, 0, 512), IND(IDW, A(vu, 0, 32)))
-        nd = sp
+        nd = two(SP[t], 0, 16, 1)
         if dead[K] is not None:
-            nd = B(16)
-            tt(A(nd, 0, 16), A(dead[K], 0, 16), A(sp, 0, 16), OP.max)
-        if not last:
-            for k in range(2, 2 + C["nb"][t]):
-                step(t + 1, K, k)
-        else:
-            act(A(kw, 1024, 1280), IND(IDW, A(vu, 64, 80)))
-            put(C["silu"][3][1], A(ru, 16 * K, 16 * K + 16), A(kw, 1024, 1280))
+            nd, old = A(B(16), 0, 16), nd
+            tt(nd, dead[K], old, OP.max)
         dead[K] = nd
-        both = [(A(ou, 32, 64), A(kw, 512, 1024)), (tg, A(kw, 0, 512))]
-        for i in range(2):
-            put(C["silu"][t][1 + i], *both[i ^ C["nf"][t]])
+        both = [(A(ou, 32, 64), A(kw, 512, 1024)), (A(ou, 0, 32), A(kw, 0, 512))]
+        cut = (0,) + tuple(C["nb"][t]) + (1 if last else 3,)
+        for i in range(3):
+            for k in range(cut[i], cut[i + 1]):
+                if last:
+                    roots(K, C["silu"][3][1])
+                else:
+                    step(t + 1, K, k + 2)
+            if i < 2:
+                put(C["silu"][t][1 + i], *both[i ^ C["nf"][t]])
         if not last:
             demand(t + 1, P)
             demand(t + 1, K)
-            for k in range(1, 5):
-                step(t + 1, P, k)
-            for k in range(2 + C["nb"][t], 5):
-                step(t + 1, K, k)
         else:
-            results(K, nv, nd)
-            act(A(YO, 0, 1024), IND(A(YW, 0, 1536), A(yo, 0, 64)), m1k)
-            act(A(YO, 1024, 1536), IND(A(YW, 0, 1536), A(yo, 64, 96)), m1k)
-            rows = slice(1, 128, 16)
-            dma("Y", T.yn[:], A(YO, 0, 1024, p=rows)["ap"], 32768, ins=[A(YO, 0, 1024)])
-            dma("Y", T.yl[:], A(YO, 1024, 1536, p=rows)["ap"], 16384, ins=[A(YO, 1024, 1536)])
-            if lift:
-                yc = A(F(256), 0, 256)
-                dma("Y", yc["ap"], A(ST, 0, 4096, p=rows)["ap"], 131072, ins=[STW], outs=[yc])
-                ts(yc, yc, 12582912.0 - lift, OP.add, 12582912.0, OP.subtract)
-                dma("Y", T.ys[:], yc["ap"], 131072, ins=[yc])
-            else:
-                dma("Y", T.ys[:], A(ST, 0, 4096, p=rows)["ap"], 131072, ins=[STW])
+            results(K)
+            act(A(YO, 0, 512, p=top16), A(PATH[0], 0, 512, p=top16))
+            act(A(YO, 512, 768, p=top16), A(CNT[0], 256, 512, p=top16))
+            for s in range(2):
+                dma("S", T.yn[:, 512 * s:512 * s + 512], A(YO, 256 * s, 256 * s + 256, p=top16)["ap"], 16384, ins=[A(YO, 0, 512)])
+            dma("S", T.yl[:], A(YO, 512, 768, p=top16)["ap"], 16384, ins=[A(YO, 512, 768)])
+            yc = A(F(256), 0, 256)
+            dma("Y", yc["ap"], A(ST, 0, 4096, p=slice(1, 128, 16))["ap"], 131072, ins=[STW], outs=[yc])
+            ts(yc, yc, 12582912.0 - LIFT, OP.add, 12582912.0, OP.subtract)
+            dma("Y", T.ys[:], yc["ap"], 131072, ins=[yc])
 
     if "t0" not in INFO:
         INFO["t0"], INFO["end"] = arrange(ops, C["lat"], C["iters"])

@@ -1,10 +1,11 @@
 import numpy as np
 from concourse.mybir import AluOpType as OP, ActivationFunctionType as AF
 
-NLF, NLB, NLU, NLI = 20480, 30720, 4096, 1024
+NLF, NLB, NLU, NLI = 16384, 27136, 2048, 1024
 SCRATCH = {
     "XW": ("sbuf", [128, 4096], "bfloat16"),
     "ST": ("sbuf", [128, 5120], "float32"),
+    "SB": ("sbuf", [128, 5120], "float32"),
     "IDT": ("sbuf", [128, 8192], "float32"),
     "LF": ("sbuf", [128, NLF], "float32"),
     "LB": ("sbuf", [128, NLB], "bfloat16"),
@@ -13,21 +14,23 @@ SCRATCH = {
 }
 for _b in range(8):
     SCRATCH["PS%d" % _b] = ("psum", [128, 512], "float32")
-NDMA = 40
+NDMA = 48
 SEMAPHORES = ["sV", "sS", "sP", "sG", "sent"] + ["d%d" % i for i in range(NDMA)] + ["r%d" % i for i in range(8)]
 
 CFG = {
     "pre": [[0, 0, 0, 0, 0, 0, 0, 0], [0, 0, 0, 0, 0, 0, 0, 0], [0, 0, 0, 0, 0, 0, 1, 1]],
-    "nb": [[1, 1], [1, 1], [0, 1]], "pp": [[4, 4], [4, 4], [4, 4]],
+    "cx": [0, 0, 0], "kv": [[0, 0], [0, 1], [1, 0]], "rf": [1, 1], "rv": [0, 0], "yp": 1, "kl": 1, "kfe": 0, "ige": 0, "sb": 3, "sbe": 1, "sk": [3, 3], "df": 1,
+    "nb": [[1, 1], [1, 1], [0, 0]], "pp": [[4, 4], [4, 4], [4, 4]],
     "idv": 0, "ide": 2,
-    "lP": 0, "ld": 0, "lS": 0, "lv": 0, "c3": [1, 0],
-    "silu": [[1, 0, 1], [1, 0, 1], [1, 0, 0], [1, 1]],
-    "nf": [1, 1, 1], "xl": [1, 1, 1], "ws": [1, 1, 1],
-    "zd": [[1, 1], [0, 1], [0, 1]],
+    "lP": 0, "ld": 0, "lS": 0, "lv": 0, "c3": [0, 0],
+    "silu": [[1, 0, 1], [1, 0, 1], [1, 1, 0], [1, 1]],
+    "nf": [1, 1, 1], "xl": [1, 1, 1], "ws": [1, 1, 1], "sw": [2, 2, 2], "b4": 1,
+    "zd": [[0, 0], [0, 0], [0, 0]],
     "late4": [1, 1],
-    "fill": [1536, 1024], "vS": [0, 0], "d0S": 0, "llv": 1,
-    "win": 3000.0, "tol": 0.006, "seed": 1, "amp": (500.0, 1000.0, 2000.0, 4000.0),
-    "g": 0.83 * 1.35, "s": 0.83 * 2.8, "c": 0.83 * 1.15, "pe": 0.417 * 1.15, "lat": 200.0, "iters": 2500,
+    "kde": 0, "fp": 192, "xs": 4096, "fill": [2560, 0], "vS": [0, 0], "d0S": 0, "llv": 1,
+    "win": 3000.0, "tol": 0.003, "seed": 3, "amp": (500.0, 1000.0, 2000.0, 4000.0),
+    "g": 0.83 * np.array([1.3, 1.9, 1.15]), "s": 0.83 * np.array([2.6, 5.0, 2.0]), "c": 0.83 * np.array([1.05, 1.25, 1.2]),
+    "pe": 0.417 * np.array([1.05, 1.25, 1.2]), "lat": np.array([225.0, 180.0, 300.0]), "iters": 3000, "mix": 0,
 }
 INFO = {}
 LIFT = 1024.0
@@ -48,61 +51,85 @@ def arrange(ops, lat, iters):
     for i in range(N):
         for j in pred[i]:
             succ[j].append(i)
-    cost, tail, eng = [o["cost"] for o in ops], [o["lat"] + lat for o in ops], [o["eng"] for o in ops]
+    eng = ["VSPGYN".index(o["eng"]) for o in ops]
+    M = len(lat)
+    cost = [[float((o["cost"] + 0 * lat)[m]) for o in ops] for m in range(M)]
+    tail = [[float(o["lat"] + lat[m]) for o in ops] for m in range(M)]
+    fw = [[[(j, cost[m][j] + (0.0 if eng[i] == eng[j] == 2 else tail[m][j])) for j in pred[i]] for i in range(N)] for m in range(M)]
+    bw = [[[(j, cost[m][j] + (0.0 if eng[i] == eng[j] == 2 else tail[m][i])) for j in succ[i]] for i in range(N)] for m in range(M)]
 
-    def place(key, back):
-        before, after = (succ, pred) if back else (pred, succ)
-        left = [len(b) for b in before]
-        ready = [(key[i], i) for i in range(N) if left[i] == 0]
-        busy = {e: [] for e in "VSPGYN"}
+    def place(key, back, m):
+        before, cs, tl = (bw if back else fw)[m], cost[m], tail[m]
+        for i in (range(N - 1, -1, -1) if back else range(N)):
+            for j, _ in before[i]:
+                if key[j] >= key[i]:
+                    key[i] = key[j] + 1e-3
+        lo, hi = [[] for _ in range(6)], [[] for _ in range(6)]
         t0 = [0.0] * N
-        while ready:
-            m = min(ready)
-            ready.remove(m)
-            i = m[1]
-            t = tail[i] if back else 0.0
-            for j in before[i]:
-                x = t0[j] + cost[j] + (0.0 if eng[i] == eng[j] == "P" else tail[i] if back else tail[j])
-                if x > t:
-                    t = x
-            b, c = busy[eng[i]], cost[i]
-            k = len(b)
-            while k > 0 and b[k - 1][1] > t:
+        for i in sorted(range(N), key=lambda x: key[x]):
+            t = tl[i] if back else 0.0
+            for j, d in before[i]:
+                if t0[j] + d > t:
+                    t = t0[j] + d
+            a, b, c = lo[eng[i]], hi[eng[i]], cs[i]
+            k = n = len(a)
+            while k > 0 and b[k - 1] > t:
                 k -= 1
-            while k < len(b) and b[k][0] < t + c:
-                t = max(t, b[k][1])
+            while k < n and a[k] < t + c:
+                if b[k] > t:
+                    t = b[k]
                 k += 1
-            b.insert(k, (t, t + c))
+            a.insert(k, t)
+            b.insert(k, t + c)
             t0[i] = t
-            for j in after[i]:
-                left[j] -= 1
-                if left[j] == 0:
-                    ready.append((key[j], j))
-        return t0, max(t0[i] + cost[i] + (0.0 if back else tail[i]) for i in range(N))
+        return t0
+
+    def replay(t0):
+        order = sorted(range(N), key=lambda x: (t0[x], x))
+        ends = []
+        for m in range(M):
+            before, cs, tl = fw[m], cost[m], tail[m]
+            free, s, end = [0.0] * 6, [0.0] * N, 0.0
+            for i in order:
+                t = free[eng[i]]
+                for j, d in before[i]:
+                    if s[j] + d > t:
+                        t = s[j] + d
+                s[i] = t
+                free[eng[i]] = t + cs[i]
+                if t + cs[i] + tl[i] > end:
+                    end = t + cs[i] + tl[i]
+            ends.append(end)
+        return ends
 
     pr = [0.0] * N
     for i in range(N - 1, -1, -1):
-        pr[i] = cost[i] + tail[i] + max([pr[j] for j in succ[i]] + [0.0])
+        pr[i] = cost[0][i] + tail[0][i] + max([pr[j] for j in succ[i]] + [0.0])
     early = [1e6 * o.get("early", 0) for o in ops]
     for i in range(N - 1, -1, -1):
         for j in pred[i]:
             early[j] = max(early[j], early[i])
-    best = place([-pr[i] - early[i] for i in range(N)], False)
-    cur = best
+    early, c0 = np.array(early), np.array(cost)
+    t0 = place([-pr[i] - early[i] for i in range(N)], False, 0)
+    unit = replay(t0)
+    best = cur = (t0, 1.0, unit, 0)
     rng = np.random.default_rng(CFG["seed"])
     for it in range(iters):
         amp = 0.0 if it < 4 else CFG["amp"][it % 4]
         nz = rng.random(N) * amp
-        if it >= iters // 4:
-            a = rng.random() * cur[1]
-            nz = nz * (np.abs(np.array(cur[0]) - a) < CFG["win"])
-        tb, _ = place([-(cur[0][i] + cost[i]) + nz[i] for i in range(N)], True)
-        new = place([-(tb[i] + cost[i]) - early[i] for i in range(N)], False)
+        now = np.array(cur[0])
+        if it >= iters // 8:
+            nz = nz * (np.abs(now - rng.random() * now.max()) < CFG["win"])
+        m = int(rng.integers(M)) if CFG["mix"] else 0
+        tb = place((nz - now - c0[cur[3]]).tolist(), True, m)
+        t0 = place((-np.array(tb) - c0[m] - early).tolist(), False, m)
+        ends = replay(t0)
+        new = (t0, sum(a / b for a, b in zip(ends, unit)) / M, ends, m)
         if new[1] <= cur[1] * (1.0 + CFG["tol"] * (1.0 - it / iters)):
             cur = new
         if new[1] < best[1]:
             best = new
-    return best
+    return best[0], best[2]
 
 
 def rank_program(g, core, T, topo):
@@ -217,8 +244,8 @@ def rank_program(g, core, T, topo):
             fn = lambda: [g.scalar.activation(out["ap"], a["ap"], AF.Identity, bias=bias["ap"])]
         return add("S", fn, [a, bias], [out], cost)
 
-    def put(on_s, off, val):
-        out = IND(STS, off)
+    def put(on_s, off, val, tab="ST"):
+        out = IND(A((tab, 0), 0, 5120), off)
         if not on_s:
             return cp(out, val)
         return add("S", lambda: [g.scalar.activation(out["ap"], val["ap"], AF.Silu)], [val], [out], 70 + C["s"] * out["n"])
@@ -246,14 +273,14 @@ def rank_program(g, core, T, topo):
             fn = lambda: [g.iota(out["ap"], pat, base, cm)]
         else:
             fn = lambda: [g.iota(out["ap"], pat, base, cm, allow_small_or_imprecise_dtypes=True)]
-        return add("G", fn, [], [out], 260 + 2 * C["c"] * out["n"])
+        return add("G", fn, [], [out], 130 + C["lat"] + 2 * C["c"] * out["n"])
 
     def pick(out, a, pat, op, base):
-        return add("G", lambda: [g.affine_select(out["ap"], a["ap"], pat, op, 0.0, base, 1)], [a], [out], 300 + 2 * C["c"] * out["n"])
+        return add("G", lambda: [g.affine_select(out["ap"], a["ap"], pat, op, 0.0, base, 1)], [a], [out], 170 + C["lat"] + 2 * C["c"] * out["n"])
 
     def send(src, land, nbytes):
         sem = "r%d" % nsem["r"]
-        s = add("G", lambda: [g.remote_dma(land["ap"], src["ap"], T.sem[sem], T.sem.sent, pid, rid, mask_out)], [src], [], 400, "x")
+        s = add("G", lambda: [g.remote_dma(land["ap"], src["ap"], T.sem[sem], T.sem.sent, pid, rid, mask_out)], [src], [], 500 + 1500 * (sem == "r0"), "x")
         return add("N", None, [], [land], 0, "r", 2500 + nbytes / 60.0, extra=[s])
 
     F = lambda k: al("LF", k)
@@ -261,8 +288,8 @@ def rank_program(g, core, T, topo):
     U = lambda k: al("LU", k)
     PS = [("PS%d" % i, 0) for i in range(8)]
     PATH, CNT, ZB, MA, MB = PS[0:2], PS[2:4], PS[4:6], PS[6], PS[7]
-    XW, STW, STS, IDW = A(("XW", 0), 0, 4096), A(("ST", 0), 0, 4096), A(("ST", 0), 0, 5120), A(("IDT", 0), 0, 8192)
-    ST, IDT = ("ST", 0), ("IDT", 0)
+    XW, STW, SBW, IDW = A(("XW", 0), 0, 4096), A(("ST", 0), 0, 4096), A(("SB", 0), 0, 4096), A(("IDT", 0), 0, 8192)
+    ST, SB, IDT = ("ST", 0), ("SB", 0), ("IDT", 0)
 
     ns, kd, ro, ne = al("LI", 256), al("LI", 256), al("LI", 32), al("LI", 64)
     soon(30, dma("Y", A(ns, 0, 256)["ap"], T.nsum[:], 131072, outs=[A(ns, 0, 256)]))
@@ -274,7 +301,8 @@ def rank_program(g, core, T, topo):
         soon(28, dma("YS"[par], o["ap"], T.rho[par::2, :], 8192, outs=[o]))
     d0 = B(512)
     soon(27.5, dma("S", A(d0, 0, 512)["ap"], T.dem[:, 0:512], 131072, outs=[A(d0, 0, 512)]))
-    soon(27, dma("S", XW["ap"], T.x[:], 1 << 20, outs=[XW]))
+    xs = C["xs"]
+    soon(27, dma("S", T.XW[:, 0:xs], T.x[:, 0:xs], 256 * xs, outs=[A(("XW", 0), 0, xs)]))
     DW = [None, [B(768), B(768)], [B(768), B(768)]]
 
     pi, J, Jc, cols = al("LI", 48), F(144), F(128), F(16)
@@ -303,10 +331,10 @@ def rank_program(g, core, T, topo):
     for u in range(3):
         act(A(Bm[u], 0, 144), A(Bc, 0, 144), scale=A(mk, u, u + 1))
     ts(A(Id, 0, 144), A(J, 0, 144), 0.0, OP.is_equal)
-    I32, I64, I256, I512, Sh, Sh2, Ip, In, In2 = B(128), B(128), B(128), B(128), B(128), B(128), F(128), F(128), F(128)
+    I32, I64, I256, Sh, Sh2, Ip, In, In2 = B(128), B(128), B(128), B(128), B(128), F(128), F(128), F(128)
     if any(C[k] for k in ("lP", "ld", "lS", "lv")):
         act(A(Ip, 0, 128), A(Id, 15, 143))
-    for b_, v in ((In, -1.0), (In2, -2.0), (I32, -32.0), (I64, -64.0), (I256, -256.0), (I512, -512.0)):
+    for b_, v in ((In, -1.0), (In2, -2.0), (I32, -32.0), (I64, -64.0), (I256, -256.0)):
         act(A(b_, 0, 128), A(Id, 15, 143), scale=v)
     ts(A(Sh, 0, 128), A(J, 15, 143), 16.0, OP.is_equal, -256.0, OP.mult)
     ts(A(Sh2, 0, 128), A(J, 15, 143), -112.0, OP.is_equal, -256.0, OP.mult)
@@ -342,35 +370,58 @@ def rank_program(g, core, T, topo):
     LW, Z0 = [B(768) for _ in range(3)], B(128)
     if C["lS"]:
         ms(A(Z0, 0, 128), 0.0)
-    NN, EZ, EB = B(352), B(320), [F(320), F(320)]
+    NN, EZ, EB = B(352), B(384), [F(320), F(320)]
+    KP = (EZ[0], EZ[1] + 320)
     ms(A(NN, 0, 352), 1.0)
     N = [(NN[0], NN[1] + 176 * par) for par in range(2)]
     for par in range(2):
         ms(five(N[par], 0, 32, 1), 0.0)
         ms(five(EB[par], 0, 32, 0), 0.0)
-    ms(A(EZ, 0, 320), 0.0)
+    ms(A(EZ, 0, 384), 0.0)
     EM, SP = [(EZ[0], EZ[1] + 64 * i) for i in range(2)], [(EZ[0], EZ[1] + 64 * i) for i in range(2, 5)]
     Sel = F(128)
     ms(A(Sel, 0, 128), 1.0)
     pick(A(Sel, 0, 128), A(Sel, 0, 128), [[-2, 8], [-16, 8], [-1, 2]], OP.is_equal, 0)
 
     fa, fb = C["fill"]
-    for a in range(0, fa, 512):
-        soon(15, ms(A(ST, a, a + 512), 0.0))
+    for a in [0] + list(range(512, fa, C["fp"])):
+        soon(15, ms(A(ST, a, min(fa, a + C["fp"]) if a else 512), 0.0))
     if fb:
         soon(15, iota(A(ST, fa, fa + fb), [[0, fb]], 0, 0))
     for a in range(fa + fb, 4096, 512):
-        soon(15, act(A(ST, a, a + 512), A(ST, 0, 512)))
+        o, i_ = A(ST, a, a + 512), A(ST, 0, 512)
+        soon(19 + 6 * (a == fa + fb), add("S", lambda o=o, i_=i_: [g.scalar.activation(o["ap"], i_["ap"], AF.Silu)], [i_], [o], 40 + C["c"] * 512 + 1500 * (a == fa + fb)))
     hi_, lo_, wh_ = A(F(256), 0, 256), A(F(256), 0, 256), A(F(256), 0, 256)
     ts(hi_, A(ns, 0, 256), 1610612736.0, OP.add, 1610612736.0, OP.subtract)
     tt(lo_, hi_, A(ns, 0, 256), OP.subtract)
     ts(wh_, A(ns, 0, 256), LIFT, OP.add)
     for r_, src in ((0, hi_), (2, lo_), (1, wh_)):
         soon(14, dma("Y", T.ST[r_:128:16, 0:4096], src["ap"], 131072, ins=[src, A(ST, 16, 4096)], outs=[A(ST, 4 * r_, 4 * r_ + 4)]))
-    soon(13, dma("Y", A(kd, 0, 256)["ap"], T.kid[:], 131072, ins=[wh_], outs=[A(kd, 0, 256)]))
+
+    def behind():
+        for r_, src in ((0, hi_), (2, lo_)):
+            dma("Y", T.SB[r_:128:16, 0:4096], src["ap"], 131072, ins=[src, A(SB, 16, 4096)], outs=[A(SB, 4 * r_, 4 * r_ + 4)])
+
+    if C["sb"] == 1:
+        for a in range(0, 4096, 1024):
+            iota(A(SB, a, a + 1024), [[0, 1024]], 4096 + int(LIFT), 0)
+        behind()
+    elif C["sb"]:
+        for a in range(0, 4096 * (C["sb"] == 2), 1024):
+            soon(C["sbe"], dma("Y", A(SB, a, a + 1024)["ap"], A(ST, a, a + 1024)["ap"], 1 << 20, ins=[STW], outs=[A(SB, a, a + 1024)]))
+        flat = A(F(256), 0, 256)
+        iota(flat, [[0, 256]], 4096 + int(LIFT), 0)
+        dma("Y", T.SB[1:128:16, 0:4096], flat["ap"], 131072, ins=[flat], outs=[SBW])
+    late = [hi_, lo_, wh_, A(ST, 16, 4096)]
+    if xs < 4096:
+        soon(13.5, dma("Y", T.XW[:, xs:4096], T.x[:, xs:4096], 256 * (4096 - xs) + 300000, ins=late, outs=[A(("XW", 0), xs, 4096)]))
+    if C["kde"]:
+        soon(27.2, dma("Y", A(kd, 0, 256)["ap"], T.kid[:], 200000, outs=[A(kd, 0, 256)]))
+    else:
+        soon(13.7, dma("Y", A(kd, 0, 256)["ap"], T.kid[:], 400000, ins=late, outs=[A(kd, 0, 256)]))
     for t in (1, 2):
         dr = B(512)
-        dma("Y", A(dr, 0, 512)["ap"], T.dem[:, 512 * t:512 * t + 512], 131072, ins=[A(kd, 0, 256)], outs=[A(dr, 0, 512)])
+        dma("Y", A(dr, 0, 512)["ap"], T.dem[:, 512 * t:512 * t + 512], 131072, ins=[STW], outs=[A(dr, 0, 512)])
         for par in range(2):
             for hh in range(2):
                 pick(two(DW[t][par], 0, 128, hh), two(dr, 128 * hh, 128 * hh + 128, par), [[0, 128]], OP.is_ge, 0)
@@ -389,23 +440,25 @@ def rank_program(g, core, T, topo):
         soon(4 * (k <= C["ide"]))
     hc, lc, q256 = F(256), F(256), F(1)
     for k in range(4):
-        iota(A(IDT, 4096 + 1024 * k, 5120 + 1024 * k), [[1, 1024]], 4096 + 1024 * k + int(LIFT), 0)
+        soon(C["ige"], iota(A(IDT, 4096 + 1024 * k, 5120 + 1024 * k), [[1, 1024]], 4096 + 1024 * k + int(LIFT), 0))
     iota(A(hc, 0, 256), [[128, 2], [0, 128]], 4096 + 256, 0)
     iota(A(lc, 0, 256), [[0, 2], [-1, 128]], 256, 0)
     ts(A(q256, 0, 1), q, 256.0, OP.mult)
-    add("S", lambda: [g.scalar.activation(A(hc, 0, 256)["ap"], A(hc, 0, 256)["ap"], AF.Silu, bias=A(q256, 0, 1)["ap"])],
-        [A(hc, 0, 256), A(q256, 0, 1)], [A(hc, 0, 256)], 1700)
+    act(A(hc, 0, 256), A(hc, 0, 256), A(q256, 0, 1))
     dma("Y", T.IDT[0:128:16, 4096:8192], A(hc, 0, 256)["ap"], 131072, ins=[A(hc, 0, 256), A(IDT, 4104, 8192)], outs=[A(IDT, 4096, 4100)])
     dma("Y", T.IDT[2:128:16, 4096:8192], A(lc, 0, 256)["ap"], 131072, ins=[A(lc, 0, 256), A(IDT, 4104, 8192)], outs=[A(IDT, 4100, 4104)])
     rn, rnu, k2 = al("LI", 32), U(32), A(al("LI", 256), 0, 256)
-    dma("Y", A(rn, 0, 32)["ap"], T.rho[:], 16384, ins=[wh_], outs=[A(rn, 0, 32)])
+    soon(12, dma("Y", A(rn, 0, 32)["ap"], T.rho[:], 400000, ins=late, outs=[A(rn, 0, 32)]))
     cp(A(rnu, 0, 32), A(rn, 0, 32))
-    act(A(LW[0], 0, 512), IND(A(IDT, 0, 4096), A(rnu, 0, 32)))
-    for t in (1, 2):
-        dma("Y", A(LW[t], 0, 512)["ap"], A(LW[0], 0, 512)["ap"], 131072, ins=[A(LW[0], 0, 512)], outs=[A(LW[t], 0, 512)])
     ts(k2, A(kd, 0, 256), 1023, OP.bitwise_and)
-    ts(A(kf, 0, 256), k2, -255.0, OP.add)
-    dma("Y", T.IDT[3:128:16, 0:4096], A(kf, 0, 256)["ap"], 131072, ins=[A(kf, 0, 256)], outs=[A(IDT, 0, 4096)])
+    soon(C["kde"], ts(A(kf, 0, 256), k2, -255.0, OP.add))
+    for i in range(2):
+        if i == C["kl"]:
+            soon(C["kfe"], dma("Y", T.IDT[3:128:16, 0:4096], A(kf, 0, 256)["ap"], 131072, ins=[A(kf, 0, 256)], outs=[A(IDT, 0, 4096)]))
+        else:
+            act(A(LW[0], 0, 512), IND(A(IDT, 0, 4096), A(rnu, 0, 32)))
+            for t in (1, 2):
+                dma("Y", A(LW[t], 0, 512)["ap"], A(LW[0], 0, 512)["ap"], 131072, ins=[A(LW[0], 0, 512)], outs=[A(LW[t], 0, 512)])
 
     R, ru = [F(32), F(32)], U(32)
     for par in range(2):
@@ -417,7 +470,7 @@ def rank_program(g, core, T, topo):
     for par in range(2):
         cp(A(O[0][par], 0, 32), A(ne, 32 * par, 32 * par + 32))
         cp(five(EB[par], 0, 32), A(ne, 32 * par, 32 * par + 32))
-    dead = [None, None]
+    dead, FR = [None, None], [None, None]
     z = [[B(512), B(512)] for _ in range(3)]
     sg = [[B(512), B(512)], [B(512), B(512)]]
     xg = [[B(512), B(512)], [B(512), B(512)]]
@@ -434,7 +487,7 @@ def rank_program(g, core, T, topo):
     def step(t, par, k):
         e, o, s, ps = EB[par], O[t][par], sg[par][k % 2], A(PATH[par], 0, 32)
         v = [A(R[par], 0, 32), five(e, 0, 32), five(e, 32, 64), A(V3[par], 0, 32)]
-        act(A(s, 0, 512), IND(STW, A(o, 32 * k - 32, 32 * k)))
+        act(A(s, 0, 512), IND(SBW if t and par == t % 2 and k - 2 >= C["sk"][t - 1] else STW, A(o, 32 * k - 32, 32 * k)))
         less = [(In, v[k - 1])] if k < 4 else [(In2, v[3]), (In, five(e, 0, 32, 1))]
         mm([(ps, full(m_), x, i == 0, False) for i, (m_, x) in enumerate(less)])
         mm(w2l(PATH[par], 0, s, 0, 512, Bm[0], start=False))
@@ -502,18 +555,21 @@ def rank_program(g, core, T, topo):
             mm(w2l(cn, 64, cm[par], 1024, 512, Bc, more=more))
         for k in range(0 if C["c3"][0 if isp else 1] else 2, 3):
             ts(five(nn, 0, 32, 4 - k), A(cn, 32 * k, 32 * k + 32), 8.5, OP.is_lt)
+        if C["b4"]:
+            cn = ZB[par] if not any(C["pre"][t][0 if isp else 4:][:4]) else MA if t == 2 and C["df"] else cn
         more = [(A(cn, 96, 112), full(I32), A(fl, 16 * i, 16 * i + 16), False, False) for i in range(2)]
         if dead[par] is not None:
-            more.append((A(cn, 96, 112), full(I512), dead[par], False, False))
+            more.append((A(cn, 96, 112), full(I256), dead[par], False, False))
         mm(w2l(cn, 96, cm[par], 1536, 512, Bc, stop=False, more=more))
         scan(A(OS, 0, 160), A(nn, 0, 160), A(e, 0, 160))
         tt(A(fl, 32, 48), five(OS, 0, 16), five(OS, 16, 32), OP.is_equal)
-        tt(two(ed, 0, 32, 0), five(OS, 0, 32), A(dump, 0, 32), OP.subtract)
+        if isp or C["sw"][t] != 1:
+            tt(two(ed, 0, 32, 0), five(OS, 0, 32), A(dump, 0, 32), OP.subtract)
         if C["late4"][0 if isp else 1]:
             cp(five(e, 0, 32, 0), A(PATH[par], 0, 32))
         scan(A(OS, 160, 320), A(nn, 1, 161), A(e, 0, 160))
         mm([(A(cn, 96, 128), full(I64), five(nn, 0, 32, 2 + i), False, False) for i in range(3)]
-           + [(A(cn, 96, 112), full(I512), A(fl, 32, 48), False, True)])
+           + [(A(cn, 96, 112), full(I256), A(fl, 32, 48), False, True)])
         ts(A(hit, 0, 32), A(cn, 96, 128), -183.5, OP.is_gt)
         if t < 2:
             flags(t, par, hit)
@@ -524,6 +580,8 @@ def rank_program(g, core, T, topo):
     def move(t, par, OS):
         k = 64 if t < 2 and par != t % 2 else 32
         e, D = EB[par], F(64)
+        if t == 2 and C["rf"][par]:
+            rootsum(par, OS)
         tt(A(D, 0, k), five(OS, 0, k), five(e, 0, k), OP.subtract)
         for a in range(0, k, 32):
             tt(A(D, a, a + 32), A(D, a, a + 32), two(EM[par], 0, 32, 1), OP.mult)
@@ -541,10 +599,22 @@ def rank_program(g, core, T, topo):
         ts(A(uo, 0, 16), o, q, OP.add, 512.0, OP.add)
         send(A(uo, 0, 16), A(zoff[t + 1][par], 0, 16), 4096)
 
+    def rootsum(par, OS):
+        fr = F(32)
+        tt(two(fr, 0, 16, 1), five(EB[par], 0, 16), five(EB[par], 16, 32), OP.add)
+        tt(two(fr, 0, 16, 0), five(OS, 0, 16), five(OS, 16, 32), OP.add)
+        tt(two(fr, 0, 16, 0), two(fr, 0, 16, 0), two(fr, 0, 16, 1), OP.subtract)
+        FR[par] = fr
+
     def roots(par, on_s):
         vu, w = U(16), F(256)
-        cp(A(vu, 0, 16), A(comb(C["lP"], CNT[par], 192, 16, [(1, five(EB[par], 0, 16)), (1, five(EB[par], 16, 32))]), 0, 16))
-        act(A(w, 0, 256), IND(IDW, A(vu, 0, 16)))
+        if C["rf"][par]:
+            r = F(32)
+            scan(A(r, 0, 32), A(EM[par], 0, 32), A(FR[par], 0, 32))
+            cp(A(vu, 0, 16), two(r, 0, 16, 1))
+        else:
+            cp(A(vu, 0, 16), A(comb(C["lP"], CNT[par], 192, 16, [(1, five(EB[par], 0, 16)), (1, five(EB[par], 16, 32))]), 0, 16))
+        (cp if C["rv"][par] else act)(A(w, 0, 256), IND(IDW, A(vu, 0, 16)))
         put(on_s, A(ru, 16 * par, 16 * par + 16), A(w, 0, 256))
 
     top16 = slice(0, 16)
@@ -587,7 +657,6 @@ def rank_program(g, core, T, topo):
                 lst.append((A(MB, 16 * u, 16 * u + 16), L(Bm[u], i), A(LW[t], a, a + 241, 16), i == 0, i == 15))
         mm(lst)
         LL, lu, sv = F(32), U(32), B(512)
-        cp(A(lu, 0, 32), A(MB, 0, 32))
         (cp if C["llv"] else act)(A(LL, 0, 32), A(MB, 0, 32))
         pw = F(512)
         act(A(pw, 0, 512), IND(IDW, A(vu, 0, 32)))
@@ -596,7 +665,10 @@ def rank_program(g, core, T, topo):
         put(C["silu"][t][0], A(pu, 0, 32), A(pw, 0, 512))
         for k in range(pp + 1, ps + 1):
             step(t, K, k)
-        act(A(sv, 0, 512), IND(STW, A(lu, 0, 32)))
+        diff = last and C["df"]
+        if not diff:
+            cp(A(lu, 0, 32), A(MB, 0, 32))
+            act(A(sv, 0, 512), IND(STW, A(lu, 0, 32)))
         for k in range(ps + 1, 5):
             step(t, K, k)
         svm = w2l(MA, 0, sv, 0, 512, Bm[0], start=not C["lS"])
@@ -611,32 +683,77 @@ def rank_program(g, core, T, topo):
         kp, tk, nf, vu, of, ou = F(16), F(32), F(16), U(64), F(128), U(64)
         w0, w1, pv, pb, X = five(OS, 0, 16), five(OS, 16, 32), A(LL, 0, 16), A(LL, 16, 32), five(OS, 32, 64)
         tw, tv, cn = A(tk, 0, 16), A(tk, 16, 32), CNT[K]
-        dd = comb(C["ld"], ZB[P], 160, 32, [], [(0, 16, [(1, w0), (-1, w1)]), (16, 32, [(1, pv), (-1, pb)])])
+        sw, x0, x1 = C["sw"][t], five(OS, 32, 48), five(OS, 48, 64)
+        if sw < 2:
+            dd = comb(C["ld"], ZB[P], 160, 32, [], [(0, 16, [(1, w0), (-1, w1)]), (16, 32, [(1, x0), (-1, x1)] if sw else [(1, pv), (-1, pb)])])
         tt(A(nf, 0, 16), pv, pb, OP.is_equal)
-        if C["lS"]:
+        if sw == 2:
+            pr, res = F(128), F(128)
+            for i, (a, b_, u, v, op) in enumerate(((pv, pb, x0, pb, OP.add), (pb, pv, x1, pv, OP.add), (w0, w1, w1, pb, OP.subtract), (w1, w0, w0, pv, OP.subtract))):
+                tt(two(pr, 16 * i, 16 * i + 16, 0), a, b_, OP.subtract)
+                tt(two(pr, 16 * i, 16 * i + 16, 1), u, v, op)
+            mm(w2l(ZB[P], 128, kc, 0, 256, Bc))
+            for s in range(2):
+                ts(two(KP, 16 * s, 16 * s + 16, 1), A(ZB[P], 128, 144), 8.5, OP.is_gt)
+            scan(A(res, 0, 64), A(KP, 0, 64), A(pr, 0, 64))
+            ts(A(vu, 0, 32), two(res, 0, 32, 1), 8191.0, OP.min)
+            if not diff:
+                mm(svm)
+                if C["cx"][t]:
+                    tt(two(pr, 32, 64, 1), two(pr, 32, 64, 1), A(MA, 0, 32), OP.add)
+            scan(A(res, 64, 128), A(KP, 0, 64), A(pr, 64, 128))
+            if not diff and not C["cx"][t]:
+                tt(two(res, 32, 64, 1), two(res, 32, 64, 1), A(MA, 0, 32), OP.add)
+            ts(A(vu, 32, 64), two(res, 32, 64, 1), 4096.0 * diff, OP.add, 8191.0, OP.min)
+        elif sw:
+            mm(w2l(ZB[P], 128, kc, 0, 256, Bc))
+            ts(A(kp, 0, 16), A(ZB[P], 128, 144), 8.5, OP.is_gt)
+            for s in range(2):
+                tt(A(tk, 16 * s, 16 * s + 16), A(dd, 16 * s, 16 * s + 16), A(kp, 0, 16), OP.mult)
+            cw = comb(0, None, 0, 32, [], [(0, 16, [(1, w1), (1, tw)]), (16, 32, [(1, w0), (-1, tw)])])
+            tt(two(FDK, 0, 32, 0), A(cw, 0, 32), A(dump, 0, 32), OP.subtract)
+            vl = comb(0, None, 0, 32, [(1, A(LL, 0, 32))], [(0, 16, [(1, x1), (1, tv)]), (16, 32, [(1, x0), (-1, tv)])])
+            if C["lS"] and not diff:
+                mm([(A(MA, 0, 32), full(Z0), A(Z0, 0, 32), True, False)] + lin([(A(MA, 0, 16), -1, pb), (A(MA, 16, 32), -1, pv), None], False))
+                mm(svm)
+                cd = comb(0, None, 0, 32, [(1, A(cw, 0, 32)), (1, A(MA, 0, 32))])
+            else:
+                if not diff:
+                    mm(svm)
+                cd = comb(0, None, 0, 32, [] if diff else [(1, A(MA, 0, 32))], [(0, 16, [(1, A(cw, 0, 16)), (-1, pb)]), (16, 32, [(1, A(cw, 16, 32)), (-1, pv)])])
+        elif diff:
+            cd = comb(0, None, 0, 32, [], [(0, 16, [(1, w1), (-1, pb)]), (16, 32, [(1, w0), (-1, pv)])])
+        elif C["lS"]:
             mm([(A(MA, 0, 32), full(Z0), A(Z0, 0, 32), True, False)]
                + lin([(A(MA, 0, 16), 1, w1), (A(MA, 0, 16), -1, pb), (A(MA, 16, 32), 1, w0), (A(MA, 16, 32), -1, pv), None], False))
         else:
             mm(svm)
             cd = comb(0, None, 0, 32, [], [(0, 16, [(1, w1), (-1, pb)]), (16, 32, [(1, w0), (-1, pv)])])
-        mm(w2l(ZB[P], 128, kc, 0, 256, Bc))
-        ts(A(kp, 0, 16), A(ZB[P], 128, 144), 8.5, OP.is_gt)
-        for s in range(2):
-            tt(A(tk, 16 * s, 16 * s + 16), A(dd, 16 * s, 16 * s + 16), A(kp, 0, 16), OP.mult)
-        if C["lS"]:
+        if not sw:
+            mm(w2l(ZB[P], 128, kc, 0, 256, Bc))
+            ts(A(kp, 0, 16), A(ZB[P], 128, 144), 8.5, OP.is_gt)
+            for s in range(2):
+                tt(A(tk, 16 * s, 16 * s + 16), A(dd, 16 * s, 16 * s + 16), A(kp, 0, 16), OP.mult)
+        if sw:
+            pass
+        elif C["lS"] and not diff:
             mm(lin([(A(MA, 0, 16), 1, tw), (A(MA, 16, 32), -1, tw), None], False))
             mm(svm)
             cd = MA
         else:
-            cd = comb(0, None, 0, 32, [(1, A(MA, 0, 32))], [(0, 16, [(1, A(cd, 0, 16)), (1, tw)]), (16, 32, [(1, A(cd, 16, 32)), (-1, tw)])])
-        ts(A(vu, 32, 64), A(cd, 0, 32), 8191.0, OP.min)
-        if C["lv"]:
+            cd = comb(0, None, 0, 32, [] if diff else [(1, A(MA, 0, 32))], [(0, 16, [(1, A(cd, 0, 16)), (1, tw)]), (16, 32, [(1, A(cd, 16, 32)), (-1, tw)])])
+        if sw < 2:
+            ts(A(vu, 32, 64), A(cd, 0, 32), 4096.0 * diff, OP.add, 8191.0, OP.min)
+        if sw:
+            pass
+        elif C["lv"]:
             vl = comb(1, cn, 160, 32, [(1, X)], [(0, 16, [(1, pb), (1, tv)]), (16, 32, [(1, pv), (-1, tv)])])
         elif C["xl"][t]:
             vl = comb(0, None, 0, 32, [(1, X)], [(0, 16, [(1, pb), (1, tv)]), (16, 32, [(1, pv), (-1, tv)])])
         else:
             vl = comb(0, None, 0, 32, [], [(0, 16, [(1, pb), (1, five(OS, 32, 48)), (1, tv)]), (16, 32, [(1, pv), (1, five(OS, 48, 64)), (-1, tv)])])
-        ts(A(vu, 0, 32), A(vl, 0, 32), 8191.0, OP.min)
+        if sw < 2:
+            ts(A(vu, 0, 32), A(vl, 0, 32), 8191.0, OP.min)
         tt(two(FD2, 0, 32, 0), A(LL, 0, 32), A(dump, 32, 64), OP.subtract)
         for s in range(2):
             tt(two(SP[t], 16 * s, 16 * s + 16, 1), two(EM[K], 0, 16, 1), A(nf, 0, 16), OP.is_gt)
@@ -646,14 +763,14 @@ def rank_program(g, core, T, topo):
             cp(A(ou, 32 * i, 32 * i + 32), two(of, 32 * i, 32 * i + 32, 1))
         move(t, K, OS)
         kw = F(1024)
-        act(A(kw, 512, 1024), IND(IDW, A(vu, 32, 64)))
-        act(A(kw, 0, 512), IND(IDW, A(vu, 0, 32)))
+        (cp if C["kv"][t][0] else act)(A(kw, 512, 1024), IND(IDW, A(vu, 32, 64)))
+        (cp if C["kv"][t][1] else act)(A(kw, 0, 512), IND(IDW, A(vu, 0, 32)))
         nd = two(SP[t], 0, 16, 1)
         if dead[K] is not None:
             nd, old = A(B(16), 0, 16), nd
             tt(nd, dead[K], old, OP.max)
         dead[K] = nd
-        both = [(A(ou, 32, 64), A(kw, 512, 1024)), (A(ou, 0, 32), A(kw, 0, 512))]
+        both = [(A(ou, 32, 64), A(kw, 512, 1024), "SB" if diff else "ST"), (A(ou, 0, 32), A(kw, 0, 512))]
         cut = (0,) + tuple(C["nb"][t]) + (1 if last else 3,)
         for i in range(3):
             for k in range(cut[i], cut[i + 1]):
@@ -663,6 +780,10 @@ def rank_program(g, core, T, topo):
                     step(t + 1, K, k + 2)
             if i < 2:
                 put(C["silu"][t][1 + i], *both[i ^ C["nf"][t]])
+        if t == 0 and C["sk"][1] < 3:
+            for r_, dst in ((0, hi_), (2, lo_)):
+                dma("Y", dst["ap"], T.ST[r_:128:16, 0:4096], 131072, ins=[STW], outs=[dst])
+            behind()
         if not last:
             demand(t + 1, P)
             demand(t + 1, K)
@@ -675,7 +796,14 @@ def rank_program(g, core, T, topo):
             dma("S", T.yl[:], A(YO, 512, 768, p=top16)["ap"], 16384, ins=[A(YO, 512, 768)])
             yc = A(F(256), 0, 256)
             dma("Y", yc["ap"], A(ST, 0, 4096, p=slice(1, 128, 16))["ap"], 131072, ins=[STW], outs=[yc])
-            ts(yc, yc, 12582912.0 - LIFT, OP.add, 12582912.0, OP.subtract)
+            if diff:
+                yd = A(F(256), 0, 256)
+                dma("Y", yd["ap"], A(SB, 0, 4096, p=slice(1, 128, 16))["ap"], 131072, ins=[SBW], outs=[yd])
+                if C["yp"]:
+                    cp(A(MB, 0, 256), yd)
+                    yd = A(MB, 0, 256)
+                tt(yc, yc, yd, OP.add)
+            ts(yc, yc, 12582912.0 - LIFT - diff * (4096 + LIFT), OP.add, 12582912.0, OP.subtract)
             dma("Y", T.ys[:], yc["ap"], 131072, ins=[yc])
 
     if "t0" not in INFO:

import numpy as np
from concourse.mybir import AluOpType as OP, ActivationFunctionType as AF

NLF, NLB, NLU, NLI = 16384, 27136, 2048, 1024
SCRATCH = {
    "XW": ("sbuf", [128, 4096], "bfloat16"),
    "ST": ("sbuf", [128, 5120], "float32"),
    "SB": ("sbuf", [128, 5120], "float32"),
    "IDT": ("sbuf", [128, 8192], "float32"),
    "LF": ("sbuf", [128, NLF], "float32"),
    "LB": ("sbuf", [128, NLB], "bfloat16"),
    "LU": ("sbuf", [128, NLU], "uint16"),
    "LI": ("sbuf", [128, NLI], "int32"),
}
for _b in range(8):
    SCRATCH["PS%d" % _b] = ("psum", [128, 512], "float32")
NDMA = 48
SEMAPHORES = ["sV", "sS", "sP", "sG", "sent"] + ["d%d" % i for i in range(NDMA)] + ["r%d" % i for i in range(8)]

CFG = {
    "pre": [[0, 0, 0, 0, 0, 0, 0, 0], [0, 0, 0, 0, 0, 0, 0, 0], [0, 0, 0, 0, 0, 0, 1, 1]],
    "cx": [0, 0, 0], "kv": [[0, 0], [0, 1], [1, 0]], "rf": [1, 1], "rv": [0, 0], "yp": 1, "kl": 1, "kfe": 0, "ige": 0, "sb": 3, "sbe": 1, "sk": [3, 3], "df": 1,
    "nb": [[1, 1], [1, 1], [0, 0]], "pp": [[4, 4], [4, 4], [4, 4]],
    "idv": 0, "ide": 2,
    "lP": 0, "ld": 0, "lS": 0, "lv": 0, "c3": [0, 0],
    "silu": [[1, 0, 1], [1, 0, 1], [1, 1, 0], [1, 1]],
    "nf": [1, 1, 1], "xl": [1, 1, 1], "ws": [1, 1, 1], "sw": [2, 2, 2], "b4": 1,
    "zd": [[0, 0], [0, 0], [0, 0]],
    "late4": [1, 1],
    "kde": 0, "fp": 192, "xs": 4096, "fill": [2560, 0], "vS": [0, 0], "d0S": 0, "llv": 1,
    "win": 3000.0, "tol": 0.003, "seed": 3, "amp": (500.0, 1000.0, 2000.0, 4000.0),
    "g": 0.83 * np.array([1.3, 1.9, 1.15]), "s": 0.83 * np.array([2.6, 5.0, 2.0]), "c": 0.83 * np.array([1.05, 1.25, 1.2]),
    "pe": 0.417 * np.array([1.05, 1.25, 1.2]), "lat": np.array([225.0, 180.0, 300.0]), "iters": 3000, "mix": 0,
}
INFO = {}
LIFT = 1024.0


def arrange(ops, lat, iters):
    N = len(ops)
    pred, anc = [], []
    for o in ops:
        keep, seen = [], 0
        for j in sorted(o["deps"], reverse=True):
            if not seen >> j & 1:
                keep.append(j)
                seen |= anc[j] | 1 << j
        pred.append(keep)
        anc.append(seen)
    succ = [[] for _ in range(N)]
    for i in range(N):
        for j in pred[i]:
            succ[j].append(i)
    eng = ["VSPGYN".index(o["eng"]) for o in ops]
    M = len(lat)
    cost = [[float((o["cost"] + 0 * lat)[m]) for o in ops] for m in range(M)]
    tail = [[float(o["lat"] + lat[m]) for o in ops] for m in range(M)]
    fw = [[[(j, cost[m][j] + (0.0 if eng[i] == eng[j] == 2 else tail[m][j])) for j in pred[i]] for i in range(N)] for m in range(M)]
    bw = [[[(j, cost[m][j] + (0.0 if eng[i] == eng[j] == 2 else tail[m][i])) for j in succ[i]] for i in range(N)] for m in range(M)]

    def place(key, back, m):
        before, cs, tl = (bw if back else fw)[m], cost[m], tail[m]
        for i in (range(N - 1, -1, -1) if back else range(N)):
            for j, _ in before[i]:
                if key[j] >= key[i]:
                    key[i] = key[j] + 1e-3
        lo, hi = [[] for _ in range(6)], [[] for _ in range(6)]
        t0 = [0.0] * N
        for i in sorted(range(N), key=lambda x: key[x]):
            t = tl[i] if back else 0.0
            for j, d in before[i]:
                if t0[j] + d > t:
                    t = t0[j] + d
            a, b, c = lo[eng[i]], hi[eng[i]], cs[i]
            k = n = len(a)
            while k > 0 and b[k - 1] > t:
                k -= 1
            while k < n and a[k] < t + c:
                if b[k] > t:
                    t = b[k]
                k += 1
            a.insert(k, t)
            b.insert(k, t + c)
            t0[i] = t
        return t0

    def replay(t0):
        order = sorted(range(N), key=lambda x: (t0[x], x))
        ends = []
        for m in range(M):
            before, cs, tl = fw[m], cost[m], tail[m]
            free, s, end = [0.0] * 6, [0.0] * N, 0.0
            for i in order:
                t = free[eng[i]]
                for j, d in before[i]:
                    if s[j] + d > t:
                        t = s[j] + d
                s[i] = t
                free[eng[i]] = t + cs[i]
                if t + cs[i] + tl[i] > end:
                    end = t + cs[i] + tl[i]
            ends.append(end)
        return ends

    pr = [0.0] * N
    for i in range(N - 1, -1, -1):
        pr[i] = cost[0][i] + tail[0][i] + max([pr[j] for j in succ[i]] + [0.0])
    early = [1e6 * o.get("early", 0) for o in ops]
    for i in range(N - 1, -1, -1):
        for j in pred[i]:
            early[j] = max(early[j], early[i])
    early, c0 = np.array(early), np.array(cost)
    t0 = place([-pr[i] - early[i] for i in range(N)], False, 0)
    unit = replay(t0)
    best = cur = (t0, 1.0, unit, 0)
    rng = np.random.default_rng(CFG["seed"])
    for it in range(iters):
        amp = 0.0 if it < 4 else CFG["amp"][it % 4]
        nz = rng.random(N) * amp
        now = np.array(cur[0])
        if it >= iters // 8:
            nz = nz * (np.abs(now - rng.random() * now.max()) < CFG["win"])
        m = int(rng.integers(M)) if CFG["mix"] else 0
        tb = place((nz - now - c0[cur[3]]).tolist(), True, m)
        t0 = place((-np.array(tb) - c0[m] - early).tolist(), False, m)
        ends = replay(t0)
        new = (t0, sum(a / b for a, b in zip(ends, unit)) / M, ends, m)
        if new[1] <= cur[1] * (1.0 + CFG["tol"] * (1.0 - it / iters)):
            cur = new
        if new[1] < best[1]:
            best = new
    return best[0], best[2]


def rank_program(g, core, T, topo):
    rank = T.rank_of(core)
    if rank is None:
        return
    n = len(T.cores)
    nxt, prv = T.cores[(rank + 1) % n], T.cores[(rank - 1) % n]
    rid, pid = topo.addr(nxt, core)
    mask_out = topo.mask(core, nxt)
    n_out, n_in = len(topo.engines(core, nxt)), len(topo.engines(prv, core))
    C = CFG
    ops, acc, top = [], {}, {"LF": 0, "LB": 0, "LU": 0, "LI": 0}
    nsem = {"d": 0, "r": 0}

    def al(buf, k):
        a = top[buf]
        top[buf] = a + (k + 15) // 16 * 16
        assert top[buf] <= T[buf].shape[1], buf
        return (buf, a)

    def A(b, lo, hi, step=1, p=None):
        buf, a = b
        ps = p if p is not None else slice(0, 128)
        ap = T[buf][ps, a + lo:a + hi] if step == 1 else T[buf][ps, a + lo:a + hi:step]
        return {"ap": ap, "rg": [(buf, ((1 << (hi - lo + step - 1) // step * step) - 1) // ((1 << step) - 1) << a + lo)], "n": len(range(lo, hi, step)), "buf": buf, "ind": False}

    def five(b, i0, i1, pos=4):
        return A(b, 5 * i0 + pos, 5 * (i1 - 1) + pos + 1, 5)

    def two(b, i0, i1, pos):
        return A(b, 2 * i0 + pos, 2 * (i1 - 1) + pos + 1, 2)

    def IND(win, off):
        return {"ap": win["ap"].indirect(off["ap"]), "rg": win["rg"], "off": off["rg"], "n": 16 * off["n"], "buf": win["buf"], "ind": True}

    def add(eng, fn, ins, outs, cost, kind="c", lat=0.0, extra=()):
        rd, wr = [], []
        for a in ins:
            if isinstance(a, dict):
                rd += a["rg"] + a.get("off", [])
        for a in outs:
            wr += a["rg"]
            rd += a.get("off", [])
        me = len(ops)
        deps = set(extra)
        for lst, w in ((rd, False), (wr, True)):
            for buf, bits in lst:
                psum = buf.startswith("PS")
                for (b2, o2, w2) in acc.get(buf, []):
                    e2 = ops[o2]["eng"]
                    if psum and (e2 != eng or eng == "P"):
                        deps.add(o2)
                    elif (w or w2) and bits & b2:
                        deps.add(o2)
        for lst, w in ((rd, False), (wr, True)):
            for buf, bits in lst:
                acc.setdefault(buf, []).append((bits, me, w))
        o = {"eng": eng, "fn": fn, "deps": deps, "cost": cost, "kind": kind, "lat": lat}
        if kind in ("d", "r"):
            o["sem"] = "%s%d" % (kind, nsem[kind])
            nsem[kind] += 1
        ops.append(o)
        return me

    def soon(k, i=-1):
        ops[i]["early"] = k

    def vcost(out, ins, two_):
        for a in ins:
            if isinstance(a, dict) and a["ind"]:
                return 55 + C["g"] * a["n"]
        if out["ind"]:
            return 55 + C["s"] * out["n"]
        full_ = [a for a in ins if isinstance(a, dict)]
        f = 1.0
        if two_:
            f = 1.0 if any(a["buf"].startswith("PS") for a in full_) else 2.0
        elif all(a["buf"] in ("LB", "LU", "XW") for a in full_ + [out]):
            f = 0.5
        return 5 + C["c"] * max(64, f * out["n"])

    def sc(x):
        return x["ap"] if isinstance(x, dict) else x

    def tt(out, a, b, op):
        return add("V", lambda: [g.vector.tensor_tensor(out["ap"], a["ap"], b["ap"], op)], [a, b], [out], vcost(out, [a, b], True))

    def ts(out, a, s1, op0, s2=None, op1=None):
        if op1 is None:
            fn = lambda: [g.vector.tensor_scalar(out["ap"], a["ap"], sc(s1), None, op0)]
        else:
            fn = lambda: [g.vector.tensor_scalar(out["ap"], a["ap"], sc(s1), sc(s2), op0, op1)]
        return add("V", fn, [a, s1, s2], [out], vcost(out, [a], False))

    def scan(out, a, b):
        return add("V", lambda: [g.vector.tensor_tensor_scan(out["ap"], a["ap"], b["ap"], 0.0, OP.mult, OP.add)], [a, b], [out], vcost(out, [a, b], False))

    def cp(out, a):
        return add("V", lambda: [g.vector.tensor_copy(out["ap"], a["ap"])], [a], [out], vcost(out, [a], False))

    def ms(out, v):
        return add("V", lambda: [g.vector.memset(out["ap"], v)], [], [out], vcost(out, [], False))

    def act(out, a, bias=None, scale=None):
        cost = 70 + C["g"] * a["n"] if a["ind"] else 40 + C["c"] * max(64, a["n"])
        if scale is not None:
            return add("S", lambda: [g.scalar.activation(out["ap"], a["ap"], AF.Identity, scale=sc(scale))], [a, scale], [out], cost)
        if bias is None:
            fn = lambda: [g.scalar.activation(out["ap"], a["ap"], AF.Copy)]
        else:
            fn = lambda: [g.scalar.activation(out["ap"], a["ap"], AF.Identity, bias=bias["ap"])]
        return add("S", fn, [a, bias], [out], cost)

    def put(on_s, off, val, tab="ST"):
        out = IND(A((tab, 0), 0, 5120), off)
        if not on_s:
            return cp(out, val)
        return add("S", lambda: [g.scalar.activation(out["ap"], val["ap"], AF.Silu)], [val], [out], 70 + C["s"] * out["n"])

    def mm(lst):
        def fn():
            r = []
            for i, (o, l, x, st, sp) in enumerate(lst):
                ins = g.tensor.matmul(o["ap"], l["ap"], x["ap"], st, sp)
                if sp or i == len(lst) - 1:
                    r.append(ins)
            return r
        k = sum(1 for i, m in enumerate(lst) if m[4] or i == len(lst) - 1)
        me = add("P", fn, [m[1] for m in lst] + [m[2] for m in lst], [m[0] for m in lst],
                 10 + sum(C["pe"] * max(min(64, m[1]["n"]), m[2]["n"]) * (4 if m[2]["buf"] == "LF" else 1) for m in lst), lat=30.0)
        ops[me]["k"] = k
        return me

    def dma(q, out, in_, nbytes, ins=(), outs=()):
        e = g.sync if q == "Y" else g.scalar
        return add(q, lambda: [e.dma_start(out, in_)], list(ins), list(outs), 60, "d", 1900 + nbytes / 250.0)

    def iota(out, pat, base, cm):
        if out["buf"] == "LI":
            fn = lambda: [g.iota(out["ap"], pat, base, cm)]
        else:
            fn = lambda: [g.iota(out["ap"], pat, base, cm, allow_small_or_imprecise_dtypes=True)]
        return add("G", fn, [], [out], 130 + C["lat"] + 2 * C["c"] * out["n"])

    def pick(out, a, pat, op, base):
        return add("G", lambda: [g.affine_select(out["ap"], a["ap"], pat, op, 0.0, base, 1)], [a], [out], 170 + C["lat"] + 2 * C["c"] * out["n"])

    def send(src, land, nbytes):
        sem = "r%d" % nsem["r"]
        s = add("G", lambda: [g.remote_dma(land["ap"], src["ap"], T.sem[sem], T.sem.sent, pid, rid, mask_out)], [src], [], 500 + 1500 * (sem == "r0"), "x")
        return add("N", None, [], [land], 0, "r", 2500 + nbytes / 60.0, extra=[s])

    F = lambda k: al("LF", k)
    B = lambda k: al("LB", k)
    U = lambda k: al("LU", k)
    PS = [("PS%d" % i, 0) for i in range(8)]
    PATH, CNT, ZB, MA, MB = PS[0:2], PS[2:4], PS[4:6], PS[6], PS[7]
    XW, STW, SBW, IDW = A(("XW", 0), 0, 4096), A(("ST", 0), 0, 4096), A(("SB", 0), 0, 4096), A(("IDT", 0), 0, 8192)
    ST, SB, IDT = ("ST", 0), ("SB", 0), ("IDT", 0)

    ns, kd, ro, ne = al("LI", 256), al("LI", 256), al("LI", 32), al("LI", 64)
    soon(30, dma("Y", A(ns, 0, 256)["ap"], T.nsum[:], 131072, outs=[A(ns, 0, 256)]))
    for par in range(2):
        for s in range(2):
            o = A(ne, 32 * par + 16 * s, 32 * par + 16 * s + 16)
            soon(29, dma("YS"[par], o["ap"], T.nei[par::2, 32 * s:32 * s + 32], 8192, outs=[o]))
        o = A(ro, 16 * par, 16 * par + 16)
        soon(28, dma("YS"[par], o["ap"], T.rho[par::2, :], 8192, outs=[o]))
    d0 = B(512)
    soon(27.5, dma("S", A(d0, 0, 512)["ap"], T.dem[:, 0:512], 131072, outs=[A(d0, 0, 512)]))
    xs = C["xs"]
    soon(27, dma("S", T.XW[:, 0:xs], T.x[:, 0:xs], 256 * xs, outs=[A(("XW", 0), 0, xs)]))
    DW = [None, [B(768), B(768)], [B(768), B(768)]]

    pi, J, Jc, cols = al("LI", 48), F(144), F(128), F(16)
    soon(22, iota(A(pi, 0, 1), [[0, 1]], 0, 1))
    soon(21, iota(A(Jc, 0, 128), [[1, 128]], 0, 0))
    soon(20, iota(A(J, 0, 144), [[1, 144]], -15, -1))
    ts(A(pi, 16, 17), A(pi, 0, 1), 15, OP.bitwise_and)
    col = lambda i: A(cols, i, i + 1)
    q, wlo, whi, ca, cb, c1k = [col(i) for i in range(6)]
    cp(q, A(pi, 16, 17))
    oh, mk = F(16), F(8)
    ts(A(oh, 0, 16), A(Jc, 0, 16), q, OP.is_equal)
    ts(wlo, A(oh, 1, 2), A(oh, 2, 3), OP.subtract, A(oh, 6, 7), OP.subtract)
    ts(whi, A(oh, 0, 1), A(oh, 1, 2), OP.add, A(oh, 4, 5), OP.add)
    ts(ca, A(oh, 0, 1), A(oh, 2, 3), OP.add, A(oh, 4, 5), OP.add)
    ts(cb, A(oh, 1, 2), LIFT / 256.0, OP.mult, A(oh, 6, 7), OP.add)
    ts(ca, ca, cb, OP.add, 256.0, OP.mult)
    ts(c1k, A(oh, 5, 6), 255.0, OP.mult, ca, OP.add)
    tt(A(mk, 0, 2), A(oh, 0, 8, 4), A(oh, 2, 8, 4), OP.subtract)
    tt(A(mk, 4, 6), A(oh, 0, 8, 4), A(oh, 2, 8, 4), OP.add)
    tt(A(mk, 2, 3), A(oh, 3, 4), A(oh, 5, 6), OP.add)
    tt(A(mk, 3, 4), A(mk, 4, 5), A(mk, 2, 3), OP.add)
    Bc, Id = B(144), B(144)
    Bm = [B(144) for _ in range(3)]
    ts(A(Bc, 0, 144), A(J, 0, 144), q, OP.add, 0.0, OP.is_equal)
    for u in range(3):
        act(A(Bm[u], 0, 144), A(Bc, 0, 144), scale=A(mk, u, u + 1))
    ts(A(Id, 0, 144), A(J, 0, 144), 0.0, OP.is_equal)
    I32, I64, I256, Sh, Sh2, Ip, In, In2 = B(128), B(128), B(128), B(128), B(128), F(128), F(128), F(128)
    if any(C[k] for k in ("lP", "ld", "lS", "lv")):
        act(A(Ip, 0, 128), A(Id, 15, 143))
    for b_, v in ((In, -1.0), (In2, -2.0), (I32, -32.0), (I64, -64.0), (I256, -256.0)):
        act(A(b_, 0, 128), A(Id, 15, 143), scale=v)
    ts(A(Sh, 0, 128), A(J, 15, 143), 16.0, OP.is_equal, -256.0, OP.mult)
    ts(A(Sh2, 0, 128), A(J, 15, 143), -112.0, OP.is_equal, -256.0, OP.mult)
    L = lambda b_, k: A(b_, 15 - k, 143 - k)
    full = lambda b_: A(b_, 0, 128)

    def lin(terms, start=True):
        return [(m[0], A(Ip if m[1] > 0 else In, 0, 128), m[2], start and i == 0, i == len(terms) - 1) for i, m in enumerate(terms) if m]

    def comb(pe, bank, lo, k, whole, parts=()):
        if pe:
            o = lambda a, b: A(bank, lo + a, lo + b)
            if whole:
                mm(lin([(o(0, k), s_, x) for s_, x in whole] + [(o(a, b), s_, x) for a, b, tm in parts for s_, x in tm]))
            else:
                mm([m for a, b, tm in parts for m in lin([(o(a, b), s_, x) for s_, x in tm])])
            return (bank[0], lo)
        r = F(k)
        for a, b, tm in list(parts) + [(0, k, ([(1, A(r, 0, k))] if parts else []) + list(whole))]:
            for i in range(1, len(tm)):
                tt(A(r, a, b), tm[0][1] if i == 1 else A(r, a, b), tm[i][1], OP.add if tm[i][0] > 0 else OP.subtract)
        return r

    c2, dump, dumk, base, FD = F(128), F(64), F(16), B(16), F(224)
    iota(A(c2, 0, 128), [[16, 64], [0, 2]], 0, 0)
    ts(A(dump, 0, 64), two(c2, 0, 64, 0), q, OP.add, 4096.0, OP.add)
    ts(A(dumk, 0, 16), two(c2, 0, 16, 0), q, OP.add, 512.0, OP.add)
    ts(A(FD, 0, 128), A(c2, 0, 128), q, OP.add, 4096.0, OP.add)
    act(A(FD, 128, 192), A(FD, 0, 64))
    ts(A(FD, 192, 224), A(c2, 0, 32), q, OP.add, 512.0, OP.add)
    FDK, FD2, FDP, FDL = [(FD[0], FD[1] + a) for a in (0, 64, 128, 192)]
    act(A(base, 0, 16), two(c2, 0, 16, 0))
    LW, Z0 = [B(768) for _ in range(3)], B(128)
    if C["lS"]:
        ms(A(Z0, 0, 128), 0.0)
    NN, EZ, EB = B(352), B(384), [F(320), F(320)]
    KP = (EZ[0], EZ[1] + 320)
    ms(A(NN, 0, 352), 1.0)
    N = [(NN[0], NN[1] + 176 * par) for par in range(2)]
    for par in range(2):
        ms(five(N[par], 0, 32, 1), 0.0)
        ms(five(EB[par], 0, 32, 0), 0.0)
    ms(A(EZ, 0, 384), 0.0)
    EM, SP = [(EZ[0], EZ[1] + 64 * i) for i in range(2)], [(EZ[0], EZ[1] + 64 * i) for i in range(2, 5)]
    Sel = F(128)
    ms(A(Sel, 0, 128), 1.0)
    pick(A(Sel, 0, 128), A(Sel, 0, 128), [[-2, 8], [-16, 8], [-1, 2]], OP.is_equal, 0)

    fa, fb = C["fill"]
    for a in [0] + list(range(512, fa, C["fp"])):
        soon(15, ms(A(ST, a, min(fa, a + C["fp"]) if a else 512), 0.0))
    if fb:
        soon(15, iota(A(ST, fa, fa + fb), [[0, fb]], 0, 0))
    for a in range(fa + fb, 4096, 512):
        o, i_ = A(ST, a, a + 512), A(ST, 0, 512)
        soon(19 + 6 * (a == fa + fb), add("S", lambda o=o, i_=i_: [g.scalar.activation(o["ap"], i_["ap"], AF.Silu)], [i_], [o], 40 + C["c"] * 512 + 1500 * (a == fa + fb)))
    hi_, lo_, wh_ = A(F(256), 0, 256), A(F(256), 0, 256), A(F(256), 0, 256)
    ts(hi_, A(ns, 0, 256), 1610612736.0, OP.add, 1610612736.0, OP.subtract)
    tt(lo_, hi_, A(ns, 0, 256), OP.subtract)
    ts(wh_, A(ns, 0, 256), LIFT, OP.add)
    for r_, src in ((0, hi_), (2, lo_), (1, wh_)):
        soon(14, dma("Y", T.ST[r_:128:16, 0:4096], src["ap"], 131072, ins=[src, A(ST, 16, 4096)], outs=[A(ST, 4 * r_, 4 * r_ + 4)]))

    def behind():
        for r_, src in ((0, hi_), (2, lo_)):
            dma("Y", T.SB[r_:128:16, 0:4096], src["ap"], 131072, ins=[src, A(SB, 16, 4096)], outs=[A(SB, 4 * r_, 4 * r_ + 4)])

    if C["sb"] == 1:
        for a in range(0, 4096, 1024):
            iota(A(SB, a, a + 1024), [[0, 1024]], 4096 + int(LIFT), 0)
        behind()
    elif C["sb"]:
        for a in range(0, 4096 * (C["sb"] == 2), 1024):
            soon(C["sbe"], dma("Y", A(SB, a, a + 1024)["ap"], A(ST, a, a + 1024)["ap"], 1 << 20, ins=[STW], outs=[A(SB, a, a + 1024)]))
        flat = A(F(256), 0, 256)
        iota(flat, [[0, 256]], 4096 + int(LIFT), 0)
        dma("Y", T.SB[1:128:16, 0:4096], flat["ap"], 131072, ins=[flat], outs=[SBW])
    late = [hi_, lo_, wh_, A(ST, 16, 4096)]
    if xs < 4096:
        soon(13.5, dma("Y", T.XW[:, xs:4096], T.x[:, xs:4096], 256 * (4096 - xs) + 300000, ins=late, outs=[A(("XW", 0), xs, 4096)]))
    if C["kde"]:
        soon(27.2, dma("Y", A(kd, 0, 256)["ap"], T.kid[:], 200000, outs=[A(kd, 0, 256)]))
    else:
        soon(13.7, dma("Y", A(kd, 0, 256)["ap"], T.kid[:], 400000, ins=late, outs=[A(kd, 0, 256)]))
    for t in (1, 2):
        dr = B(512)
        dma("Y", A(dr, 0, 512)["ap"], T.dem[:, 512 * t:512 * t + 512], 131072, ins=[STW], outs=[A(dr, 0, 512)])
        for par in range(2):
            for hh in range(2):
                pick(two(DW[t][par], 0, 128, hh), two(dr, 128 * hh, 128 * hh + 128, par), [[0, 128]], OP.is_ge, 0)

    bi, kf = F(64), F(256)
    ts(A(IDT, 0, 128), A(Jc, 0, 128), wlo, OP.mult, c1k, OP.add)
    ts(A(bi, 0, 32), A(Jc, 0, 32), 128.0, OP.mult, whi, OP.mult)
    for w in (128, 256):
        soon(18, act(A(IDT, w, 2 * w), A(IDT, 0, w), A(bi, w // 128, w // 128 + 1)))
    for k in range(1, 8):
        o, bb = A(IDT, 512 * k, 512 * k + 512), A(bi, 4 * k, 4 * k + 1)
        if k <= C["idv"]:
            ts(o, A(IDT, 0, 512), bb, OP.add)
        else:
            act(o, A(IDT, 0, 512), bb)
        soon(4 * (k <= C["ide"]))
    hc, lc, q256 = F(256), F(256), F(1)
    for k in range(4):
        soon(C["ige"], iota(A(IDT, 4096 + 1024 * k, 5120 + 1024 * k), [[1, 1024]], 4096 + 1024 * k + int(LIFT), 0))
    iota(A(hc, 0, 256), [[128, 2], [0, 128]], 4096 + 256, 0)
    iota(A(lc, 0, 256), [[0, 2], [-1, 128]], 256, 0)
    ts(A(q256, 0, 1), q, 256.0, OP.mult)
    act(A(hc, 0, 256), A(hc, 0, 256), A(q256, 0, 1))
    dma("Y", T.IDT[0:128:16, 4096:8192], A(hc, 0, 256)["ap"], 131072, ins=[A(hc, 0, 256), A(IDT, 4104, 8192)], outs=[A(IDT, 4096, 4100)])
    dma("Y", T.IDT[2:128:16, 4096:8192], A(lc, 0, 256)["ap"], 131072, ins=[A(lc, 0, 256), A(IDT, 4104, 8192)], outs=[A(IDT, 4100, 4104)])
    rn, rnu, k2 = al("LI", 32), U(32), A(al("LI", 256), 0, 256)
    soon(12, dma("Y", A(rn, 0, 32)["ap"], T.rho[:], 400000, ins=late, outs=[A(rn, 0, 32)]))
    cp(A(rnu, 0, 32), A(rn, 0, 32))
    ts(k2, A(kd, 0, 256), 1023, OP.bitwise_and)
    soon(C["kde"], ts(A(kf, 0, 256), k2, -255.0, OP.add))
    for i in range(2):
        if i == C["kl"]:
            soon(C["kfe"], dma("Y", T.IDT[3:128:16, 0:4096], A(kf, 0, 256)["ap"], 131072, ins=[A(kf, 0, 256)], outs=[A(IDT, 0, 4096)]))
        else:
            act(A(LW[0], 0, 512), IND(A(IDT, 0, 4096), A(rnu, 0, 32)))
            for t in (1, 2):
                dma("Y", A(LW[t], 0, 512)["ap"], A(LW[0], 0, 512)["ap"], 131072, ins=[A(LW[0], 0, 512)], outs=[A(LW[t], 0, 512)])

    R, ru = [F(32), F(32)], U(32)
    for par in range(2):
        for s in range(2):
            cp(A(R[par], 16 * s, 16 * s + 16), A(ro, 16 * par, 16 * par + 16))
    cp(A(ru, 0, 32), A(ro, 0, 32))
    V3 = [F(32), F(32)]
    O = [[U(128), U(128)] for _ in range(3)]
    for par in range(2):
        cp(A(O[0][par], 0, 32), A(ne, 32 * par, 32 * par + 32))
        cp(five(EB[par], 0, 32), A(ne, 32 * par, 32 * par + 32))
    dead, FR = [None, None], [None, None]
    z = [[B(512), B(512)] for _ in range(3)]
    sg = [[B(512), B(512)], [B(512), B(512)]]
    xg = [[B(512), B(512)], [B(512), B(512)]]
    cm = [B(2048), B(2048)]
    zoff = [None, [U(16), U(16)], [U(16), U(16)]]
    lod = [None, B(256), B(256)]
    YO = F(768)

    def w2l(out, lo, wide, a, k, lhs, start=True, stop=True, more=()):
        o = A(out, lo, lo + k // 16)
        lst = [(o, L(lhs, i), A(wide, a + i, a + k, 16), start and i == 0, stop and i == 15) for i in range(16)]
        return lst[:1] + list(more) + lst[1:]

    def step(t, par, k):
        e, o, s, ps = EB[par], O[t][par], sg[par][k % 2], A(PATH[par], 0, 32)
        v = [A(R[par], 0, 32), five(e, 0, 32), five(e, 32, 64), A(V3[par], 0, 32)]
        act(A(s, 0, 512), IND(SBW if t and par == t % 2 and k - 2 >= C["sk"][t - 1] else STW, A(o, 32 * k - 32, 32 * k)))
        less = [(In, v[k - 1])] if k < 4 else [(In2, v[3]), (In, five(e, 0, 32, 1))]
        mm([(ps, full(m_), x, i == 0, False) for i, (m_, x) in enumerate(less)])
        mm(w2l(PATH[par], 0, s, 0, 512, Bm[0], start=False))
        if k < 4:
            ts(A(o, 32 * k, 32 * k + 32), ps, 4095.0, OP.min)
            if k < 3:
                (act if C["vS"][k - 1] else cp)(v[k + 1], ps)
            tt(five(e, 0, 32, 4 - k), ps, v[k], OP.subtract)
        elif not C["late4"][par != t % 2]:
            cp(five(e, 0, 32, 0), ps)

    def demand(t, par):
        zz = A(z[t][par], 0, 256)
        role = 0 if par == t % 2 else 1
        if t == 0:
            for hh in range(2):
                (act if C["d0S"] else cp)(two(z[t][par], 0, 128, hh), two(d0, 128 * hh, 128 * hh + 128, par))
        else:
            act(zz, IND(A(DW[t][par], 0, 768), A(zoff[t][par], 0, 16)))
        if C["zd"][t][role]:
            pick(A(z[t][par], 256, 512), zz, [[0, 256]], OP.is_ge, 0)
        if t < 2:
            if par == 0:
                ld = A(DW[t + 1][0], 256, 512)
                send(zz, ld, 65536)
                dma("Y", A(DW[t + 1][0], 512, 768)["ap"], ld["ap"], 65536, ins=[ld], outs=[A(DW[t + 1][0], 512, 768)])
            else:
                ld = lod[t + 1]
                send(zz, A(ld, 0, 256), 65536)
                for c0 in (256, 512):
                    for a, b_ in ((slice(16, 128), slice(0, 112)), (slice(0, 16), slice(112, 128))):
                        dma("Y", A(DW[t + 1][1], c0, c0 + 256, p=a)["ap"], A(ld, 0, 256, p=b_)["ap"], 60000,
                            ins=[A(ld, 0, 256)], outs=[A(DW[t + 1][1], c0 + (a.start > 0) * 128, c0 + 128 + (a.start > 0) * 128)])
        if any(C["pre"][t][4 * role:4 * role + 4]):
            mm([(A(ZB[par], 256 * s, 256 * s + 256), A(Id, 15, 143), zz, True, True) for s in range(2)])

    def look(t, par, k):
        role = 0 if par == t % 2 else 1
        o = O[t][par]
        if C["pre"][t][4 * role + k]:
            xx = A(xg[par][k % 2], 0, 512)
            act(xx, IND(XW, A(o, 32 * k, 32 * k + 32)))
            tt(A(cm[par], 512 * k, 512 * k + 512), xx, A(ZB[par], 0, 512), OP.is_ge)
        elif C["zd"][t][role]:
            tt(A(cm[par], 512 * k, 512 * k + 512), IND(XW, A(o, 32 * k, 32 * k + 32)), A(z[t][par], 0, 512), OP.is_ge)
        else:
            for s in range(2):
                tt(A(cm[par], 512 * k + 256 * s, 512 * k + 256 * s + 256), IND(XW, A(o, 32 * k + 16 * s, 32 * k + 16 * s + 16)),
                   A(z[t][par], 0, 256), OP.is_ge)

    def decide(t, par):
        isp = par == t % 2
        e, cn, nn, em = EB[par], CNT[par], N[par], EM[par]
        fl, OS, hit, ed = B(48), F(320), B(32), FDP if isp else FDK
        for k in range(4):
            look(t, par, k)
        tt(A(fl, 0, 32), five(e, 16, 48), five(e, 32, 64), OP.is_equal)
        more = [(A(cn, 64, 80), full(I32), A(fl, 0, 16), False, False)]
        if C["c3"][0 if isp else 1]:
            mm(w2l(cn, 0, cm[par], 0, 1536, Bc, more=more))
        else:
            mm(w2l(cn, 0, cm[par], 0, 1024, Bc))
            for k in range(2):
                ts(five(nn, 0, 32, 4 - k), A(cn, 32 * k, 32 * k + 32), 8.5, OP.is_lt)
            mm(w2l(cn, 64, cm[par], 1024, 512, Bc, more=more))
        for k in range(0 if C["c3"][0 if isp else 1] else 2, 3):
            ts(five(nn, 0, 32, 4 - k), A(cn, 32 * k, 32 * k + 32), 8.5, OP.is_lt)
        if C["b4"]:
            cn = ZB[par] if not any(C["pre"][t][0 if isp else 4:][:4]) else MA if t == 2 and C["df"] else cn
        more = [(A(cn, 96, 112), full(I32), A(fl, 16 * i, 16 * i + 16), False, False) for i in range(2)]
        if dead[par] is not None:
            more.append((A(cn, 96, 112), full(I256), dead[par], False, False))
        mm(w2l(cn, 96, cm[par], 1536, 512, Bc, stop=False, more=more))
        scan(A(OS, 0, 160), A(nn, 0, 160), A(e, 0, 160))
        tt(A(fl, 32, 48), five(OS, 0, 16), five(OS, 16, 32), OP.is_equal)
        if isp or C["sw"][t] != 1:
            tt(two(ed, 0, 32, 0), five(OS, 0, 32), A(dump, 0, 32), OP.subtract)
        if C["late4"][0 if isp else 1]:
            cp(five(e, 0, 32, 0), A(PATH[par], 0, 32))
        scan(A(OS, 160, 320), A(nn, 1, 161), A(e, 0, 160))
        mm([(A(cn, 96, 128), full(I64), five(nn, 0, 32, 2 + i), False, False) for i in range(3)]
           + [(A(cn, 96, 112), full(I256), A(fl, 32, 48), False, True)])
        ts(A(hit, 0, 32), A(cn, 96, 128), -183.5, OP.is_gt)
        if t < 2:
            flags(t, par, hit)
        for s in range(2):
            tt(two(em, 16 * s, 16 * s + 16, 1), A(hit, 0, 16), A(hit, 16, 32), OP.mult)
        return OS

    def move(t, par, OS):
        k = 64 if t < 2 and par != t % 2 else 32
        e, D = EB[par], F(64)
        if t == 2 and C["rf"][par]:
            rootsum(par, OS)
        tt(A(D, 0, k), five(OS, 0, k), five(e, 0, k), OP.subtract)
        for a in range(0, k, 32):
            tt(A(D, a, a + 32), A(D, a, a + 32), two(EM[par], 0, 32, 1), OP.mult)
        tt(five(e, 0, k), five(e, 0, k), A(D, 0, k), OP.add)
        if t < 2:
            ts(A(O[t + 1][par], 0, k), five(e, 0, k), 4095.0, OP.min)
        if k == 64:
            tt(five(e, 0, 32, 3), five(e, 32, 64), five(e, 0, 32), OP.subtract)

    def flags(t, par, hit):
        uo = U(16)
        o = A(CNT[par], 128, 144)
        mv = [(o, full(m_), A(hit, 16 * s, 16 * s + 16), False, False) for s in range(2) for m_ in ((Sh, Sh2) if par else (I256,))]
        mm([(o, A(Id, 15, 143), A(base, 0, 16), True, False)] + mv[:-1] + [mv[-1][:4] + (True,)])
        ts(A(uo, 0, 16), o, q, OP.add, 512.0, OP.add)
        send(A(uo, 0, 16), A(zoff[t + 1][par], 0, 16), 4096)

    def rootsum(par, OS):
        fr = F(32)
        tt(two(fr, 0, 16, 1), five(EB[par], 0, 16), five(EB[par], 16, 32), OP.add)
        tt(two(fr, 0, 16, 0), five(OS, 0, 16), five(OS, 16, 32), OP.add)
        tt(two(fr, 0, 16, 0), two(fr, 0, 16, 0), two(fr, 0, 16, 1), OP.subtract)
        FR[par] = fr

    def roots(par, on_s):
        vu, w = U(16), F(256)
        if C["rf"][par]:
            r = F(32)
            scan(A(r, 0, 32), A(EM[par], 0, 32), A(FR[par], 0, 32))
            cp(A(vu, 0, 16), two(r, 0, 16, 1))
        else:
            cp(A(vu, 0, 16), A(comb(C["lP"], CNT[par], 192, 16, [(1, five(EB[par], 0, 16)), (1, five(EB[par], 16, 32))]), 0, 16))
        (cp if C["rv"][par] else act)(A(w, 0, 256), IND(IDW, A(vu, 0, 16)))
        put(on_s, A(ru, 16 * par, 16 * par + 16), A(w, 0, 256))

    top16 = slice(0, 16)

    def results(par):
        lv = F(16)
        ts(A(lv, 0, 16), dead[par], 0.5, OP.is_lt)
        mm([(A(PATH[0], 2 * a + par, 512, 16, p=top16), A(Sel, 16 * a, 16 * a + 16), five(EB[par], 0, 32), True, True) for a in range(8)])
        mm([(A(CNT[0], 256 + 2 * a + par, 512, 16, p=top16), A(Sel, 16 * a, 16 * a + 16), A(lv, 0, 16), True, True) for a in range(8)])

    for par in range(2):
        demand(0, par)
    for k in range(1, 5):
        step(0, 0, k)

    for t in range(3):
        P, K = t % 2, 1 - t % 2
        last = t == 2
        OS = decide(t, P)
        pp, ps = C["pp"][t]
        vu, cn, wu = U(32), CNT[P], U(48)
        ts(A(vu, 0, 32), A(comb(C["lP"], cn, 160, 32, [(1, five(OS, 32, 64)), (1, A(R[P], 0, 32))]), 0, 32), 8191.0, OP.min)
        for a, b_ in ((0, 16), (32, 48)) if C["ws"][t] else ((0, 48),):
            ts(A(wu, a, b_), five(OS, a, b_), 4095.0, OP.min)
        gw = B(512)
        act(A(gw, 0, 256), IND(A(IDT, 0, 4096), A(wu, 0, 16)), scale=A(mk, 3, 4))
        act(A(gw, 256, 512), IND(A(IDT, 0, 4096), A(wu, 32, 48)), scale=A(mk, 5, 6))
        mm(w2l(MB, 64, gw, 0, 256, Bm[2], more=[(A(MB, 64, 80), full(In), A(dumk, 0, 16), False, False)]))
        ts(two(FDL, 0, 16, 0), A(MB, 64, 80), 0.0, OP.min)
        of, pu = F(96), U(48)
        scan(A(of, 0, 64), A(EM[P], 0, 64), A(FDP, 0, 64))
        scan(A(of, 64, 96), A(EM[P], 0, 32), A(FDL, 0, 32))
        cp(A(pu, 0, 48), two(of, 0, 48, 1))
        tt(IND(A(LW[t], 0, 768), A(pu, 32, 48)), A(gw, 0, 256), A(gw, 256, 512), OP.add)
        move(t, P, OS)
        lst = []
        for u in range(2):
            for i in range(16):
                a = 256 * (i % 2) + (i - i % 2) + K
                lst.append((A(MB, 16 * u, 16 * u + 16), L(Bm[u], i), A(LW[t], a, a + 241, 16), i == 0, i == 15))
        mm(lst)
        LL, lu, sv = F(32), U(32), B(512)
        (cp if C["llv"] else act)(A(LL, 0, 32), A(MB, 0, 32))
        pw = F(512)
        act(A(pw, 0, 512), IND(IDW, A(vu, 0, 32)))
        for k in range(1, pp + 1):
            step(t, K, k)
        put(C["silu"][t][0], A(pu, 0, 32), A(pw, 0, 512))
        for k in range(pp + 1, ps + 1):
            step(t, K, k)
        diff = last and C["df"]
        if not diff:
            cp(A(lu, 0, 32), A(MB, 0, 32))
            act(A(sv, 0, 512), IND(STW, A(lu, 0, 32)))
        for k in range(ps + 1, 5):
            step(t, K, k)
        svm = w2l(MA, 0, sv, 0, 512, Bm[0], start=not C["lS"])
        if last:
            roots(P, C["silu"][3][0])
            results(P)
        OS = decide(t, K)
        wu, x1, kc = U(32), B(256), B(256)
        ts(A(wu, 0, 32), five(OS, 0, 32), 4095.0, OP.min)
        act(A(x1, 0, 256), IND(XW, A(wu, 16, 32)))
        tt(A(kc, 0, 256), IND(XW, A(wu, 0, 16)), A(x1, 0, 256), OP.is_ge)
        kp, tk, nf, vu, of, ou = F(16), F(32), F(16), U(64), F(128), U(64)
        w0, w1, pv, pb, X = five(OS, 0, 16), five(OS, 16, 32), A(LL, 0, 16), A(LL, 16, 32), five(OS, 32, 64)
        tw, tv, cn = A(tk, 0, 16), A(tk, 16, 32), CNT[K]
        sw, x0, x1 = C["sw"][t], five(OS, 32, 48), five(OS, 48, 64)
        if sw < 2:
            dd = comb(C["ld"], ZB[P], 160, 32, [], [(0, 16, [(1, w0), (-1, w1)]), (16, 32, [(1, x0), (-1, x1)] if sw else [(1, pv), (-1, pb)])])
        tt(A(nf, 0, 16), pv, pb, OP.is_equal)
        if sw == 2:
            pr, res = F(128), F(128)
            for i, (a, b_, u, v, op) in enumerate(((pv, pb, x0, pb, OP.add), (pb, pv, x1, pv, OP.add), (w0, w1, w1, pb, OP.subtract), (w1, w0, w0, pv, OP.subtract))):
                tt(two(pr, 16 * i, 16 * i + 16, 0), a, b_, OP.subtract)
                tt(two(pr, 16 * i, 16 * i + 16, 1), u, v, op)
            mm(w2l(ZB[P], 128, kc, 0, 256, Bc))
            for s in range(2):
                ts(two(KP, 16 * s, 16 * s + 16, 1), A(ZB[P], 128, 144), 8.5, OP.is_gt)
            scan(A(res, 0, 64), A(KP, 0, 64), A(pr, 0, 64))
            ts(A(vu, 0, 32), two(res, 0, 32, 1), 8191.0, OP.min)
            if not diff:
                mm(svm)
                if C["cx"][t]:
                    tt(two(pr, 32, 64, 1), two(pr, 32, 64, 1), A(MA, 0, 32), OP.add)
            scan(A(res, 64, 128), A(KP, 0, 64), A(pr, 64, 128))
            if not diff and not C["cx"][t]:
                tt(two(res, 32, 64, 1), two(res, 32, 64, 1), A(MA, 0, 32), OP.add)
            ts(A(vu, 32, 64), two(res, 32, 64, 1), 4096.0 * diff, OP.add, 8191.0, OP.min)
        elif sw:
            mm(w2l(ZB[P], 128, kc, 0, 256, Bc))
            ts(A(kp, 0, 16), A(ZB[P], 128, 144), 8.5, OP.is_gt)
            for s in range(2):
                tt(A(tk, 16 * s, 16 * s + 16), A(dd, 16 * s, 16 * s + 16), A(kp, 0, 16), OP.mult)
            cw = comb(0, None, 0, 32, [], [(0, 16, [(1, w1), (1, tw)]), (16, 32, [(1, w0), (-1, tw)])])
            tt(two(FDK, 0, 32, 0), A(cw, 0, 32), A(dump, 0, 32), OP.subtract)
            vl = comb(0, None, 0, 32, [(1, A(LL, 0, 32))], [(0, 16, [(1, x1), (1, tv)]), (16, 32, [(1, x0), (-1, tv)])])
            if C["lS"] and not diff:
                mm([(A(MA, 0, 32), full(Z0), A(Z0, 0, 32), True, False)] + lin([(A(MA, 0, 16), -1, pb), (A(MA, 16, 32), -1, pv), None], False))
                mm(svm)
                cd = comb(0, None, 0, 32, [(1, A(cw, 0, 32)), (1, A(MA, 0, 32))])
            else:
                if not diff:
                    mm(svm)
                cd = comb(0, None, 0, 32, [] if diff else [(1, A(MA, 0, 32))], [(0, 16, [(1, A(cw, 0, 16)), (-1, pb)]), (16, 32, [(1, A(cw, 16, 32)), (-1, pv)])])
        elif diff:
            cd = comb(0, None, 0, 32, [], [(0, 16, [(1, w1), (-1, pb)]), (16, 32, [(1, w0), (-1, pv)])])
        elif C["lS"]:
            mm([(A(MA, 0, 32), full(Z0), A(Z0, 0, 32), True, False)]
               + lin([(A(MA, 0, 16), 1, w1), (A(MA, 0, 16), -1, pb), (A(MA, 16, 32), 1, w0), (A(MA, 16, 32), -1, pv), None], False))
        else:
            mm(svm)
            cd = comb(0, None, 0, 32, [], [(0, 16, [(1, w1), (-1, pb)]), (16, 32, [(1, w0), (-1, pv)])])
        if not sw:
            mm(w2l(ZB[P], 128, kc, 0, 256, Bc))
            ts(A(kp, 0, 16), A(ZB[P], 128, 144), 8.5, OP.is_gt)
            for s in range(2):
                tt(A(tk, 16 * s, 16 * s + 16), A(dd, 16 * s, 16 * s + 16), A(kp, 0, 16), OP.mult)
        if sw:
            pass
        elif C["lS"] and not diff:
            mm(lin([(A(MA, 0, 16), 1, tw), (A(MA, 16, 32), -1, tw), None], False))
            mm(svm)
            cd = MA
        else:
            cd = comb(0, None, 0, 32, [] if diff else [(1, A(MA, 0, 32))], [(0, 16, [(1, A(cd, 0, 16)), (1, tw)]), (16, 32, [(1, A(cd, 16, 32)), (-1, tw)])])
        if sw < 2:
            ts(A(vu, 32, 64), A(cd, 0, 32), 4096.0 * diff, OP.add, 8191.0, OP.min)
        if sw:
            pass
        elif C["lv"]:
            vl = comb(1, cn, 160, 32, [(1, X)], [(0, 16, [(1, pb), (1, tv)]), (16, 32, [(1, pv), (-1, tv)])])
        elif C["xl"][t]:
            vl = comb(0, None, 0, 32, [(1, X)], [(0, 16, [(1, pb), (1, tv)]), (16, 32, [(1, pv), (-1, tv)])])
        else:
            vl = comb(0, None, 0, 32, [], [(0, 16, [(1, pb), (1, five(OS, 32, 48)), (1, tv)]), (16, 32, [(1, pv), (1, five(OS, 48, 64)), (-1, tv)])])
        if sw < 2:
            ts(A(vu, 0, 32), A(vl, 0, 32), 8191.0, OP.min)
        tt(two(FD2, 0, 32, 0), A(LL, 0, 32), A(dump, 32, 64), OP.subtract)
        for s in range(2):
            tt(two(SP[t], 16 * s, 16 * s + 16, 1), two(EM[K], 0, 16, 1), A(nf, 0, 16), OP.is_gt)
        scan(A(of, 0, 64), A(EM[K], 0, 64), A(FDK, 0, 64))
        scan(A(of, 64, 128), A(SP[t], 0, 64), A(FD2, 0, 64))
        for i in range(2):
            cp(A(ou, 32 * i, 32 * i + 32), two(of, 32 * i, 32 * i + 32, 1))
        move(t, K, OS)
        kw = F(1024)
        (cp if C["kv"][t][0] else act)(A(kw, 512, 1024), IND(IDW, A(vu, 32, 64)))
        (cp if C["kv"][t][1] else act)(A(kw, 0, 512), IND(IDW, A(vu, 0, 32)))
        nd = two(SP[t], 0, 16, 1)
        if dead[K] is not None:
            nd, old = A(B(16), 0, 16), nd
            tt(nd, dead[K], old, OP.max)
        dead[K] = nd
        both = [(A(ou, 32, 64), A(kw, 512, 1024), "SB" if diff else "ST"), (A(ou, 0, 32), A(kw, 0, 512))]
        cut = (0,) + tuple(C["nb"][t]) + (1 if last else 3,)
        for i in range(3):
            for k in range(cut[i], cut[i + 1]):
                if last:
                    roots(K, C["silu"][3][1])
                else:
                    step(t + 1, K, k + 2)
            if i < 2:
                put(C["silu"][t][1 + i], *both[i ^ C["nf"][t]])
        if t == 0 and C["sk"][1] < 3:
            for r_, dst in ((0, hi_), (2, lo_)):
                dma("Y", dst["ap"], T.ST[r_:128:16, 0:4096], 131072, ins=[STW], outs=[dst])
            behind()
        if not last:
            demand(t + 1, P)
            demand(t + 1, K)
        else:
            results(K)
            act(A(YO, 0, 512, p=top16), A(PATH[0], 0, 512, p=top16))
            act(A(YO, 512, 768, p=top16), A(CNT[0], 256, 512, p=top16))
            for s in range(2):
                dma("S", T.yn[:, 512 * s:512 * s + 512], A(YO, 256 * s, 256 * s + 256, p=top16)["ap"], 16384, ins=[A(YO, 0, 512)])
            dma("S", T.yl[:], A(YO, 512, 768, p=top16)["ap"], 16384, ins=[A(YO, 512, 768)])
            yc = A(F(256), 0, 256)
            dma("Y", yc["ap"], A(ST, 0, 4096, p=slice(1, 128, 16))["ap"], 131072, ins=[STW], outs=[yc])
            if diff:
                yd = A(F(256), 0, 256)
                dma("Y", yd["ap"], A(SB, 0, 4096, p=slice(1, 128, 16))["ap"], 131072, ins=[SBW], outs=[yd])
                if C["yp"]:
                    cp(A(MB, 0, 256), yd)
                    yd = A(MB, 0, 256)
                tt(yc, yc, yd, OP.add)
            ts(yc, yc, 12582912.0 - LIFT - diff * (4096 + LIFT), OP.add, 12582912.0, OP.subtract)
            dma("Y", T.ys[:], yc["ap"], 131072, ins=[yc])

    if "t0" not in INFO:
        INFO["t0"], INFO["end"] = arrange(ops, C["lat"], C["iters"])
    order = {e: [] for e in "VSPGYN"}
    for i in sorted(range(len(ops)), key=lambda j: (INFO["t0"][j], j)):
        ops[i]["t0"] = INFO["t0"][i]
        order[ops[i]["eng"]].append(i)
    prev = None
    for i in order["G"]:
        if ops[i]["kind"] == "c":
            if prev is not None:
                ops[i]["deps"].add(prev)
            prev = i
    INFO["busy"] = {e: sum(ops[i]["cost"] for i in order[e]) for e in order}
    INFO["ops"] = ops
    INFO["order"] = order
    INFO["top"] = dict(top)

    tot = {}
    for e in "VSPG":
        c = 0
        for i in order[e]:
            if ops[i]["kind"] == "c":
                c += ops[i].get("k", 1)
                ops[i]["done"] = ("s" + e, c)
        tot["s" + e] = c
    for o in ops:
        if o["kind"] == "d":
            o["done"] = (o["sem"], 16)
            tot[o["sem"]] = 16
        elif o["kind"] == "r":
            o["done"] = (o["sem"], n_in)
            tot[o["sem"]] = n_in
    tot["sent"] = n_out * nsem["r"]
    queue = {"V": g.vector, "S": g.scalar, "P": g.tensor, "G": g, "Y": g.sync}
    for e in "YSVPG":
        seen = {}
        for i in order[e]:
            o = ops[i]
            need = {}
            for j in o["deps"]:
                if e == "P" and ops[j]["eng"] == "P":
                    continue
                s, c = ops[j]["done"]
                need[s] = max(need.get(s, 0), c)
            for s in sorted(need):
                if need[s] > seen.get(s, 0):
                    queue[e].wait_ge(T.sem[s], need[s])
                    seen[s] = need[s]
            for ins in o["fn"]():
                if o["kind"] == "c":
                    ins.then_inc(T.sem["s" + e], 1)
                elif o["kind"] == "d":
                    ins.then_inc(T.sem[o["sem"]], 16)
        if e == "G":
            for s in sorted(tot):
                if tot[s] > seen.get(s, 0):
                    g.wait_ge(T.sem[s], tot[s])
